import numpy as np, ml_dtypes
CORES = [16,17,18,19,32,33,34,35]
N = 8
import mx_ref
BF = ml_dtypes.bfloat16
def gentries(a):
    return np.ascontiguousarray(a.reshape(8, 16, -1).transpose(0, 2, 1)).reshape(8, -1)
def gtable(e):
    e = np.asarray(e); return np.ascontiguousarray(e.reshape(8, -1, 16).transpose(0, 2, 1)).reshape(128, -1).astype(np.int32)
def gcols(t, e):
    v = np.concatenate([t.reshape(8, 16, -1, 4), np.zeros((8, 16, 1, 4), BF)], axis=2)
    return np.ascontiguousarray(np.stack([v[g][:, e[g]] for g in range(8)])).reshape(128, -1)
def tile(rs):
    return np.stack(rs, axis=2).reshape(128, -1).astype(BF)
def pick(q, e):
    c = np.concatenate([q[0].reshape(128, -1, 4), np.zeros((128, 1, 4), np.uint8)], axis=1); s = np.concatenate([q[1], np.ones((16, 1), np.uint8)], axis=1)
    return (np.ascontiguousarray(c[:, e].reshape(128, -1)), np.ascontiguousarray(s[:, e]))
def join(*qs):
    return (np.concatenate([q[0] for q in qs], axis=1), np.concatenate([q[1] for q in qs], axis=1))
def put(q, e, v):
    c, s = q[0].reshape(128, -1, 4).copy(), q[1].copy(); c[:, e] = v[0].reshape(128, -1, 4); s[:, e] = v[1]
    return (c.reshape(128, -1), s)
def pk(c, s):
    return (np.ascontiguousarray(c), mx_ref.live(s))
def emit(q):
    return q[0], q[1]
def packed(v, rng):
    q = [mx_ref.quantize(np.ascontiguousarray(v[r])) for r in range(N)]
    return np.stack([a for a, b in q]), np.stack([mx_ref.plane(b, rng) for a, b in q])
def values_of_codes():
    e, c = np.zeros((128, 128, 4), np.float32), np.zeros((128, 2, 4), np.uint8)
    e[np.arange(128), np.arange(128), 0] = 1
    c[:127, :, 0] = np.arange(256).reshape(2, 128).T[:127]
    return mx_ref.matmul(mx_ref.quantize(e.reshape(128, 512).astype(BF)), (c.reshape(128, 8), np.full((16, 2), 127, np.uint8))).T.reshape(-1).astype(np.float64)
CODE_VALUE, SCALE_VALUE = values_of_codes(), 2.0 ** (np.arange(256) - 127.0)
def decode(q):
    return (CODE_VALUE[q[0]].reshape(16, 8, -1, 4) * SCALE_VALUE[q[1]][:, None, :, None] + 0.0).reshape(128, -1).astype(np.float32)
def f(rng, *shape):
    return mx_ref.flush((rng.standard_normal(shape, dtype=np.float32) * np.exp2(rng.integers(-2, 3, shape[:-1] + (1,)))).astype(BF))
def wide(rng, *shape, cols=0):
    v = rng.standard_normal(shape, dtype=np.float32) * np.exp2(rng.integers(-12, 13, shape)).astype(np.float32)
    if cols: v *= np.repeat(np.exp2(rng.integers(-cols, cols + 1, shape[:-2] + (1, shape[-1] // 4))) * (rng.random(shape[:-2] + (1, shape[-1] // 4)) > 0.0625), 4, axis=-1).astype(np.float32)
    return mx_ref.flush(v.astype(BF))
C, B, R = 384, 7, 3
K = 1 << B
def items(p):
    return np.sum((p.reshape(8, 16, -1)[:, :B] + np.float32(0.0) < 0) * (1 << np.arange(B))[:, None], axis=1)
def distances(a, n):
    last = K - 1 - np.argsort(a, axis=2)
    d = np.zeros((N, 8, C), np.int64)
    for j in range(C):
        i = n[:, :, j:j + 1]
        d[:, :, j] = np.sum(last > np.take_along_axis(last, i, axis=2), axis=2)
        np.put_along_axis(last, i, K + j, axis=2)
    return d, last
def big(v):
    v = v.astype(np.float32)
    v[np.abs(v) < np.float32(2.0 ** -16)] = 0
    return v.astype(BF)
def fronts(rng):
    return np.argsort(rng.random((N, 8, K)), axis=2)
def stored(a):
    return np.stack([gtable(e) for e in a])
def numbers_of(rng):
    return {"x": big(f(rng, N, 128, 4 * C)), "h": big(f(rng, N, 128, 4 * K)), "nm": stored(fronts(rng)), "u": np.array(f(rng, N, 128, 512)), "v": np.array(f(rng, N, 128, 512))}
def layers(w, rng):
    c, p = packed(np.ascontiguousarray(w).reshape(N, 128, 2048), rng)
    return {"wc": c, "ws": p}
def weights(rng, q=-1):
    w = np.array(f(rng, N, 128, 2048)).reshape(N, 128, 4, 128, 4)
    if q >= 0:
        w[:, 16 * q:16 * q + 16] = 0
        for i in range(16 * q, 16 * q + 16):
            w[:, :, :, i] = 0
            for b in range(4): w[:, i, b, i, b] = 64
    return layers(w, rng)
def seven(c, rng):
    j = np.arange(C)
    a = j % (2 * K)
    return [c[j % K], c[np.minimum(a, 2 * K - 1 - a)], c[rng.integers(0, 3, C)], c[8 * j // C], np.full(C, K - 1), rng.integers(0, K, C), rng.integers(0, K // 2, C)]
def setup_inputs(rng):
    return {**numbers_of(rng), **weights(rng)}
def setup_inputs_traces(rng):
    d, nm = numbers_of(rng), fronts(rng)
    q = int(rng.integers(8))
    size = np.exp2(np.array([-29.0, -12.0, 0.0, 10.0])[rng.permutation(N) % 4])
    x, h = d["x"].reshape(N, 128, C, 4), d["h"].reshape(N, 128, K, 4)
    x[:, 16 * q:16 * q + 16] = 0
    h[:, 16 * q:16 * q + 16] = 0
    u = d["u"].reshape(N, 128, 8, 16, 4)
    u[:, :, :, :B] = 0
    rest = np.delete(np.arange(8), q)
    k = np.arange(7 * B)
    for r in range(N):
        n = np.zeros((8, C), np.int64)
        for i, g in enumerate(rng.permutation(rest)): n[g] = seven(nm[r, g][::-1], rng)[i]
        digit = (n[rest][:, None] >> np.arange(B)[:, None]) & 1
        mark = np.zeros((64, C))
        mark[:7 * B] = np.where(digit == 1, -1, rng.integers(0, 2, digit.shape)).reshape(7 * B, C) * size[r]
        mark[:, C - 1] = 0
        x[r, 16 * q:16 * q + 16] = mark.reshape(16, 4, C).transpose(0, 2, 1).astype(np.float32).astype(BF)
        u[r, 16 * q + k // 4, rest[k // B], k % B, k % 4] = 2.0 ** -30 if size[r] < 2.0 ** -20 else 1.0
    return {"x": x.reshape(N, 128, 4 * C), "h": h.reshape(N, 128, 4 * K), "nm": stored(nm), "u": u.reshape(N, 128, 512), "v": d["v"], **weights(rng, q)}
def setup_inputs_copies(rng):
    d = setup_inputs(rng)
    o = rng.permutation(N)
    x = d["x"].reshape(N, 128, C, 4)
    for r in range(N): x[r] = x[r][:, rng.integers(0, 1 + 2 * o[r], C)]
    x[o == 1] = 0
    d["x"] = x.reshape(N, 128, 4 * C)
    return d
def setup_inputs_huge(rng):
    d = numbers_of(rng)
    o = rng.permutation(N)
    s = rng.choice([-1.0, 1.0], (N, 8, C))
    s[o == 0] = -1
    s[o == 1] = 1
    x = 2.0 ** 30 * (0.75 + 0.25 * rng.random((N, 128, C, 4))) * np.tile(s, (1, 16, 1))[:, :, :, None]
    h = 2.0 ** 28 * (0.75 + 0.25 * rng.random((N, 128, 4 * K))) * rng.choice([-1.0, 1.0], (N, 128, 4 * K))
    on = (np.arange(128)[:, None, None] % 8 == np.argsort(rng.random((8, 8)), axis=1)[:, :B]) | (o < 2)[:, None, None, None]
    u = d["u"].reshape(N, 128, 8, 16, 4)
    u[:, :, :, :B] = (2.0 ** 30 * (0.75 + 0.25 * rng.random((N, 128, 8, B, 4))) * on[:, :, :, :, None]).astype(np.float32).astype(BF)
    w = np.zeros((N, 128, 4, 128, 4), np.float32)
    i = np.arange(128)
    for b in range(4): w[:, i, b, i, b] = 32
    return {"x": x.astype(np.float32).reshape(N, 128, 4 * C).astype(BF), "h": h.astype(np.float32).astype(BF), "nm": d["nm"], "u": u.reshape(N, 128, 512), "v": d["v"], **layers(w.astype(BF), rng)}
def setup_inputs_spread(rng):
    d = setup_inputs(rng)
    d["x"] = big(wide(rng, N, 128, 4 * C, cols=6))
    d["h"] = big(wide(rng, N, 128, 4 * K, cols=6))
    return d
def check_inputs(d):
    b = []
    for k in ("x", "h", "u", "v"):
        a = np.abs(d[k].astype(np.float32))
        if not (np.isfinite(a).all() and ((a == 0) | (a >= 2.0 ** -30) & (a <= 2.0 ** 30)).all()): b.append("a value of " + k)
    if any((np.sort(gentries(d["nm"][r]), axis=1) != np.arange(K)).any() for r in range(N)): b.append("nm: a group's entries aren't a permutation")
    return b
def reference(x, h, nm, u, v, wc, ws):
    qu = [mx_ref.quantize(u[r]) for r in range(N)]
    lay = [pk(wc[r], ws[r]) for r in range(N)]
    qx = [mx_ref.quantize(x[r]) for r in range(N)]
    qf = [mx_ref.quantize(h[r]) for r in range(N)]
    a = np.stack([gentries(nm[r]) for r in range(N)]).astype(np.int64)
    for t in range(R):
        d, last = distances(a, np.stack([items(mx_ref.matmul(qu[r], qx[r])) for r in range(N)]))
        m = np.argsort(-last, axis=2, kind="stable")
        s = np.take_along_axis(last, m, axis=2)
        border = []
        for r in range(N):
            own, front = decode(qx[r]).astype(BF), decode(qf[r]).astype(BF)
            z = ((own.astype(np.float32) + gcols(front, d[r]).astype(np.float32)) * np.float32(0.5)).astype(BF)
            q = mx_ref.quantize(z)
            qx[r] = mx_ref.quantize(tile([mx_ref.matmul(pick(lay[r], np.arange(128 * b, 128 * b + 128)), q) * np.float32(0.03125) for b in range(4)]))
            both = np.concatenate([decode(qx[r]).astype(BF), front], axis=1)
            border.append(mx_ref.quantize(gcols(both, np.where(s[r] >= K, s[r] - K, C + K - 1 - s[r]))))
        qf = [border[(r - 1) % N] for r in range(N)]
        a = np.stack([m[(r - 1) % N] for r in range(N)])
    y, ol = np.zeros((N, 128, C + K), np.float32), np.zeros((N, 8, C + K), np.float32)
    oc, osc = np.zeros((N, 128, 4 * (C + K)), np.uint8), np.zeros((N, 16, C + K), np.uint8)
    for r in range(N):
        q = join(qx[r], qf[r])
        y[r] = mx_ref.matmul(mx_ref.quantize(v[r]), q)
        ol[r] = np.concatenate([d[r], a[r]], axis=1)
        oc[r], osc[r] = emit(q)
    return {"y": y, "ol": ol, "oc": oc, "osc": osc}

@@ -1,0 +1,557 @@
+import numpy as np
+from concourse.mybir import dt, AluOpType as A, ActivationFunctionType as F
+
+C, K, R = 384, 128, 3
+BIG = 1024.0
+Q, U8, BF, F32, I32, U16, HALF = "float8_e4m3fn_x4", "uint8", "bfloat16", "float32", "int32", "uint16", "float16"
+CUT = [(0, 192), (192, 384)]
+CFG = {"neq_s": (6, 3, 3), "e_s": 2, "y_v": ((), (3,)), "x_v": (), "cut": CUT, "cut0": CUT, "pb": (2, 3), "rt_s": 14,
+       "tb": ((2, 3, 6, 7), (4, 5, 0, 1)), "tv": ((), (1, 3)), "wake": 90.0, "far": 3500.0, "dma": 2200.0}
+ORDER = [
+    22, 2, 37, 0, 41, 8, 40, 26, 10, 11, 17, 9, 18, 29, 16, 38, 19, 50, 20, 24, 59, 72, 52, 21, 35, 3, 73, 28, 60, 53,
+    36, 4, 25, 63, 61, 12, 44, 33, 45, 23, 54, 43, 32, 68, 62, 74, 27, 55, 64, 31, 57, 56, 39, 75, 42, 69, 88, 89, 1,
+    65, 30, 79, 80, 81, 13, 95, 66, 97, 51, 46, 90, 96, 98, 103, 47, 99, 104, 100, 49, 34, 105, 101, 106, 102, 107, 91,
+    14, 123, 48, 125, 70, 135, 15, 116, 82, 92, 71, 114, 129, 124, 117, 130, 67, 115, 127, 128, 133, 119, 86, 85, 191,
+    120, 134, 126, 193, 137, 138, 118, 131, 139, 136, 132, 140, 7, 58, 143, 144, 121, 94, 145, 147, 87, 146, 122, 148,
+    166, 167, 192, 141, 168, 195, 155, 149, 150, 169, 142, 151, 84, 76, 152, 156, 175, 153, 160, 93, 161, 157, 158, 176,
+    189, 162, 159, 154, 163, 190, 177, 5, 164, 173, 110, 111, 108, 77, 109, 112, 165, 196, 180, 205, 194, 199, 198, 201,
+    206, 170, 200, 113, 197, 202, 172, 207, 174, 208, 171, 203, 204, 209, 178, 6, 217, 218, 213, 211, 214, 215, 212,
+    210, 216, 222, 223, 181, 219, 220, 226, 224, 182, 227, 229, 221, 225, 228, 230, 231, 232, 233, 247, 78, 234, 183,
+    235, 179, 184, 237, 238, 249, 236, 248, 243, 245, 187, 239, 185, 240, 188, 186, 250, 260, 242, 261, 241, 262, 277,
+    244, 283, 273, 263, 281, 269, 253, 275, 264, 271, 284, 279, 285, 278, 265, 251, 254, 280, 246, 270, 282, 276, 274,
+    272, 289, 259, 286, 252, 290, 255, 266, 291, 312, 267, 292, 313, 293, 294, 268, 295, 314, 287, 301, 296, 315, 322,
+    256, 319, 288, 318, 320, 297, 298, 302, 326, 299, 323, 306, 303, 307, 308, 304, 300, 309, 305, 321, 316, 257, 317,
+    324, 258, 337, 338, 310, 311, 341, 335, 336, 344, 339, 340, 343, 342, 345, 351, 346, 347, 348, 350, 354, 352, 349,
+    361, 353, 362, 359, 363, 360, 364, 357, 355, 356, 358, 368, 327, 369, 366, 367, 372, 365, 328, 373, 329, 370, 371,
+    374, 325, 375, 376, 330, 379, 377, 378, 380, 331, 381, 383, 389, 390, 332, 397, 384, 391, 382, 393, 385, 386, 406,
+    387, 394, 388, 407, 419, 423, 415, 408, 420, 424, 409, 333, 334, 425, 392, 429, 426, 399, 427, 421, 417, 416, 395,
+    430, 396, 422, 428, 398, 418, 405, 400, 411, 401, 403, 410, 435, 436, 412, 437, 431, 413, 438, 439, 414, 402, 460,
+    440, 404, 461, 432, 462, 441, 433, 442, 434, 443, 444, 463, 468, 466, 467, 464, 447, 489, 485, 445, 452, 448, 446,
+    449, 465, 453, 474, 454, 450, 470, 483, 455, 484, 490, 451, 456, 471, 457, 498, 487, 488, 486, 491, 495, 496, 493,
+    469, 502, 494, 492, 503, 497, 507, 499, 500, 501, 511, 472, 504, 509, 508, 510, 505, 506, 520, 516, 518, 514, 512,
+    475, 517, 513, 476, 527, 519, 515, 528, 521, 477, 525, 529, 526, 522, 530, 535, 473, 536, 523, 533, 478, 481, 479,
+    480, 534, 537, 538, 540, 531, 482, 541, 524, 532, 539, 542, 543, 548, 83, 547, 550, 551, 552, 549, 544, 559, 555,
+    554, 553, 560, 458, 545, 546, 556, 557, 558, 459, 561, 562, 563, 564, 566, 567, 565, 568]
+WIDTH = {Q: 4, U8: 1, BF: 2, F32: 4, I32: 4, U16: 2, HALF: 2}
+SCRATCH, PLACE = {}, {}
+
+
+def _declare():
+    def own(name, n, d):
+        SCRATCH[name] = ("sbuf", [128, n], d)
+        PLACE[name] = (name, 0, n, d)
+
+    def shared(buf, d, items):
+        at = 0
+        for name, n in items:
+            PLACE[name] = (buf, at, n, d)
+            at += (n + 31) // 32 * 32
+        SCRATCH[buf] = ("sbuf", [128, at], d)
+    for name, n in (("w", 512), ("u", K), ("v", K), ("e", 512), ("x0", C), ("x0e", C), ("h", K), ("o", C), ("z", C)):
+        own("q" + name, n, Q)
+        own("s" + name, n, U8)
+    for name, n in (("y", C), ("b", K), ("l", K)):
+        shared("q" + name, Q, [("q%s%d" % (name, t), n) for t in range(R)])
+        shared("s" + name, U8, [("s%s%d" % (name, t), n) for t in range(R)])
+    shared("snd", I32, [("snd%d" % t, 16) for t in range(R)])
+    shared("lnd", I32, [("lnd%d" % t, 16) for t in range(R)])
+    for name, n in (("xt", 4 * C), ("ht", 512), ("ut", 512), ("vt", 512), ("em", 528), ("xf", 16 * 512),
+                    ("zt", 4 * C), ("yt", 4 * C), ("bt", 512), ("eg", 4 * C),
+                    ("r16", C), ("hp", C), ("keep", C), ("dc", C), ("d01", C), ("inc", C), ("d24", K),
+                    ("inct", 288), ("keept", 288), ("sg", C), ("x1", C), ("hh", C), ("bc", C), ("re_", C), ("rt", C),
+                    ("m1", 3 * C), ("m2", 3 * C), ("dd", 8 * C), ("ag", 24 + 8 * C), ("a1", 288), ("nq", 288),
+                    ("nq2", 288), ("gt", 304), ("ct", 304), ("alv", 512), ("pre", 512), ("rg", C), ("jk", 8 * K)):
+        own(name, n, BF)
+    for name, n in (("io5", 512), ("ca", 512), ("pt", 512), ("tab", 256), ("sc", 256), ("yo", 512), ("on", K),
+                    ("df", 24), ("wf", 48), ("nu", 32), ("dcf", K)):
+        own(name, n, F32)
+    shared("fs", F32, (("col", 16), ("kk", 16), ("kn", 8), ("kb", 8), ("nrep", K), ("c1", 24), ("c2", 24), ("c3", 24),
+                       ("c4", 24), ("c5", 24), ("c6", 24), ("c7", 24), ("c8", 24), ("c9", 24), ("uu", 144), ("gq", 32),
+                       ("mn", 32), ("a2", 288), ("cq", 32), ("a15", 8), ("fin", 8), ("fa", K), ("acc", 8), ("fp", K),
+                       ("s1", K), ("s2", K)))
+    own("am", C, HALF)
+    own("amg", C, HALF)
+    own("al", C, HALF)
+    own("nmi", 8, I32)
+    shared("ns", I32, (("pi", 8), ("ci", 24), ("ni", 56), ("lo", 56), ("oo", 56), ("pk", 8), ("bi", 8)))
+    for name, n in (("lje", 24), ("let", 24), ("lti", 18), ("ltj", 18), ("lend", 2), ("lkn", 8), ("lnm", 8),
+                    ("off", 56), ("offp", 24), ("offd", 24), ("lfin", 8), ("lrk", 8), ("lb", 8)):
+        own(name, n, U16)
+    for b in range(8):
+        SCRATCH["ps%d" % b] = ("psum", [128, 512], F32)
+        PLACE["ps%d" % b] = ("ps%d" % b, 0, 512, F32)
+
+
+_declare()
+POOL = {"v": 50, "s": 34, "t": 16, "y": 28, "g": 12}
+SEMAPHORES = (["%s%d" % (e, i) for e in POOL for i in range(POOL[e])]
+              + ["arl%d" % t for t in range(R)] + ["arb%d" % t for t in range(R)] + ["sent"])
+
+
+def _depend(ops):
+    lastw = {b: np.full(SCRATCH[b][1][1], -1) for b in SCRATCH}
+    readers = {b: [] for b in SCRATCH}
+    for i, o in enumerate(ops):
+        need = set(o.get("after", []))
+        for b, idx in o["R"]:
+            need.update(int(d) for d in np.unique(lastw[b][idx]))
+        for b, idx in o["W"]:
+            need.update(int(d) for d in np.unique(lastw[b][idx]))
+            for rd in readers[b]:
+                if rd[1][idx].any():
+                    need.add(rd[0])
+        for b, idx in o["W"]:
+            lastw[b][idx] = i
+            for rd in readers[b]:
+                rd[1][idx] = False
+            readers[b] = [rd for rd in readers[b] if rd[1].any()]
+        for b, idx in o["R"]:
+            m = np.zeros(len(lastw[b]), bool)
+            m[idx] = True
+            readers[b].append((i, m))
+        o["dep"] = sorted(need - {-1, i})
+
+
+def _schedule(ops):
+    pos = {i: k for k, i in enumerate(ORDER)}
+    assert sorted(ORDER) == list(range(len(ops)))
+    assert all(pos[d] < pos[i] for i, o in enumerate(ops) for d in o["dep"])
+    return ORDER
+
+
+def _emit(g, T, ops, tail):
+    queue = {"v": g.vector, "s": g.scalar, "t": g.tensor, "g": g, "y": g.sync}
+    _depend(ops)
+    order = _schedule(ops)
+    pos = {i: k for k, i in enumerate(order)}
+    known = {e: set() for e in queue}
+    for i in order:
+        o = ops[i]
+        if o["e"] == "x":
+            o["known"] = set()
+            continue
+        kn = known[o["e"]]
+        o["waits"] = []
+        for d in sorted(o["dep"], key=lambda d: -pos[d]):
+            if d not in kn:
+                o["waits"].append(d)
+                ops[d]["inc"] = True
+                kn.add(d)
+                kn.update(ops[d]["known"])
+        o["known"] = set(kn)
+    slots = {e: [[None, 0] for _ in range(POOL[e])] for e in POOL}
+    for i in order:
+        o = ops[i]
+        if o["e"] == "x":
+            continue
+        e = "y" if o["dma"] else o["e"]
+        if o["dma"] or o.get("inc"):
+            o["inc"] = True
+            free = [k for k, s in enumerate(slots[e]) if s[0] is None or s[0] in o["known"]]
+            if free:
+                k = free[0]
+            else:
+                k = min(range(POOL[e]), key=lambda m: pos[slots[e][m][0]])
+                o["waits"].append(slots[e][k][0])
+            step = 16 if o["dma"] else 1
+            slots[e][k] = [i, slots[e][k][1] + step]
+            o["sem"], o["val"], o["step"] = "%s%d" % (e, k), slots[e][k][1], step
+    waited = set()
+    for i in order:
+        o = ops[i]
+        if o["e"] == "x":
+            continue
+        for d in o["waits"]:
+            queue[o["e"]].wait_ge(T.sem[ops[d]["sem"]], ops[d]["val"])
+            waited.add(d)
+        ins = o["f"]()
+        if o.get("inc"):
+            ins.then_inc(T.sem[o["sem"]], o["step"])
+    for name, val in tail:
+        g.wait_ge(T.sem[name], val)
+    for i in order:
+        if ops[i]["e"] != "x" and ops[i]["dma"] and i not in waited:
+            queue[ops[i]["e"]].wait_ge(T.sem[ops[i]["sem"]], ops[i]["val"])
+
+
+def rank_program(g, core, T, topo):
+    rank = T.rank_of(core)
+    if rank is None:
+        return
+    nr = len(T.cores)
+    nxt, prv = T.cores[(rank + 1) % nr], T.cores[(rank - 1) % nr]
+    rid, pid = topo.addr(nxt)[0], topo.addr(nxt)[1]
+    mask, n_out, n_in = topo.mask(core, nxt), len(topo.engines(core, nxt)), len(topo.engines(prv, core))
+    VE, SE, PE = g.vector, g.scalar, g.tensor
+    ops = []
+    sent = [0]
+
+    def v(name, a=0, b=None, s=1):
+        buf, at, n, d = PLACE[name]
+        b = n if b is None else b
+        if s > 0:
+            ap, idx = T[buf][:, at + a:at + b:s], np.arange(at + a, at + b, s)
+        else:
+            lo = at + a - 1
+            ap, idx = T[buf][:, slice(at + b - 1, lo if lo >= 0 else None, -1)], np.arange(at + a, at + b)
+        ps = buf.startswith("ps")
+        return {"ap": ap, "use": [(buf, np.arange(512) if ps else idx)], "n": len(idx), "w": WIDTH[d], "ps": ps, "ind": False}
+
+    def ind(win, off, cast=None):
+        ap = win["ap"] if cast is None else win["ap"].bitcast(cast)
+        return {"ap": ap.indirect(off["ap"]), "use": win["use"] + off["use"], "n": 16 * off["n"], "w": 4, "ps": False, "ind": True}
+
+    def op(e, f, outs, ins, c, lat=0.0, dma=False, after=()):
+        rd, wr = [], []
+        for x in ins:
+            if isinstance(x, dict):
+                (wr if x["ps"] else rd).extend(x["use"])
+        for x in outs:
+            wr.append(x["use"][0])
+            rd.extend(x["use"][1:])
+        ops.append({"e": e, "f": f, "R": rd, "W": wr, "c": c, "lat": lat, "dma": dma, "after": list(after)})
+        return len(ops) - 1
+
+    def ap(x):
+        return x["ap"] if isinstance(x, dict) else x
+
+    def cost(out, ins, rate):
+        if out["ind"]:
+            return 60 + 3.9 * out["n"]
+        if ins and ins[0]["ind"]:
+            return 70 + 1.6 * out["n"]
+        if rate == 0.5 and any(x["w"] != 2 for x in [out] + ins):
+            rate = 1
+        return 1.04 * max(64, rate * out["n"])
+
+    def ts(out, a, s1, s2, o0, o1=None):
+        if s2 is None:
+            f = lambda: VE.tensor_scalar(ap(out), ap(a), ap(s1), None, o0)
+        else:
+            f = lambda: VE.tensor_scalar(ap(out), ap(a), ap(s1), ap(s2), o0, o1)
+        op("v", f, [out], [a, s1, s2], cost(out, [a], 0.5))
+
+    def tt(out, a, b, o):
+        op("v", lambda: VE.tensor_tensor(ap(out), ap(a), ap(b), o), [out], [a, b], cost(out, [a, b], 1 if a["ps"] else 2))
+
+    def cp(out, a):
+        op("v", lambda: VE.tensor_copy(ap(out), ap(a)), [out], [a], cost(out, [a], 0.5))
+
+    def scan(out, d0, d1, init, o0, o1):
+        op("v", lambda: VE.tensor_tensor_scan(ap(out), ap(d0), ap(d1), init, o0, o1), [out], [d0, d1], cost(out, [d0, d1], 0.5))
+
+    def tr(out, a):
+        op("v", lambda: VE.transpose(ap(out), ap(a)), [out], [a], cost(out, [a], 0.5))
+
+    def ms(out, c):
+        op("v", lambda: VE.memset(ap(out), c), [out], [], cost(out, [], 0.5))
+
+    def act(out, a, f, **kw):
+        outs = [out] + ([kw["accum_out"]] if "accum_out" in kw else [])
+        ins = [a] + [kw[k] for k in ("bias", "scale") if k in kw]
+        op("s", lambda: SE.activation(ap(out), ap(a), f, **{k: ap(x) for k, x in kw.items()}), outs, ins, cost(out, [a], 1))
+
+    def quant(name, tile, a=0, b=None):
+        q, s = v("q" + name, a, b), v("s" + name, a, b)
+        op("v", lambda: VE.quantize_mx(ap(q), ap(s), ap(tile)), [q, s], [tile], 15 + 0.275 * tile["n"])
+
+    def mm(bank, st, a, mv, c0=0, c1=None):
+        q1, s1, q2, s2 = v("q" + st, a, a + 128), v("s" + st, a, a + 128), v("q" + mv, c0, c1), v("s" + mv, c0, c1)
+        out = v("ps%d" % bank, 0, q2["n"])
+        op("t", lambda: PE.matmul_mx(ap(out), ap(q1), ap(s1), ap(q2), ap(s2), True, True), [out], [q1, s1, q2, s2],
+           0.9 * (q2["n"] + 16))
+
+    def iota(out, pat, base, cm, small=True):
+        kw = {"allow_small_or_imprecise_dtypes": True} if small else {}
+        op("g", lambda: g.iota(ap(out), pat, base, cm, **kw), [out], [], 160 + 2.1 * out["n"])
+
+    def load(out, src, cast=None, e="y"):
+        dst = out["ap"] if cast is None else out["ap"].bitcast(cast)
+        q = g.sync if e == "y" else g.scalar
+        op(e, lambda: q.dma_start(dst, src), [out], [], 60.0, CFG["dma"] + out["n"] * out["w"] * 0.6, True)
+
+    def store(dst, a, src=None, e="y"):
+        q = g.sync if e == "y" else g.scalar
+        op(e, lambda: q.dma_start(dst, ap(a) if src is None else src), [], [a], 60.0, CFG["dma"] + a["n"] * a["w"] * 0.6, True)
+
+    def send(out, a, sem, cast=None):
+        o, i = (out["ap"], a["ap"]) if cast is None else (out["ap"].bitcast(cast), a["ap"].bitcast(cast))
+        sent[0] += n_out
+        return op("g", lambda: g.remote_dma(o, i, T.sem[sem], T.sem.sent, pid, rid, mask), [], [a], 300.0)
+
+    def arrive(sem, val, outs, after):
+        ops.append({"e": "x", "sem": sem, "val": val, "R": [], "W": [x["use"][0] for x in outs], "c": 0.0,
+                    "lat": CFG["far"], "dma": False, "after": after})
+
+    def pick(dst, src, lst):
+        out, a = v("q" + dst), ind(v("q" + src), v(lst), dt.uint32)
+        op("v", lambda: VE.tensor_copy(ap(out).bitcast(dt.uint32), ap(a)), [out], [a], cost(out, [a], 1))
+        act(v("s" + dst), ind(v("s" + src), v(lst)), F.Copy)
+
+    def xpl(t, b):
+        return v("xf", (4 * t + b) * 512, (4 * t + b) * 512 + C)
+
+    def fpl(t, b):
+        return v("xf", (4 * t + 4 + b) * 512 + C, (4 * t + 5 + b) * 512)
+
+    def ps(b, n):
+        return v("ps%d" % b, 0, n)
+
+    cl, ch, csc, cbi, c24, cu, c16h, c2l, cca = (v("col", i, i + 1) for i in range(9))
+
+    for c0, c1 in CFG["cut0"]:
+        load(v("xt", 4 * c0, 4 * c1), T.x[:, 4 * c0:4 * c1])
+    load(v("ut"), T.u[:], None, "s")
+    load(v("nmi"), T.nm[:])
+    load(v("ht"), T.h[:])
+    load(v("qw"), T.wc[:], dt.uint8)
+    load(v("sw"), T.ws[:])
+    load(v("vt"), T.v[:])
+
+    iota(v("pi", 0, 1), [[1, 1]], 0, 1, False)
+    iota(v("r16"), [[0, 24], [1, 16]], 0, 0)
+    iota(v("c1"), [[16, 24]], 0, 0)
+    iota(v("kk", 1, 9), [[16, 4], [64, 2]], 0, 0)
+    iota(v("io5"), [[1, 512]], 0, 0)
+    em = v("em")
+    iota(em, [[0, 528]], 0, 0)
+    op("g", lambda: g.affine_select(ap(em), ap(em), [[-1, 528]], A.not_equal, 0.5, 3, 4), [em], [em], 1300.0)
+    iota(v("pt", 0, C), [[-256, 16], [-4096, 24]], 256 * 383, 0)
+    iota(v("pt", C, 512), [[256, K]], 256 * C, 0)
+    ts(v("pi", 1, 2), v("pi", 0, 1), 15, None, A.bitwise_and)
+    ts(v("pi", 2, 3), v("pi", 0, 1), 4, 1, A.arith_shift_right, A.bitwise_and)
+    cp(v("col", 0, 2), v("pi", 1, 3))
+    for name, base, mark, step in (("inc", 1.0, BIG, 24), ("d24", 24.0, BIG, 16),
+                                   ("inct", 1.0, BIG, 24), ("keept", 1.0, 0.0, 24)):
+        ms(v(name), base)
+        ms(v(name, 0, None, step), mark)
+    ms(v("inct", 1, None, 25), BIG)
+    ms(v("keept", 1, None, 25), 0.0)
+    ts(csc, cl, 7.0, -1.0, A.is_lt, A.mult)
+    ts(cbi, cl, 7.0, -(2.0 ** -100), A.is_ge, A.add)
+    act(c24, cl, F.Copy, scale=24.0)
+    act(cu, cl, F.Identity, scale=-24.0, bias=float(C))
+    act(c16h, ch, F.Identity, scale=16.0, bias=-1.0)
+    act(c2l, cl, F.Identity, scale=2.0, bias=1.0)
+    act(cca, cl, F.Identity, scale=24.0, bias=-float(C))
+    ms(v("kk", 0, 1), 112.0)
+    ms(v("gt", 0, 16), BIG)
+    ms(v("ct", 0, 16), 0.0)
+    ms(v("nu", 24, 32), 0.0)
+    ms(v("sc"), 0.0)
+    act(v("col", 9, 10), cl, F.Copy, scale=-512.0)
+    act(v("keep"), v("r16"), F.Sign)
+    act(v("hh"), v("r16"), F.Sign, bias=6.5, scale=-1.0)
+    act(v("hp"), v("hh"), F.Identity, bias=1.0)
+    act(v("dc"), v("r16"), F.Abs, bias=v("col", 9, 10), scale=512.0)
+    act(v("d01"), v("dc"), F.Relu, bias=1.0, scale=-1.0)
+    act(v("dcf"), v("dc", 0, K), F.Copy, scale=1024.0)
+    act(v("ca"), v("io5"), F.Identity, bias=cca)
+    act(v("c2"), v("c1"), F.Identity, bias=cl)
+    ts(v("lje"), v("c1"), 1.0 / 16, c24, A.mult, A.add)
+    tt(v("kn"), v("kk", 0, 8), v("kk", 1, 9), A.subtract)
+    ts(v("kn"), v("kn"), ch, None, A.mult)
+    tt(v("kn"), v("kn"), v("kk", 1, 9), A.add)
+    ts(v("kn"), v("kn"), 2.0, c2l, A.mult, A.add)
+    act(v("kb"), v("kn"), F.Copy, scale=-BIG)
+    cp(v("lkn"), v("kn"))
+    act(v("nrep"), ind(v("io5"), v("lkn")), F.Copy)
+    ts(v("c3"), v("c2"), -11.5, 1.0 / 24, A.add, A.mult)
+    cp(v("ci"), v("c3"))
+    ts(v("c3"), v("ci"), -24.0, None, A.mult)
+    tt(v("c3"), v("c3"), v("c2"), A.add)
+    ts(v("c4"), v("ci"), 1.0, None, A.add)
+    tt(v("c5"), v("c3"), v("c4"), A.is_ge)
+    tt(v("c6"), v("c5"), v("c4"), A.mult)
+    tt(v("c7"), v("c3"), v("c6"), A.subtract)
+    cp(v("lti"), v("c7", 0, 18))
+    ts(v("c8"), v("c4"), -2.0, 24.0, A.mult, A.add)
+    tt(v("c8"), v("c8"), v("c5"), A.mult)
+    tt(v("c8"), v("c8"), v("c4"), A.add)
+    cp(v("ltj"), v("c8", 0, 18))
+    ts(v("c9", 0, 2), v("c2", 0, 2), 25.0, -9.0, A.mult, A.add)
+    ts(v("c9", 2, 4), v("c2", 0, 2), -24.0, 591.0, A.mult, A.add)
+    tt(v("c9", 4, 6), v("c9", 0, 2), v("c9", 2, 4), A.min)
+    cp(v("lend"), v("c9", 4, 6))
+    ts(v("c5"), v("c3"), 16.0, None, A.mult)
+    tt(v("c5"), v("c5"), v("ci"), A.add)
+    cp(v("let"), v("c5"))
+    quant("u", v("ut"))
+    for c0, c1 in CFG["cut0"]:
+        quant("x0", v("xt", 4 * c0, 4 * c1), c0, c1)
+    quant("h", v("ht"))
+    quant("v", v("vt"))
+    for b in range(4):
+        quant("e", v("em", 3 - b, 515 - b), 128 * b, 128 * b + 128)
+    ts(v("lnm"), v("nmi"), 2.0, 1.0, A.mult, A.add)
+    ts(v("ni", 48, 56), v("nmi"), 2.0, 1.0, A.mult, A.add)
+    cp(ind(v("sc"), v("lnm")), v("io5", 0, K))
+    tt(v("s1"), ind(v("sc"), v("lkn")), v("d01", 0, K), A.mult)
+    scan(v("s2"), v("keep", 0, K), v("s1"), 0.0, A.mult, A.add)
+    pick("x0e", "x0", "lje")
+
+    def unpack_x(t, name, on_v):
+        for b in range(4):
+            mm(4 + b, "e", 128 * b, name)
+            if b in on_v:
+                cp(xpl(t, b), ps(4 + b, C))
+            elif t > 0 or b < 4 - CFG["e_s"]:
+                act(xpl(t, b), ps(4 + b, C), F.Copy)
+
+    def border(t, on_v):
+        for b in range(4):
+            win = ind(v("xf", (4 * t + 4 + b) * 512, (4 * t + 5 + b) * 512), v("lb"))
+            if b in on_v:
+                ts(v("bt", b, None, 4), win, 2.0, None, A.mult)
+            else:
+                act(v("bt", b, None, 4), win, F.Copy, scale=2.0)
+        quant("b%d" % t, v("bt"))
+        s1 = send(v("ql%d" % t), v("qb%d" % t), "arb%d" % t, dt.uint8)
+        s2 = send(v("sl%d" % t), v("sb%d" % t), "arb%d" % t)
+        arrive("arb%d" % t, 2 * n_in, [v("ql%d" % t), v("sl%d" % t)], [s1, s2])
+
+    def diagonal(k, src):
+        scan(v("m1", k * C, (k + 1) * C), src, v("dc"), -1.0, A.max, A.subtract)
+        scan(v("m2", k * C, (k + 1) * C), v("keep"), v("m1", k * C, (k + 1) * C), 0.0, A.mult, A.max)
+
+    for t in range(R):
+        first = t == 0
+        qx = "x0" if first else "y%d" % (t - 1)
+        cut = CFG["cut0"] if first else CFG["cut"]
+        for k, (c0, c1) in enumerate(cut):
+            bank = CFG["pb"][k]
+            mm(bank, "u", 0, qx, c0, c1)
+            act(v("sg", c0, c1), ps(bank, c1 - c0), F.Sign, bias=cbi, scale=csc)
+        for c0, c1 in cut:
+            tr(v("x1", c0, c1), v("sg", c0, c1))
+            scan(v("hh", c0, c1, -1), v("hp", c0, c1, -1), v("x1", c0, c1, -1), 0.0, A.mult, A.add)
+            scan(v("bc", c0, c1), v("keep", c0, c1), v("hh", c0, c1), 0.0, A.mult, A.max)
+            tr(v("rt" if first else "re_", c0, c1), v("bc", c0, c1))
+        if first:
+            act(v("re_"), ind(v("rt"), v("lje")), F.Copy)
+            unpack_x(0, "x0e", ())
+        else:
+            h = CFG["rt_s"]
+            act(v("rt", 0, 16 * h), ind(v("re_"), v("let", 0, h)), F.Copy)
+            cp(v("rt", 16 * h, C), ind(v("re_"), v("let", h, 24)))
+            unpack_x(t, qx, CFG["x_v"])
+            border(t - 1, ())
+            ts(v("ni", 48, 56), v("lnd%d" % (t - 1), 8, 16), 255, None, A.bitwise_and)
+        diagonal(0, v("re_"))
+        diagonal(1, v("rt", 0, C, -1))
+        act(v("wf", 0, 24), v("m2", 15, C, 16), F.Copy)
+        cp(v("ni", 0, 48), v("m2", 15, 2 * C, 16))
+        ts(v("lo"), v("ni"), 1, 15, A.arith_shift_right, A.bitwise_and)
+        tt(v("oo"), v("ni"), v("lo"), A.subtract)
+        ts(v("off"), v("oo"), c16h, None, A.add)
+        for r in range(8):
+            dd = v("dd", C * r, C * (r + 1))
+            if r >= 8 - CFG["neq_s"][t]:
+                act(dd, v("rt"), F.Abs, bias=v("kb", r, r + 1), scale=BIG)
+            else:
+                ts(dd, v("rt"), v("kn", r, r + 1), 4096.0, A.not_equal, A.mult)
+            scan(v("ag", 24 + C * r, 24 + C * (r + 1)), v("inc"), dd, 0.0, A.add, A.min)
+        act(v("a1"), ind(v("wf", 0, 24), v("ltj")), F.Copy)
+        tt(v("nq"), ind(v("wf", 0, 24), v("lti")), v("a1"), A.not_equal)
+        scan(v("gt", 16, 304), v("inct"), v("nq"), 0.0, A.add, A.mult)
+        tt(v("gq"), ind(v("gt"), v("lend")), v("io5", 0, 32), A.subtract)
+        act(v("a15"), v("ag", 23 + C, None, C), F.Copy)
+        if first:
+            cp(v("ag", 23, 24 + 7 * C, C), v("s2", 15, K, 16))
+        else:
+            ts(v("ag", 23, 24 + 7 * C, C), v("lnd%d" % (t - 1), 0, 8), 0.0, None, A.add)
+        scan(v("uu", 0, K), v("d24"), v("ag", 23, 8 * C, 24), 0.0, A.add, A.min)
+        tr(v("tab", 0, K), v("uu", 0, K))
+        act(v("uu", K, K + 16), v("uu", 0, 16), F.Copy)
+        tr(v("tab", K, 2 * K), v("uu", 16, K + 16))
+        act(v("amg"), ind(v("tab"), v("off", 0, 24)), F.Copy)
+        scan(v("am"), v("amg"), v("dc"), -1.0, A.max, A.subtract)
+        scan(v("al"), v("keep"), v("am"), 0.0, A.mult, A.max)
+        tt(v("nu", 0, 24), v("al", 15, C, 16), v("gq", 0, 24), A.min)
+        ts(v("offp"), v("nu", 0, 24), cu, None, A.add)
+        act(v("mn"), v("nu"), F.Relu, bias=-1.0, scale=-1.0)
+        tt(v("alv"), ind(v("tab"), v("off", 24, 56)), v("ca"), A.is_equal)
+        scan(v("pre"), v("alv"), v("alv"), 0.0, A.add, A.max)
+        act(v("rg"), ind(v("pre"), v("offp")), F.Copy)
+        diagonal(2, v("rg"))
+        act(v("a2"), ind(v("nu", 0, 24), v("ltj")), F.Copy)
+        tt(v("nq2"), ind(v("nu", 0, 24), v("lti")), v("a2"), A.is_gt)
+        scan(v("ct", 16, 304), v("keept"), v("nq2"), 0.0, A.mult, A.add)
+        tt(v("cq"), ind(v("ct"), v("lend")), v("mn"), A.subtract)
+        tt(v("df"), v("m2", 2 * C + 15, 3 * C, 16), v("cq", 0, 24), A.add)
+        ts(v("offd"), v("df"), -1.0, None, A.add)
+        if t == R - 1:
+            act(v("wf", 24, 48), v("df"), F.Identity, bias=-1.0)
+            store(T.ol[:, 0:C], v("wf", 24, 48))
+        act(v("fin"), v("uu", 15, K, 16), F.Identity, bias=24.0)
+        tt(v("fin"), v("fin"), v("a15"), A.min)
+        cp(v("lfin"), v("fin"))
+        act(v("fa"), ind(v("io5"), v("lfin")), F.Copy)
+        for r in range(8):
+            act(v("jk", K * r, K * (r + 1)), v("fa"), F.Sign, bias=v("fin", r, r + 1), scale=-1.0, accum_out=v("acc", r, r + 1))
+        ts(v("lrk"), v("acc"), 127.0, 0.5, A.add, A.mult)
+        ts(v("snd%d" % t, 0, 8), v("acc"), 127.0, 0.5, A.add, A.mult)
+        tt(v("fp"), ind(v("pt"), v("lfin")), v("nrep"), A.add)
+        cp(ind(v("sc", 0, K), v("lrk")), v("fp"))
+        scan(v("s1"), v("sc", 0, K), v("dcf"), -1.0, A.max, A.subtract)
+        scan(v("s2"), v("keep", 0, K), v("s1"), 0.0, A.mult, A.max)
+        cp(v("snd%d" % t, 8, 16), v("s2", 15, K, 16))
+        ts(v("bi"), v("snd%d" % t, 8, 16), 8, None, A.arith_shift_right)
+        cp(v("lb"), v("bi"))
+        s1 = send(v("lnd%d" % t), v("snd%d" % t), "arl%d" % t)
+        arrive("arl%d" % t, n_in, [v("lnd%d" % t)], [s1])
+        fq = "h" if first else "l%d" % (t - 1)
+        for b in range(4):
+            mm(b, "e", 128 * b, fq)
+            act(fpl(t, b), ps(b, K), F.Copy)
+        nb = 4 + (4 - CFG["e_s"])
+        for k, (c0, c1) in enumerate(CFG["cut"]):
+            lst = v("offd", c0 // 16, c1 // 16)
+            for b in range(4):
+                z = v("zt", 4 * c0 + b, 4 * c1, 4)
+                if b >= 4 - CFG["e_s"]:
+                    act(v("eg", b * C + c0, b * C + c1), ind(fpl(t, b), lst), F.Copy)
+                    tt(z, v("ps%d" % (4 + b), c0, c1), v("eg", b * C + c0, b * C + c1), A.add)
+                else:
+                    tt(z, ind(fpl(t, b), lst), v("xf", (4 * t + b) * 512 + c0, (4 * t + b) * 512 + c1), A.add)
+            quant("z", v("zt", 4 * c0, 4 * c1), c0, c1)
+        for k, (c0, c1) in enumerate(CFG["cut"]):
+            for b in range(4):
+                bank = (4 * k + b) % nb
+                mm(bank, "w", 128 * b, "z", c0, c1)
+                if b in CFG["y_v"][k]:
+                    ts(v("yt", 4 * c0 + b, 4 * c1, 4), ps(bank, c1 - c0), 0.03125, None, A.mult)
+                else:
+                    act(v("yt", 4 * c0 + b, 4 * c1, 4), ps(bank, c1 - c0), F.Copy, scale=0.03125)
+            quant("y%d" % t, v("yt", 4 * c0, 4 * c1), c0, c1)
+
+    t = R - 1
+    for k, (c0, c1) in enumerate(CFG["cut"]):
+        for b in range(4):
+            bank = CFG["tb"][k][b]
+            mm(bank, "e", 128 * b, "y%d" % t, c0, c1)
+            out = v("xf", (4 * R + b) * 512 + c0, (4 * R + b) * 512 + c1)
+            if b in CFG["tv"][k]:
+                cp(out, ps(bank, c1 - c0))
+            else:
+                act(out, ps(bank, c1 - c0), F.Copy)
+    border(t, (1, 3))
+    pick("o", "y%d" % t, "let")
+    mm(0, "v", 0, "o")
+    store(T.oc[:, 0:4 * C], v("qo"), T.qo[:].bitcast(dt.uint8))
+    for k in range(4):
+        store(T.osc[4 * k:4 * k + 4, 0:C], v("so"), T.so[32 * k:32 * k + 4, :])
+    ts(v("pk"), v("lnd%d" % t, 8, 16), 255, None, A.bitwise_and)
+    cp(v("lnm"), v("pk"))
+    ts(v("on"), ind(v("io5"), v("lnm")), -1.0, 0.5, A.add, A.mult)
+    store(T.ol[:, C:512], v("on"), T.on[0:128:16, :])
+    act(v("yo", 0, C), ps(0, C), F.Copy)
+    store(T.y[:, 0:C], v("yo", 0, C))
+    fq = "l%d" % t
+    mm(1, "v", 0, fq)
+    cp(v("yo", C, 512), ps(1, K))
+    store(T.y[:, C:512], v("yo", C, 512))
+    store(T.oc[:, 4 * C:4 * 512], v("q" + fq), ap(v("q" + fq)).bitcast(dt.uint8), "s")
+    for k in range(4):
+        store(T.osc[4 * k:4 * k + 4, C:512], v("s" + fq), T.sl[32 * k:32 * k + 4, K * t:K * (t + 1)], "s")
+    _emit(g, T, ops, [("sent", sent[0])])

@@ -5,46 +5,38 @@ C, K, R = 384, 128, 3
 BIG = 1024.0
 Q, U8, BF, F32, I32, U16, HALF = "float8_e4m3fn_x4", "uint8", "bfloat16", "float32", "int32", "uint16", "float16"
 CUT = [(0, 192), (192, 384)]
-CFG = {"neq_s": (6, 3, 3), "e_s": 2, "y_v": ((), (3,)), "x_v": (), "cut": CUT, "cut0": CUT, "pb": (2, 3), "rt_s": 14,
-       "tb": ((2, 3, 6, 7), (4, 5, 0, 1)), "tv": ((), (1, 3)), "wake": 90.0, "far": 3500.0, "dma": 2200.0}
 ORDER = [
-    22, 2, 37, 0, 41, 8, 40, 26, 10, 11, 17, 9, 18, 29, 16, 38, 19, 50, 20, 24, 59, 72, 52, 21, 35, 3, 73, 28, 60, 53,
-    36, 4, 25, 63, 61, 12, 44, 33, 45, 23, 54, 43, 32, 68, 62, 74, 27, 55, 64, 31, 57, 56, 39, 75, 42, 69, 88, 89, 1,
-    65, 30, 79, 80, 81, 13, 95, 66, 97, 51, 46, 90, 96, 98, 103, 47, 99, 104, 100, 49, 34, 105, 101, 106, 102, 107, 91,
-    14, 123, 48, 125, 70, 135, 15, 116, 82, 92, 71, 114, 129, 124, 117, 130, 67, 115, 127, 128, 133, 119, 86, 85, 191,
-    120, 134, 126, 193, 137, 138, 118, 131, 139, 136, 132, 140, 7, 58, 143, 144, 121, 94, 145, 147, 87, 146, 122, 148,
-    166, 167, 192, 141, 168, 195, 155, 149, 150, 169, 142, 151, 84, 76, 152, 156, 175, 153, 160, 93, 161, 157, 158, 176,
-    189, 162, 159, 154, 163, 190, 177, 5, 164, 173, 110, 111, 108, 77, 109, 112, 165, 196, 180, 205, 194, 199, 198, 201,
-    206, 170, 200, 113, 197, 202, 172, 207, 174, 208, 171, 203, 204, 209, 178, 6, 217, 218, 213, 211, 214, 215, 212,
-    210, 216, 222, 223, 181, 219, 220, 226, 224, 182, 227, 229, 221, 225, 228, 230, 231, 232, 233, 247, 78, 234, 183,
-    235, 179, 184, 237, 238, 249, 236, 248, 243, 245, 187, 239, 185, 240, 188, 186, 250, 260, 242, 261, 241, 262, 277,
-    244, 283, 273, 263, 281, 269, 253, 275, 264, 271, 284, 279, 285, 278, 265, 251, 254, 280, 246, 270, 282, 276, 274,
-    272, 289, 259, 286, 252, 290, 255, 266, 291, 312, 267, 292, 313, 293, 294, 268, 295, 314, 287, 301, 296, 315, 322,
-    256, 319, 288, 318, 320, 297, 298, 302, 326, 299, 323, 306, 303, 307, 308, 304, 300, 309, 305, 321, 316, 257, 317,
-    324, 258, 337, 338, 310, 311, 341, 335, 336, 344, 339, 340, 343, 342, 345, 351, 346, 347, 348, 350, 354, 352, 349,
-    361, 353, 362, 359, 363, 360, 364, 357, 355, 356, 358, 368, 327, 369, 366, 367, 372, 365, 328, 373, 329, 370, 371,
-    374, 325, 375, 376, 330, 379, 377, 378, 380, 331, 381, 383, 389, 390, 332, 397, 384, 391, 382, 393, 385, 386, 406,
-    387, 394, 388, 407, 419, 423, 415, 408, 420, 424, 409, 333, 334, 425, 392, 429, 426, 399, 427, 421, 417, 416, 395,
-    430, 396, 422, 428, 398, 418, 405, 400, 411, 401, 403, 410, 435, 436, 412, 437, 431, 413, 438, 439, 414, 402, 460,
-    440, 404, 461, 432, 462, 441, 433, 442, 434, 443, 444, 463, 468, 466, 467, 464, 447, 489, 485, 445, 452, 448, 446,
-    449, 465, 453, 474, 454, 450, 470, 483, 455, 484, 490, 451, 456, 471, 457, 498, 487, 488, 486, 491, 495, 496, 493,
-    469, 502, 494, 492, 503, 497, 507, 499, 500, 501, 511, 472, 504, 509, 508, 510, 505, 506, 520, 516, 518, 514, 512,
-    475, 517, 513, 476, 527, 519, 515, 528, 521, 477, 525, 529, 526, 522, 530, 535, 473, 536, 523, 533, 478, 481, 479,
-    480, 534, 537, 538, 540, 531, 482, 541, 524, 532, 539, 542, 543, 548, 83, 547, 550, 551, 552, 549, 544, 559, 555,
-    554, 553, 560, 458, 545, 546, 556, 557, 558, 459, 561, 562, 563, 564, 566, 567, 565, 568]
-WIDTH = {Q: 4, U8: 1, BF: 2, F32: 4, I32: 4, U16: 2, HALF: 2}
+    22,20,26,2,8,17,39,42,11,10,9,12,23,37,18,19,53,1,55,29,41,47,44,3,35,24,76,75,30,62,0,34,28,92,56,91,31,63,82,57,
+    64,4,13,84,100,38,36,45,83,58,15,27,65,66,98,49,48,93,32,101,54,106,99,40,102,67,107,21,103,46,71,68,50,108,59,104,
+    60,69,109,52,105,130,72,94,73,119,95,85,120,110,131,132,128,136,126,25,140,117,5,77,129,70,118,133,127,134,122,121,
+    138,74,141,146,135,137,139,142,14,88,123,147,89,124,148,143,125,149,97,150,151,193,191,78,6,168,169,171,192,144,157,
+    152,145,90,153,194,158,33,154,177,162,87,195,155,16,79,96,43,159,163,111,196,160,164,156,161,113,172,51,175,165,166,
+    189,112,114,167,190,174,170,116,197,205,201,198,115,202,199,176,200,204,203,208,215,213,209,206,173,61,214,207,178,
+    80,211,212,217,218,210,220,180,221,222,181,226,216,223,182,227,219,224,225,228,183,229,81,231,184,249,230,232,179,
+    233,237,234,247,187,250,238,245,235,239,188,236,185,240,186,248,260,246,241,242,261,262,254,253,271,269,275,273,277,
+    279,280,274,270,276,278,283,264,243,244,263,281,252,272,251,284,289,282,265,259,255,290,266,285,286,291,311,267,312,
+    292,256,293,268,294,287,300,295,315,314,313,320,257,288,319,296,301,318,258,297,316,317,323,305,321,298,322,302,324,
+    306,303,307,304,299,334,335,338,332,308,339,325,309,333,310,336,326,337,342,340,344,341,349,347,343,351,345,350,346,
+    360,348,352,354,355,356,327,361,353,357,358,359,363,7,367,368,365,364,362,366,369,370,372,373,371,376,377,374,378,
+    330,375,388,389,386,387,392,328,331,393,380,329,381,382,379,402,432,383,384,403,397,385,404,424,416,405,422,407,418,
+    390,391,414,406,420,412,423,421,413,426,417,419,395,394,396,408,427,425,415,409,398,399,428,433,410,429,434,411,436,
+    435,437,430,456,443,438,431,457,439,440,444,463,464,441,468,448,445,442,449,460,462,446,458,450,447,451,400,461,452,
+    459,465,401,483,484,477,478,479,481,482,480,453,466,485,487,492,486,489,488,494,490,495,496,491,497,501,502,505,506,
+    493,498,469,503,499,454,510,467,504,508,514,511,500,512,507,509,513,521,470,515,523,522,516,519,471,517,472,473,529,
+    524,531,518,475,525,520,530,526,527,474,532,528,535,455,536,533,534,537,86,542,476,541,543,538,539,540,553,547,549,
+    550,559,548,551,554,544,561,560,545,546,562,558,552,555,556,557]
 SCRATCH, PLACE = {}, {}
 
 
 def _declare():
     def own(name, n, d):
         SCRATCH[name] = ("sbuf", [128, n], d)
-        PLACE[name] = (name, 0, n, d)
+        PLACE[name] = (name, 0, n)
 
     def shared(buf, d, items):
         at = 0
         for name, n in items:
-            PLACE[name] = (buf, at, n, d)
+            PLACE[name] = (buf, at, n)
             at += (n + 31) // 32 * 32
         SCRATCH[buf] = ("sbuf", [128, at], d)
     for name, n in (("w", 512), ("u", K), ("v", K), ("e", 512), ("x0", C), ("x0e", C), ("h", K), ("o", C), ("z", C)):
@@ -57,29 +49,28 @@ def _declare():
     shared("lnd", I32, [("lnd%d" % t, 16) for t in range(R)])
     for name, n in (("xt", 4 * C), ("ht", 512), ("ut", 512), ("vt", 512), ("em", 528), ("xf", 16 * 512),
                     ("zt", 4 * C), ("yt", 4 * C), ("bt", 512), ("eg", 4 * C),
-                    ("r16", C), ("hp", C), ("keep", C), ("dc", C), ("d01", C), ("inc", C), ("d24", K),
+                    ("r16", C), ("hp", C), ("keep", C), ("dc", C), ("d01", C), ("inc", C), ("d24", 136),
                     ("inct", 288), ("keept", 288), ("sg", C), ("x1", C), ("hh", C), ("bc", C), ("re_", C), ("rt", C),
-                    ("m1", 3 * C), ("m2", 3 * C), ("dd", 8 * C), ("ag", 24 + 8 * C), ("a1", 288), ("nq", 288),
+                    ("m1", 3 * C), ("m2", 3 * C), ("dd", 8 * C), ("ag", 8 * 408), ("a1", 288), ("nq", 288),
                     ("nq2", 288), ("gt", 304), ("ct", 304), ("alv", 512), ("pre", 512), ("rg", C), ("jk", 8 * K)):
         own(name, n, BF)
     for name, n in (("io5", 512), ("ca", 512), ("pt", 512), ("tab", 256), ("sc", 256), ("yo", 512), ("on", K),
                     ("df", 24), ("wf", 48), ("nu", 32), ("dcf", K)):
         own(name, n, F32)
     shared("fs", F32, (("col", 16), ("kk", 16), ("kn", 8), ("kb", 8), ("nrep", K), ("c1", 24), ("c2", 24), ("c3", 24),
-                       ("c4", 24), ("c5", 24), ("c6", 24), ("c7", 24), ("c8", 24), ("c9", 24), ("uu", 144), ("gq", 32),
-                       ("mn", 32), ("a2", 288), ("cq", 32), ("a15", 8), ("fin", 8), ("fa", K), ("acc", 8), ("fp", K),
-                       ("s1", K), ("s2", K)))
-    own("am", C, HALF)
-    own("amg", C, HALF)
-    own("al", C, HALF)
+                       ("c4", 24), ("c5", 24), ("c6", 24), ("c7", 24), ("c8", 24), ("c9", 24), ("uu", 144),
+                       ("u17", 136), ("k17", 10), ("gq", 32), ("mn", 32), ("a2", 288), ("cq", 32), ("fa", K),
+                       ("acc", 8), ("fp", K), ("s1", K), ("s2", K)))
+    for name in ("am", "amg", "al"):
+        own(name, C, HALF)
     own("nmi", 8, I32)
     shared("ns", I32, (("pi", 8), ("ci", 24), ("ni", 56), ("lo", 56), ("oo", 56), ("pk", 8), ("bi", 8)))
     for name, n in (("lje", 24), ("let", 24), ("lti", 18), ("ltj", 18), ("lend", 2), ("lkn", 8), ("lnm", 8),
-                    ("off", 56), ("offp", 24), ("offd", 24), ("lfin", 8), ("lrk", 8), ("lb", 8)):
+                    ("off", 56), ("offp", 24), ("offd", 24), ("lfin", 8), ("l17", 10), ("lrk", 8), ("lb", 8)):
         own(name, n, U16)
     for b in range(8):
         SCRATCH["ps%d" % b] = ("psum", [128, 512], F32)
-        PLACE["ps%d" % b] = ("ps%d" % b, 0, 512, F32)
+        PLACE["ps%d" % b] = ("ps%d" % b, 0, 512)
 
 
 _declare()
@@ -92,7 +83,7 @@ def _depend(ops):
     lastw = {b: np.full(SCRATCH[b][1][1], -1) for b in SCRATCH}
     readers = {b: [] for b in SCRATCH}
     for i, o in enumerate(ops):
-        need = set(o.get("after", []))
+        need = set(o["after"])
         for b, idx in o["R"]:
             need.update(int(d) for d in np.unique(lastw[b][idx]))
         for b, idx in o["W"]:
@@ -112,20 +103,14 @@ def _depend(ops):
         o["dep"] = sorted(need - {-1, i})
 
 
-def _schedule(ops):
-    pos = {i: k for k, i in enumerate(ORDER)}
-    assert sorted(ORDER) == list(range(len(ops)))
-    assert all(pos[d] < pos[i] for i, o in enumerate(ops) for d in o["dep"])
-    return ORDER
-
-
 def _emit(g, T, ops, tail):
     queue = {"v": g.vector, "s": g.scalar, "t": g.tensor, "g": g, "y": g.sync}
     _depend(ops)
-    order = _schedule(ops)
-    pos = {i: k for k, i in enumerate(order)}
+    pos = {i: k for k, i in enumerate(ORDER)}
+    assert sorted(ORDER) == list(range(len(ops)))
+    assert all(pos[d] < pos[i] for i, o in enumerate(ops) for d in o["dep"])
     known = {e: set() for e in queue}
-    for i in order:
+    for i in ORDER:
         o = ops[i]
         if o["e"] == "x":
             o["known"] = set()
@@ -139,11 +124,10 @@ def _emit(g, T, ops, tail):
                 kn.add(d)
                 kn.update(ops[d]["known"])
         o["known"] = set(kn)
+    own = [i for i in ORDER if ops[i]["e"] != "x"]
     slots = {e: [[None, 0] for _ in range(POOL[e])] for e in POOL}
-    for i in order:
+    for i in own:
         o = ops[i]
-        if o["e"] == "x":
-            continue
         e = "y" if o["dma"] else o["e"]
         if o["dma"] or o.get("inc"):
             o["inc"] = True
@@ -157,10 +141,8 @@ def _emit(g, T, ops, tail):
             slots[e][k] = [i, slots[e][k][1] + step]
             o["sem"], o["val"], o["step"] = "%s%d" % (e, k), slots[e][k][1], step
     waited = set()
-    for i in order:
+    for i in own:
         o = ops[i]
-        if o["e"] == "x":
-            continue
         for d in o["waits"]:
             queue[o["e"]].wait_ge(T.sem[ops[d]["sem"]], ops[d]["val"])
             waited.add(d)
@@ -169,8 +151,8 @@ def _emit(g, T, ops, tail):
             ins.then_inc(T.sem[o["sem"]], o["step"])
     for name, val in tail:
         g.wait_ge(T.sem[name], val)
-    for i in order:
-        if ops[i]["e"] != "x" and ops[i]["dma"] and i not in waited:
+    for i in own:
+        if ops[i]["dma"] and i not in waited:
             queue[ops[i]["e"]].wait_ge(T.sem[ops[i]["sem"]], ops[i]["val"])
 
 
@@ -187,7 +169,7 @@ def rank_program(g, core, T, topo):
     sent = [0]
 
     def v(name, a=0, b=None, s=1):
-        buf, at, n, d = PLACE[name]
+        buf, at, n = PLACE[name]
         b = n if b is None else b
         if s > 0:
             ap, idx = T[buf][:, at + a:at + b:s], np.arange(at + a, at + b, s)
@@ -195,13 +177,13 @@ def rank_program(g, core, T, topo):
             lo = at + a - 1
             ap, idx = T[buf][:, slice(at + b - 1, lo if lo >= 0 else None, -1)], np.arange(at + a, at + b)
         ps = buf.startswith("ps")
-        return {"ap": ap, "use": [(buf, np.arange(512) if ps else idx)], "n": len(idx), "w": WIDTH[d], "ps": ps, "ind": False}
+        return {"ap": ap, "use": [(buf, np.arange(512) if ps else idx)], "n": len(idx), "ps": ps}
 
     def ind(win, off, cast=None):
         ap = win["ap"] if cast is None else win["ap"].bitcast(cast)
-        return {"ap": ap.indirect(off["ap"]), "use": win["use"] + off["use"], "n": 16 * off["n"], "w": 4, "ps": False, "ind": True}
+        return {"ap": ap.indirect(off["ap"]), "use": win["use"] + off["use"], "ps": False}
 
-    def op(e, f, outs, ins, c, lat=0.0, dma=False, after=()):
+    def op(e, f, outs, ins, dma=False):
         rd, wr = [], []
         for x in ins:
             if isinstance(x, dict):
@@ -209,97 +191,84 @@ def rank_program(g, core, T, topo):
         for x in outs:
             wr.append(x["use"][0])
             rd.extend(x["use"][1:])
-        ops.append({"e": e, "f": f, "R": rd, "W": wr, "c": c, "lat": lat, "dma": dma, "after": list(after)})
+        ops.append({"e": e, "f": f, "R": rd, "W": wr, "dma": dma, "after": []})
         return len(ops) - 1
 
     def ap(x):
         return x["ap"] if isinstance(x, dict) else x
 
-    def cost(out, ins, rate):
-        if out["ind"]:
-            return 60 + 3.9 * out["n"]
-        if ins and ins[0]["ind"]:
-            return 70 + 1.6 * out["n"]
-        if rate == 0.5 and any(x["w"] != 2 for x in [out] + ins):
-            rate = 1
-        return 1.04 * max(64, rate * out["n"])
-
     def ts(out, a, s1, s2, o0, o1=None):
-        if s2 is None:
-            f = lambda: VE.tensor_scalar(ap(out), ap(a), ap(s1), None, o0)
-        else:
-            f = lambda: VE.tensor_scalar(ap(out), ap(a), ap(s1), ap(s2), o0, o1)
-        op("v", f, [out], [a, s1, s2], cost(out, [a], 0.5))
+        tail = (o0,) if s2 is None else (o0, o1)
+        op("v", lambda: VE.tensor_scalar(ap(out), ap(a), ap(s1), ap(s2), *tail), [out], [a, s1, s2])
 
     def tt(out, a, b, o):
-        op("v", lambda: VE.tensor_tensor(ap(out), ap(a), ap(b), o), [out], [a, b], cost(out, [a, b], 1 if a["ps"] else 2))
+        op("v", lambda: VE.tensor_tensor(ap(out), ap(a), ap(b), o), [out], [a, b])
 
     def cp(out, a):
-        op("v", lambda: VE.tensor_copy(ap(out), ap(a)), [out], [a], cost(out, [a], 0.5))
+        op("v", lambda: VE.tensor_copy(ap(out), ap(a)), [out], [a])
 
     def scan(out, d0, d1, init, o0, o1):
-        op("v", lambda: VE.tensor_tensor_scan(ap(out), ap(d0), ap(d1), init, o0, o1), [out], [d0, d1], cost(out, [d0, d1], 0.5))
+        op("v", lambda: VE.tensor_tensor_scan(ap(out), ap(d0), ap(d1), init, o0, o1), [out], [d0, d1])
 
     def tr(out, a):
-        op("v", lambda: VE.transpose(ap(out), ap(a)), [out], [a], cost(out, [a], 0.5))
+        op("v", lambda: VE.transpose(ap(out), ap(a)), [out], [a])
 
     def ms(out, c):
-        op("v", lambda: VE.memset(ap(out), c), [out], [], cost(out, [], 0.5))
+        op("v", lambda: VE.memset(ap(out), c), [out], [])
 
     def act(out, a, f, **kw):
         outs = [out] + ([kw["accum_out"]] if "accum_out" in kw else [])
         ins = [a] + [kw[k] for k in ("bias", "scale") if k in kw]
-        op("s", lambda: SE.activation(ap(out), ap(a), f, **{k: ap(x) for k, x in kw.items()}), outs, ins, cost(out, [a], 1))
+        op("s", lambda: SE.activation(ap(out), ap(a), f, **{k: ap(x) for k, x in kw.items()}), outs, ins)
 
     def quant(name, tile, a=0, b=None):
         q, s = v("q" + name, a, b), v("s" + name, a, b)
-        op("v", lambda: VE.quantize_mx(ap(q), ap(s), ap(tile)), [q, s], [tile], 15 + 0.275 * tile["n"])
+        op("v", lambda: VE.quantize_mx(ap(q), ap(s), ap(tile)), [q, s], [tile])
 
     def mm(bank, st, a, mv, c0=0, c1=None):
         q1, s1, q2, s2 = v("q" + st, a, a + 128), v("s" + st, a, a + 128), v("q" + mv, c0, c1), v("s" + mv, c0, c1)
         out = v("ps%d" % bank, 0, q2["n"])
-        op("t", lambda: PE.matmul_mx(ap(out), ap(q1), ap(s1), ap(q2), ap(s2), True, True), [out], [q1, s1, q2, s2],
-           0.9 * (q2["n"] + 16))
+        op("t", lambda: PE.matmul_mx(ap(out), ap(q1), ap(s1), ap(q2), ap(s2), True, True), [out], [q1, s1, q2, s2])
 
     def iota(out, pat, base, cm, small=True):
         kw = {"allow_small_or_imprecise_dtypes": True} if small else {}
-        op("g", lambda: g.iota(ap(out), pat, base, cm, **kw), [out], [], 160 + 2.1 * out["n"])
+        op("g", lambda: g.iota(ap(out), pat, base, cm, **kw), [out], [])
 
     def load(out, src, cast=None, e="y"):
         dst = out["ap"] if cast is None else out["ap"].bitcast(cast)
         q = g.sync if e == "y" else g.scalar
-        op(e, lambda: q.dma_start(dst, src), [out], [], 60.0, CFG["dma"] + out["n"] * out["w"] * 0.6, True)
+        op(e, lambda: q.dma_start(dst, src), [out], [], True)
 
     def store(dst, a, src=None, e="y"):
         q = g.sync if e == "y" else g.scalar
-        op(e, lambda: q.dma_start(dst, ap(a) if src is None else src), [], [a], 60.0, CFG["dma"] + a["n"] * a["w"] * 0.6, True)
+        op(e, lambda: q.dma_start(dst, ap(a) if src is None else src), [], [a], True)
 
     def send(out, a, sem, cast=None):
         o, i = (out["ap"], a["ap"]) if cast is None else (out["ap"].bitcast(cast), a["ap"].bitcast(cast))
         sent[0] += n_out
-        return op("g", lambda: g.remote_dma(o, i, T.sem[sem], T.sem.sent, pid, rid, mask), [], [a], 300.0)
+        return op("g", lambda: g.remote_dma(o, i, T.sem[sem], T.sem.sent, pid, rid, mask), [], [a])
 
     def arrive(sem, val, outs, after):
-        ops.append({"e": "x", "sem": sem, "val": val, "R": [], "W": [x["use"][0] for x in outs], "c": 0.0,
-                    "lat": CFG["far"], "dma": False, "after": after})
+        ops.append({"e": "x", "sem": sem, "val": val, "R": [], "W": [x["use"][0] for x in outs], "dma": False,
+                    "after": after})
 
     def pick(dst, src, lst):
         out, a = v("q" + dst), ind(v("q" + src), v(lst), dt.uint32)
-        op("v", lambda: VE.tensor_copy(ap(out).bitcast(dt.uint32), ap(a)), [out], [a], cost(out, [a], 1))
+        op("v", lambda: VE.tensor_copy(ap(out).bitcast(dt.uint32), ap(a)), [out], [a])
         act(v("s" + dst), ind(v("s" + src), v(lst)), F.Copy)
 
-    def xpl(t, b):
-        return v("xf", (4 * t + b) * 512, (4 * t + b) * 512 + C)
+    def xpl(t, b, c0=0, c1=C):
+        return v("xf", (4 * t + b) * 512 + c0, (4 * t + b) * 512 + c1)
 
     def fpl(t, b):
-        return v("xf", (4 * t + 4 + b) * 512 + C, (4 * t + 5 + b) * 512)
+        return xpl(t + 1, b, C, 512)
 
     def ps(b, n):
         return v("ps%d" % b, 0, n)
 
     cl, ch, csc, cbi, c24, cu, c16h, c2l, cca = (v("col", i, i + 1) for i in range(9))
 
-    for c0, c1 in CFG["cut0"]:
+    for c0, c1 in CUT:
         load(v("xt", 4 * c0, 4 * c1), T.x[:, 4 * c0:4 * c1])
     load(v("ut"), T.u[:], None, "s")
     load(v("nmi"), T.nm[:])
@@ -315,13 +284,13 @@ def rank_program(g, core, T, topo):
     iota(v("io5"), [[1, 512]], 0, 0)
     em = v("em")
     iota(em, [[0, 528]], 0, 0)
-    op("g", lambda: g.affine_select(ap(em), ap(em), [[-1, 528]], A.not_equal, 0.5, 3, 4), [em], [em], 1300.0)
+    op("g", lambda: g.affine_select(ap(em), ap(em), [[-1, 528]], A.not_equal, 0.5, 3, 4), [em], [em])
     iota(v("pt", 0, C), [[-256, 16], [-4096, 24]], 256 * 383, 0)
     iota(v("pt", C, 512), [[256, K]], 256 * C, 0)
     ts(v("pi", 1, 2), v("pi", 0, 1), 15, None, A.bitwise_and)
     ts(v("pi", 2, 3), v("pi", 0, 1), 4, 1, A.arith_shift_right, A.bitwise_and)
     cp(v("col", 0, 2), v("pi", 1, 3))
-    for name, base, mark, step in (("inc", 1.0, BIG, 24), ("d24", 24.0, BIG, 16),
+    for name, base, mark, step in (("inc", 1.0, BIG, 24), ("d24", 24.0, BIG, 17),
                                    ("inct", 1.0, BIG, 24), ("keept", 1.0, 0.0, 24)):
         ms(v(name), base)
         ms(v(name, 0, None, step), mark)
@@ -335,6 +304,9 @@ def rank_program(g, core, T, topo):
     act(c2l, cl, F.Identity, scale=2.0, bias=1.0)
     act(cca, cl, F.Identity, scale=24.0, bias=-float(C))
     ms(v("kk", 0, 1), 112.0)
+    iota(v("k17", 0, 8), [[17, 8]], 0, 0)
+    ms(v("k17", 8, 9), 0.0)
+    ts(v("l17", 0, 9), v("k17", 0, 9), cl, None, A.add)
     ms(v("gt", 0, 16), BIG)
     ms(v("ct", 0, 16), 0.0)
     ms(v("nu", 24, 32), 0.0)
@@ -377,7 +349,7 @@ def rank_program(g, core, T, topo):
     tt(v("c5"), v("c5"), v("ci"), A.add)
     cp(v("let"), v("c5"))
     quant("u", v("ut"))
-    for c0, c1 in CFG["cut0"]:
+    for c0, c1 in CUT:
         quant("x0", v("xt", 4 * c0, 4 * c1), c0, c1)
     quant("h", v("ht"))
     quant("v", v("vt"))
@@ -390,17 +362,15 @@ def rank_program(g, core, T, topo):
     scan(v("s2"), v("keep", 0, K), v("s1"), 0.0, A.mult, A.add)
     pick("x0e", "x0", "lje")
 
-    def unpack_x(t, name, on_v):
+    def unpack_x(t, name):
         for b in range(4):
             mm(4 + b, "e", 128 * b, name)
-            if b in on_v:
-                cp(xpl(t, b), ps(4 + b, C))
-            elif t > 0 or b < 4 - CFG["e_s"]:
+            if t > 0 or b < 2:
                 act(xpl(t, b), ps(4 + b, C), F.Copy)
 
     def border(t, on_v):
         for b in range(4):
-            win = ind(v("xf", (4 * t + 4 + b) * 512, (4 * t + 5 + b) * 512), v("lb"))
+            win = ind(xpl(t + 1, b, 0, 512), v("lb"))
             if b in on_v:
                 ts(v("bt", b, None, 4), win, 2.0, None, A.mult)
             else:
@@ -417,24 +387,21 @@ def rank_program(g, core, T, topo):
     for t in range(R):
         first = t == 0
         qx = "x0" if first else "y%d" % (t - 1)
-        cut = CFG["cut0"] if first else CFG["cut"]
-        for k, (c0, c1) in enumerate(cut):
-            bank = CFG["pb"][k]
-            mm(bank, "u", 0, qx, c0, c1)
-            act(v("sg", c0, c1), ps(bank, c1 - c0), F.Sign, bias=cbi, scale=csc)
-        for c0, c1 in cut:
+        for k, (c0, c1) in enumerate(CUT):
+            mm(2 + k, "u", 0, qx, c0, c1)
+            act(v("sg", c0, c1), ps(2 + k, c1 - c0), F.Sign, bias=cbi, scale=csc)
+        for c0, c1 in CUT:
             tr(v("x1", c0, c1), v("sg", c0, c1))
             scan(v("hh", c0, c1, -1), v("hp", c0, c1, -1), v("x1", c0, c1, -1), 0.0, A.mult, A.add)
             scan(v("bc", c0, c1), v("keep", c0, c1), v("hh", c0, c1), 0.0, A.mult, A.max)
             tr(v("rt" if first else "re_", c0, c1), v("bc", c0, c1))
         if first:
             act(v("re_"), ind(v("rt"), v("lje")), F.Copy)
-            unpack_x(0, "x0e", ())
+            unpack_x(0, "x0e")
         else:
-            h = CFG["rt_s"]
-            act(v("rt", 0, 16 * h), ind(v("re_"), v("let", 0, h)), F.Copy)
-            cp(v("rt", 16 * h, C), ind(v("re_"), v("let", h, 24)))
-            unpack_x(t, qx, CFG["x_v"])
+            act(v("rt", 0, 224), ind(v("re_"), v("let", 0, 14)), F.Copy)
+            cp(v("rt", 224, C), ind(v("re_"), v("let", 14, 24)))
+            unpack_x(t, qx)
             border(t - 1, ())
             ts(v("ni", 48, 56), v("lnd%d" % (t - 1), 8, 16), 255, None, A.bitwise_and)
         diagonal(0, v("re_"))
@@ -446,23 +413,22 @@ def rank_program(g, core, T, topo):
         ts(v("off"), v("oo"), c16h, None, A.add)
         for r in range(8):
             dd = v("dd", C * r, C * (r + 1))
-            if r >= 8 - CFG["neq_s"][t]:
+            if r >= (2 if first else 5):
                 act(dd, v("rt"), F.Abs, bias=v("kb", r, r + 1), scale=BIG)
             else:
                 ts(dd, v("rt"), v("kn", r, r + 1), 4096.0, A.not_equal, A.mult)
-            scan(v("ag", 24 + C * r, 24 + C * (r + 1)), v("inc"), dd, 0.0, A.add, A.min)
+            scan(v("ag", 24 + 408 * r, 408 * (r + 1)), v("inc"), dd, 0.0, A.add, A.min)
         act(v("a1"), ind(v("wf", 0, 24), v("ltj")), F.Copy)
         tt(v("nq"), ind(v("wf", 0, 24), v("lti")), v("a1"), A.not_equal)
         scan(v("gt", 16, 304), v("inct"), v("nq"), 0.0, A.add, A.mult)
         tt(v("gq"), ind(v("gt"), v("lend")), v("io5", 0, 32), A.subtract)
-        act(v("a15"), v("ag", 23 + C, None, C), F.Copy)
         if first:
-            cp(v("ag", 23, 24 + 7 * C, C), v("s2", 15, K, 16))
+            cp(v("ag", 23, None, 408), v("s2", 15, K, 16))
         else:
-            ts(v("ag", 23, 24 + 7 * C, C), v("lnd%d" % (t - 1), 0, 8), 0.0, None, A.add)
-        scan(v("uu", 0, K), v("d24"), v("ag", 23, 8 * C, 24), 0.0, A.add, A.min)
+            ts(v("ag", 23, None, 408), v("lnd%d" % (t - 1), 0, 8), 0.0, None, A.add)
+        scan(v("u17"), v("d24"), v("ag", 23, None, 24), 0.0, A.add, A.min)
+        act(v("uu"), ind(v("u17"), v("l17", 0, 9)), F.Copy)
         tr(v("tab", 0, K), v("uu", 0, K))
-        act(v("uu", K, K + 16), v("uu", 0, 16), F.Copy)
         tr(v("tab", K, 2 * K), v("uu", 16, K + 16))
         act(v("amg"), ind(v("tab"), v("off", 0, 24)), F.Copy)
         scan(v("am"), v("amg"), v("dc"), -1.0, A.max, A.subtract)
@@ -483,12 +449,11 @@ def rank_program(g, core, T, topo):
         if t == R - 1:
             act(v("wf", 24, 48), v("df"), F.Identity, bias=-1.0)
             store(T.ol[:, 0:C], v("wf", 24, 48))
-        act(v("fin"), v("uu", 15, K, 16), F.Identity, bias=24.0)
-        tt(v("fin"), v("fin"), v("a15"), A.min)
-        cp(v("lfin"), v("fin"))
+        cp(v("lfin"), v("u17", 16, None, 17))
         act(v("fa"), ind(v("io5"), v("lfin")), F.Copy)
         for r in range(8):
-            act(v("jk", K * r, K * (r + 1)), v("fa"), F.Sign, bias=v("fin", r, r + 1), scale=-1.0, accum_out=v("acc", r, r + 1))
+            act(v("jk", K * r, K * (r + 1)), v("fa"), F.Sign, bias=v("u17", 17 * r + 16, 17 * r + 17), scale=-1.0,
+                accum_out=v("acc", r, r + 1))
         ts(v("lrk"), v("acc"), 127.0, 0.5, A.add, A.mult)
         ts(v("snd%d" % t, 0, 8), v("acc"), 127.0, 0.5, A.add, A.mult)
         tt(v("fp"), ind(v("pt"), v("lfin")), v("nrep"), A.add)
@@ -504,37 +469,35 @@ def rank_program(g, core, T, topo):
         for b in range(4):
             mm(b, "e", 128 * b, fq)
             act(fpl(t, b), ps(b, K), F.Copy)
-        nb = 4 + (4 - CFG["e_s"])
-        for k, (c0, c1) in enumerate(CFG["cut"]):
+        for c0, c1 in CUT:
             lst = v("offd", c0 // 16, c1 // 16)
             for b in range(4):
                 z = v("zt", 4 * c0 + b, 4 * c1, 4)
-                if b >= 4 - CFG["e_s"]:
+                if b >= 2:
                     act(v("eg", b * C + c0, b * C + c1), ind(fpl(t, b), lst), F.Copy)
                     tt(z, v("ps%d" % (4 + b), c0, c1), v("eg", b * C + c0, b * C + c1), A.add)
                 else:
-                    tt(z, ind(fpl(t, b), lst), v("xf", (4 * t + b) * 512 + c0, (4 * t + b) * 512 + c1), A.add)
+                    tt(z, ind(fpl(t, b), lst), xpl(t, b, c0, c1), A.add)
             quant("z", v("zt", 4 * c0, 4 * c1), c0, c1)
-        for k, (c0, c1) in enumerate(CFG["cut"]):
+        for k, (c0, c1) in enumerate(CUT):
             for b in range(4):
-                bank = (4 * k + b) % nb
+                bank = (4 * k + b) % 6
                 mm(bank, "w", 128 * b, "z", c0, c1)
-                if b in CFG["y_v"][k]:
+                if k == 1 and b % 2:
                     ts(v("yt", 4 * c0 + b, 4 * c1, 4), ps(bank, c1 - c0), 0.03125, None, A.mult)
                 else:
                     act(v("yt", 4 * c0 + b, 4 * c1, 4), ps(bank, c1 - c0), F.Copy, scale=0.03125)
             quant("y%d" % t, v("yt", 4 * c0, 4 * c1), c0, c1)
 
     t = R - 1
-    for k, (c0, c1) in enumerate(CFG["cut"]):
+    for k, (c0, c1) in enumerate(CUT):
         for b in range(4):
-            bank = CFG["tb"][k][b]
+            bank = ((2, 3, 6, 7), (4, 5, 0, 1))[k][b]
             mm(bank, "e", 128 * b, "y%d" % t, c0, c1)
-            out = v("xf", (4 * R + b) * 512 + c0, (4 * R + b) * 512 + c1)
-            if b in CFG["tv"][k]:
-                cp(out, ps(bank, c1 - c0))
+            if k == 1 and b % 2:
+                cp(xpl(R, b, c0, c1), ps(bank, c1 - c0))
             else:
-                act(out, ps(bank, c1 - c0), F.Copy)
+                act(xpl(R, b, c0, c1), ps(bank, c1 - c0), F.Copy)
     border(t, (1, 3))
     pick("o", "y%d" % t, "let")
     mm(0, "v", 0, "o")
@@ -553,5 +516,6 @@ def rank_program(g, core, T, topo):
     store(T.y[:, C:512], v("yo", C, 512))
     store(T.oc[:, 4 * C:4 * 512], v("q" + fq), ap(v("q" + fq)).bitcast(dt.uint8), "s")
     for k in range(4):
-        store(T.osc[4 * k:4 * k + 4, C:512], v("s" + fq), T.sl[32 * k:32 * k + 4, K * t:K * (t + 1)], "s")
+        store(T.osc[4 * k:4 * k + 4, C:512], v("s" + fq), T.sl[32 * k:32 * k + 4, K * t:K * (t + 1)],
+              "s" if k < 2 else "y")
     _emit(g, T, ops, [("sent", sent[0])])

@@ -2,30 +2,24 @@ import numpy as np
 from concourse.mybir import dt, AluOpType as A, ActivationFunctionType as F
 
 C, K, R = 384, 128, 3
-BIG = 1024.0
+SEG = 24
+PIECES = [(0, 12), (12, 24)]
+ON_S = {"match": (6, 4), "mix": (2, 3), "y": ((0, 1, 2, 3), (0, 2)), "count": (0, 1)}
+XB, YB, FB, PB = (1, 5, 6, 7), ((0, 2, 3, 4), (4, 5, 1, 0)), (2, 3), (0, 4)
+WAKE, HOP, FIRST, LOAD, CYCLE = 0.22, 1.8, 1.0, 1.8, 0.00092
+SEED, TRIES, TEMP, NOISE, WIN = 0, 2000, 0.03, 0.7, 1.5
 Q, U8, BF, F32, I32, U16, HALF = "float8_e4m3fn_x4", "uint8", "bfloat16", "float32", "int32", "uint16", "float16"
-CUT = [(0, 192), (192, 384)]
-ORDER = [
-    22,20,26,2,8,17,39,42,11,10,9,12,23,37,18,19,53,1,55,29,41,47,44,3,35,24,76,75,30,62,0,34,28,92,56,91,31,63,82,57,
-    64,4,13,84,100,38,36,45,83,58,15,27,65,66,98,49,48,93,32,101,54,106,99,40,102,67,107,21,103,46,71,68,50,108,59,104,
-    60,69,109,52,105,130,72,94,73,119,95,85,120,110,131,132,128,136,126,25,140,117,5,77,129,70,118,133,127,134,122,121,
-    138,74,141,146,135,137,139,142,14,88,123,147,89,124,148,143,125,149,97,150,151,193,191,78,6,168,169,171,192,144,157,
-    152,145,90,153,194,158,33,154,177,162,87,195,155,16,79,96,43,159,163,111,196,160,164,156,161,113,172,51,175,165,166,
-    189,112,114,167,190,174,170,116,197,205,201,198,115,202,199,176,200,204,203,208,215,213,209,206,173,61,214,207,178,
-    80,211,212,217,218,210,220,180,221,222,181,226,216,223,182,227,219,224,225,228,183,229,81,231,184,249,230,232,179,
-    233,237,234,247,187,250,238,245,235,239,188,236,185,240,186,248,260,246,241,242,261,262,254,253,271,269,275,273,277,
-    279,280,274,270,276,278,283,264,243,244,263,281,252,272,251,284,289,282,265,259,255,290,266,285,286,291,311,267,312,
-    292,256,293,268,294,287,300,295,315,314,313,320,257,288,319,296,301,318,258,297,316,317,323,305,321,298,322,302,324,
-    306,303,307,304,299,334,335,338,332,308,339,325,309,333,310,336,326,337,342,340,344,341,349,347,343,351,345,350,346,
-    360,348,352,354,355,356,327,361,353,357,358,359,363,7,367,368,365,364,362,366,369,370,372,373,371,376,377,374,378,
-    330,375,388,389,386,387,392,328,331,393,380,329,381,382,379,402,432,383,384,403,397,385,404,424,416,405,422,407,418,
-    390,391,414,406,420,412,423,421,413,426,417,419,395,394,396,408,427,425,415,409,398,399,428,433,410,429,434,411,436,
-    435,437,430,456,443,438,431,457,439,440,444,463,464,441,468,448,445,442,449,460,462,446,458,450,447,451,400,461,452,
-    459,465,401,483,484,477,478,479,481,482,480,453,466,485,487,492,486,489,488,494,490,495,496,491,497,501,502,505,506,
-    493,498,469,503,499,454,510,467,504,508,514,511,500,512,507,509,513,521,470,515,523,522,516,519,471,517,472,473,529,
-    524,531,518,475,525,520,530,526,527,474,532,528,535,455,536,533,534,537,86,542,476,541,543,538,539,540,553,547,549,
-    550,559,548,551,554,544,561,560,545,546,562,558,552,555,556,557]
-SCRATCH, PLACE = {}, {}
+WIDTH = {Q: 4, U8: 1, BF: 2, F32: 4, I32: 4, U16: 2, HALF: 2}
+FAR = 768.0
+UNIT = 1024.0
+NONE = 700.0
+NP = len(PIECES)
+SLOTS = [c1 - c0 + 1 + (c1 == SEG) for c0, c1 in PIECES]
+BASE = [K * sum(SLOTS[:k]) for k in range(NP + 1)]
+ROWS = [(max(c0, 1), c1 - 1) for c0, c1 in PIECES]
+USED = [-(-((hi - lo + 2) // 2 * (lo + hi)) // 16) for lo, hi in ROWS]
+PAT = [sum(n + n % 2 for n in USED[:k]) for k in range(NP + 1)]
+SCRATCH, PLACE, MEMO = {}, {}, {}
 
 
 def _declare():
@@ -39,34 +33,37 @@ def _declare():
             PLACE[name] = (buf, at, n)
             at += (n + 31) // 32 * 32
         SCRATCH[buf] = ("sbuf", [128, at], d)
-    for name, n in (("w", 512), ("u", K), ("v", K), ("e", 512), ("x0", C), ("x0e", C), ("h", K), ("o", C), ("z", C)):
+    for name, n in (("w", 512), ("u", K), ("v", K), ("e", 512), ("n", K), ("x0", C), ("x0e", C), ("h", K), ("o", C),
+                    ("z", C), ("i", K * NP)):
         own("q" + name, n, Q)
         own("s" + name, n, U8)
     for name, n in (("y", C), ("b", K), ("l", K)):
         shared("q" + name, Q, [("q%s%d" % (name, t), n) for t in range(R)])
         shared("s" + name, U8, [("s%s%d" % (name, t), n) for t in range(R)])
-    shared("snd", I32, [("snd%d" % t, 16) for t in range(R)])
-    shared("lnd", I32, [("lnd%d" % t, 16) for t in range(R)])
-    for name, n in (("xt", 4 * C), ("ht", 512), ("ut", 512), ("vt", 512), ("em", 528), ("xf", 16 * 512),
-                    ("zt", 4 * C), ("yt", 4 * C), ("bt", 512), ("eg", 4 * C),
-                    ("r16", C), ("hp", C), ("keep", C), ("dc", C), ("d01", C), ("inc", C), ("d24", 136),
-                    ("inct", 288), ("keept", 288), ("sg", C), ("x1", C), ("hh", C), ("bc", C), ("re_", C), ("rt", C),
-                    ("m1", 3 * C), ("m2", 3 * C), ("dd", 8 * C), ("ag", 8 * 408), ("a1", 288), ("nq", 288),
-                    ("nq2", 288), ("gt", 304), ("ct", 304), ("alv", 512), ("pre", 512), ("rg", C), ("jk", 8 * K)):
+    shared("snd", U16, [("snd%d" % t, 16) for t in range(R)])
+    shared("lnd", U16, [("lnd%d" % t, 48) for t in range(R + 1)])
+    for name, n in (("xt", 4 * C), ("ht", 512), ("ut", 512), ("vt", 512), ("em", 528), ("cm", 512), ("xf", 16 * 512),
+                    ("zt", 4 * C), ("yt", 4 * C), ("bt", 512), ("eg", 4 * C), ("sg", 512 * NP), ("nam", K),
+                    ("dd", BASE[-1]), ("ag", BASE[-1]), ("inc", BASE[-1] // 4), ("ft", K), ("d32", K), ("g1", C),
+                    ("alv", 640), ("pre", 800), ("g3", C), ("nq", 16 * PAT[-1]), ("keept", 16 * PAT[-1]),
+                    ("ct", 16 * (PAT[-1] + 2 * NP)), ("jk", 8 * K), ("hold", K), ("blk", K)):
         own(name, n, BF)
-    for name, n in (("io5", 512), ("ca", 512), ("pt", 512), ("tab", 256), ("sc", 256), ("yo", 512), ("on", K),
-                    ("df", 24), ("wf", 48), ("nu", 32), ("dcf", K)):
+    for name, n in (("ids", 640), ("ca", 640), ("pt", 640), ("tab", 256), ("sc", K), ("yo", 512), ("on", K),
+                    ("df", SEG), ("wv", 4 * SEG), ("kp", SEG), ("t4", 160), ("d16", 16), ("w64", 64), ("t64", 64)):
         own(name, n, F32)
-    shared("fs", F32, (("col", 16), ("kk", 16), ("kn", 8), ("kb", 8), ("nrep", K), ("c1", 24), ("c2", 24), ("c3", 24),
-                       ("c4", 24), ("c5", 24), ("c6", 24), ("c7", 24), ("c8", 24), ("c9", 24), ("uu", 144),
-                       ("u17", 136), ("k17", 10), ("gq", 32), ("mn", 32), ("a2", 288), ("cq", 32), ("fa", K),
-                       ("acc", 8), ("fp", K), ("s1", K), ("s2", K)))
-    for name in ("am", "amg", "al"):
-        own(name, C, HALF)
+    shared("cs", F32, (("col", 24), ("r16", 16), ("r4", 64), ("dg4", 64), ("k1", 64), ("k2", 64), ("k3", 64),
+                       ("k4", 64), ("c1", 24), ("c2", 24), ("c3", 24), ("c4", 24), ("c5", 24), ("c6", 24), ("c7", 24),
+                       ("c8", 24), ("c9", 32), ("c10", 8), ("cc", 24), ("cn", 24), ("dgf", K), ("pw", 16), ("pv", 16)))
+    shared("fs", F32, (("t1", SEG), ("a2", 16 * PAT[-1]), ("dk", 32 * NP), ("acc", 8), ("fp", K), ("s1", K), ("s2", K),
+                       ("ownb", 8)))
+    for name, n in (("dga", C), ("dgb", C), ("m1", C), ("g2", C), ("m2", C), ("m3", 512 * NP), ("hs", K), ("fa", K)):
+        own(name, n, HALF)
     own("nmi", 8, I32)
-    shared("ns", I32, (("pi", 8), ("ci", 24), ("ni", 56), ("lo", 56), ("oo", 56), ("pk", 8), ("bi", 8)))
-    for name, n in (("lje", 24), ("let", 24), ("lti", 18), ("ltj", 18), ("lend", 2), ("lkn", 8), ("lnm", 8),
-                    ("off", 56), ("offp", 24), ("offd", 24), ("lfin", 8), ("l17", 10), ("lrk", 8), ("lb", 8)):
+    shared("ns", I32, (("pi", 8), ("ci", 24), ("bi", 32)))
+    shared("nd", I32, (("pk", 8), ("pn", 8)))
+    for name, n in (("lje", 24), ("let", 24), ("lti", PAT[-1]), ("ltj", PAT[-1]), ("lend", 2 * NP), ("lam", 24),
+                    ("l64", 4), ("l32", 2), ("of1", 24), ("of2", 24), ("offp", 24), ("offd", 24), ("lfin", 8),
+                    ("lb", 8)):
         own(name, n, U16)
     for b in range(8):
         SCRATCH["ps%d" % b] = ("psum", [128, 512], F32)
@@ -103,14 +100,68 @@ def _depend(ops):
         o["dep"] = sorted(need - {-1, i})
 
 
+def _place(ops, before, order):
+    start, end = [0.0] * len(ops), [0.0] * len(ops)
+    busy = {e: [] for e in "vstgyx"}
+    for i in order:
+        o = ops[i]
+        at = max([end[d] + (WAKE / 2 if "x" in (o["e"], ops[d]["e"]) else WAKE) for d in before[i]], default=0.0)
+        line = busy[o["e"]]
+        k = len(line)
+        while k and line[k - 1][1] > at:
+            k -= 1
+        while k < len(line) and line[k][0] < at + o["cost"]:
+            at = max(at, line[k][1])
+            k += 1
+        line.insert(k, (at, at + o["cost"]))
+        start[i], end[i] = at, at + o["cost"] + o["lat"]
+    return start, end
+
+
+def _order(ops):
+    n = len(ops)
+    before = [o["dep"] for o in ops]
+    after = [[] for _ in range(n)]
+    for i, o in enumerate(ops):
+        for d in o["dep"]:
+            after[d].append(i)
+    rank = [0.0] * n
+    for i in range(n - 1, -1, -1):
+        rank[i] = ops[i]["cost"] + ops[i]["lat"] + max([rank[s] + WAKE for s in after[i]], default=0.0)
+    best = None
+    rng = np.random.default_rng(SEED)
+    cur = None
+    for it in range(TRIES):
+        for i in range(n - 1, -1, -1):
+            for d in before[i]:
+                if rank[d] <= rank[i]:
+                    rank[d] = rank[i] + 1e-6
+        end = _place(ops, before, sorted(range(n), key=lambda i: (-rank[i], i)))[1]
+        rank = _place(ops, after, sorted(range(n), key=lambda i: (-end[i], -i)))[1]
+        start, end = _place(ops, before, sorted(range(n), key=lambda i: (-rank[i], i)))
+        score = max(end) + 0.02 * sum(end) / n
+        if cur is None or score < cur[0] + TEMP * (1 - it / TRIES) * rng.exponential():
+            cur = (score, start)
+        if best is None or score < best[0]:
+            best = (score, start)
+        t0 = rng.uniform(0, cur[0])
+        rank = [-x + (NOISE * rng.standard_normal() if abs(x - t0) < WIN else 0.0) for x in cur[1]]
+    MEMO["span"] = best[0]
+    return sorted(range(n), key=lambda i: (best[1][i], i))
+
+
 def _emit(g, T, ops, tail):
     queue = {"v": g.vector, "s": g.scalar, "t": g.tensor, "g": g, "y": g.sync}
-    _depend(ops)
-    pos = {i: k for k, i in enumerate(ORDER)}
-    assert sorted(ORDER) == list(range(len(ops)))
-    assert all(pos[d] < pos[i] for i, o in enumerate(ops) for d in o["dep"])
+    if not MEMO:
+        _depend(ops)
+        MEMO["dep"] = [o["dep"] for o in ops]
+        MEMO["order"] = _order(ops)
+    order = MEMO["order"]
+    for o, d in zip(ops, MEMO["dep"]):
+        o["dep"] = d
+    pos = {i: k for k, i in enumerate(order)}
     known = {e: set() for e in queue}
-    for i in ORDER:
+    for i in order:
         o = ops[i]
         if o["e"] == "x":
             o["known"] = set()
@@ -124,7 +175,7 @@ def _emit(g, T, ops, tail):
                 kn.add(d)
                 kn.update(ops[d]["known"])
         o["known"] = set(kn)
-    own = [i for i in ORDER if ops[i]["e"] != "x"]
+    own = [i for i in order if ops[i]["e"] != "x"]
     slots = {e: [[None, 0] for _ in range(POOL[e])] for e in POOL}
     for i in own:
         o = ops[i]
@@ -177,13 +228,15 @@ def rank_program(g, core, T, topo):
             lo = at + a - 1
             ap, idx = T[buf][:, slice(at + b - 1, lo if lo >= 0 else None, -1)], np.arange(at + a, at + b)
         ps = buf.startswith("ps")
-        return {"ap": ap, "use": [(buf, np.arange(512) if ps else idx)], "n": len(idx), "ps": ps}
+        return {"ap": ap, "use": [(buf, np.arange(512) if ps else idx)], "n": len(idx), "ps": ps,
+                "w": WIDTH[SCRATCH[buf][2]], "ind": False}
 
     def ind(win, off, cast=None):
         ap = win["ap"] if cast is None else win["ap"].bitcast(cast)
-        return {"ap": ap.indirect(off["ap"]), "use": win["use"] + off["use"], "ps": False}
+        return {"ap": ap.indirect(off["ap"]), "use": win["use"] + off["use"], "ps": False, "n": 16 * off["n"],
+                "w": win["w"], "ind": True}
 
-    def op(e, f, outs, ins, dma=False):
+    def op(e, f, outs, ins, cost, dma=False, lat=0.0):
         rd, wr = [], []
         for x in ins:
             if isinstance(x, dict):
@@ -191,71 +244,107 @@ def rank_program(g, core, T, topo):
         for x in outs:
             wr.append(x["use"][0])
             rd.extend(x["use"][1:])
-        ops.append({"e": e, "f": f, "R": rd, "W": wr, "dma": dma, "after": []})
+        ops.append({"e": e, "f": f, "R": rd, "W": wr, "dma": dma, "after": [], "cost": cost, "lat": lat})
         return len(ops) - 1
 
     def ap(x):
         return x["ap"] if isinstance(x, dict) else x
 
+    def span(out, ins, rate=1.0, fast=True):
+        if out["ind"]:
+            return 0.05 + 3.8 * CYCLE * out["n"]
+        if ins[0]["ind"]:
+            return 0.06 + 1.56 * CYCLE * out["n"]
+        narrow = fast and all(x["w"] <= 2 for x in [out] + ins)
+        return CYCLE * max(64, out["n"] * rate * (0.5 if narrow else 1.0))
+
     def ts(out, a, s1, s2, o0, o1=None):
         tail = (o0,) if s2 is None else (o0, o1)
-        op("v", lambda: VE.tensor_scalar(ap(out), ap(a), ap(s1), ap(s2), *tail), [out], [a, s1, s2])
+        op("v", lambda: VE.tensor_scalar(ap(out), ap(a), ap(s1), ap(s2), *tail), [out], [a, s1, s2], span(out, [a]))
 
     def tt(out, a, b, o):
-        op("v", lambda: VE.tensor_tensor(ap(out), ap(a), ap(b), o), [out], [a, b])
+        op("v", lambda: VE.tensor_tensor(ap(out), ap(a), ap(b), o), [out], [a, b],
+           span(out, [a, b], 1.0 if a["ps"] else 2.0))
 
     def cp(out, a):
-        op("v", lambda: VE.tensor_copy(ap(out), ap(a)), [out], [a])
+        op("v", lambda: VE.tensor_copy(ap(out), ap(a)), [out], [a], span(out, [a]))
 
     def scan(out, d0, d1, init, o0, o1):
-        op("v", lambda: VE.tensor_tensor_scan(ap(out), ap(d0), ap(d1), init, o0, o1), [out], [d0, d1])
+        op("v", lambda: VE.tensor_tensor_scan(ap(out), ap(d0), ap(d1), init, o0, o1), [out], [d0, d1],
+           span(out, [d0, d1]))
 
     def tr(out, a):
-        op("v", lambda: VE.transpose(ap(out), ap(a)), [out], [a])
+        op("v", lambda: VE.transpose(ap(out), ap(a)), [out], [a], span(out, [a]))
 
     def ms(out, c):
-        op("v", lambda: VE.memset(ap(out), c), [out], [])
+        op("v", lambda: VE.memset(ap(out), c), [out], [], span(out, [out]))
 
     def act(out, a, f, **kw):
         outs = [out] + ([kw["accum_out"]] if "accum_out" in kw else [])
         ins = [a] + [kw[k] for k in ("bias", "scale") if k in kw]
-        op("s", lambda: SE.activation(ap(out), ap(a), f, **{k: ap(x) for k, x in kw.items()}), outs, ins)
+        op("s", lambda: SE.activation(ap(out), ap(a), f, **{k: ap(x) for k, x in kw.items()}), outs, ins,
+           span(out, [a], 1.0, False) + (0.02 if len(outs) > 1 else 0.0))
+
+    def move(on_s, out, a, scale=None):
+        if on_s:
+            act(out, a, F.Copy, **({} if scale is None else {"scale": scale}))
+        elif scale is None:
+            cp(out, a)
+        else:
+            ts(out, a, scale, None, A.mult)
 
     def quant(name, tile, a=0, b=None):
         q, s = v("q" + name, a, b), v("s" + name, a, b)
-        op("v", lambda: VE.quantize_mx(ap(q), ap(s), ap(tile)), [q, s], [tile])
+        op("v", lambda: VE.quantize_mx(ap(q), ap(s), ap(tile)), [q, s], [tile], 0.012 + 0.00022 * tile["n"])
 
     def mm(bank, st, a, mv, c0=0, c1=None):
         q1, s1, q2, s2 = v("q" + st, a, a + 128), v("s" + st, a, a + 128), v("q" + mv, c0, c1), v("s" + mv, c0, c1)
         out = v("ps%d" % bank, 0, q2["n"])
-        op("t", lambda: PE.matmul_mx(ap(out), ap(q1), ap(s1), ap(q2), ap(s2), True, True), [out], [q1, s1, q2, s2])
+        op("t", lambda: PE.matmul_mx(ap(out), ap(q1), ap(s1), ap(q2), ap(s2), True, True), [out], [q1, s1, q2, s2],
+           0.000625 * (q2["n"] + 16))
 
     def iota(out, pat, base, cm, small=True):
         kw = {"allow_small_or_imprecise_dtypes": True} if small else {}
-        op("g", lambda: g.iota(ap(out), pat, base, cm, **kw), [out], [])
+        op("g", lambda: g.iota(ap(out), pat, base, cm, **kw), [out], [], 0.13 + 2 * CYCLE * out["n"])
+
+    def choose(out, pat, o, fill, base, cm):
+        op("g", lambda: g.affine_select(ap(out), ap(out), pat, o, fill, base, cm), [out], [out],
+           0.17 + 2 * CYCLE * out["n"])
 
     def load(out, src, cast=None, e="y"):
         dst = out["ap"] if cast is None else out["ap"].bitcast(cast)
         q = g.sync if e == "y" else g.scalar
-        op(e, lambda: q.dma_start(dst, src), [out], [], True)
+        op(e, lambda: q.dma_start(dst, src), [out], [], 0.06, True, LOAD + 0.0007 * out["n"] * out["w"])
 
     def store(dst, a, src=None, e="y"):
         q = g.sync if e == "y" else g.scalar
-        op(e, lambda: q.dma_start(dst, ap(a) if src is None else src), [], [a], True)
+        op(e, lambda: q.dma_start(dst, ap(a) if src is None else src), [], [a], 0.06, True,
+           LOAD + 0.0007 * a["n"] * a["w"])
 
     def send(out, a, sem, cast=None):
         o, i = (out["ap"], a["ap"]) if cast is None else (out["ap"].bitcast(cast), a["ap"].bitcast(cast))
+        cost = 0.35 if sent[0] else 0.35 + FIRST
         sent[0] += n_out
-        return op("g", lambda: g.remote_dma(o, i, T.sem[sem], T.sem.sent, pid, rid, mask), [], [a])
+        return op("g", lambda: g.remote_dma(o, i, T.sem[sem], T.sem.sent, pid, rid, mask), [], [a], cost, False,
+                  HOP + 0.0014 * a["n"] * a["w"])
 
     def arrive(sem, val, outs, after):
         ops.append({"e": "x", "sem": sem, "val": val, "R": [], "W": [x["use"][0] for x in outs], "dma": False,
-                    "after": after})
+                    "after": after, "cost": 0.0, "lat": 0.0})
 
-    def pick(dst, src, lst):
-        out, a = v("q" + dst), ind(v("q" + src), v(lst), dt.uint32)
-        op("v", lambda: VE.tensor_copy(ap(out).bitcast(dt.uint32), ap(a)), [out], [a])
-        act(v("s" + dst), ind(v("s" + src), v(lst)), F.Copy)
+    def pick(dst, src, lst, c0=0, c1=SEG):
+        out, a = v("q" + dst, 16 * c0, 16 * c1), ind(v("q" + src), v(lst, c0, c1), dt.uint32)
+        op("v", lambda: VE.tensor_copy(ap(out).bitcast(dt.uint32), ap(a)), [out], [a], span(out, [a]))
+        act(v("s" + dst, 16 * c0, 16 * c1), ind(v("s" + src), v(lst, c0, c1)), F.Copy)
+
+    def diagonal(out, src, marks, low=-4096.0):
+        scan(out, src, marks, low, A.max, A.subtract)
+
+    def marks(out, at, lane, big, end, step, k1, k2):
+        ts(k1, at, lane, 2 * big, A.is_lt, A.mult)
+        ts(k2, at, lane, big, A.is_le, A.mult)
+        tt(v(out), k1, k2, A.subtract)
+        ts(v(out, step - 1, None, step), v(out, step - 1, None, step), big + end, None, A.add)
 
     def xpl(t, b, c0=0, c1=C):
         return v("xf", (4 * t + b) * 512 + c0, (4 * t + b) * 512 + c1)
@@ -266,9 +355,10 @@ def rank_program(g, core, T, topo):
     def ps(b, n):
         return v("ps%d" % b, 0, n)
 
-    cl, ch, csc, cbi, c24, cu, c16h, c2l, cca = (v("col", i, i + 1) for i in range(9))
+    (cl, ch, codd, chalf, cquad, cgrp, cfirst, c24, cof2, cofp, cca, cfb, cfin, ctmp, cw, c32) = (
+        v("col", i, i + 1) for i in range(16))
 
-    for c0, c1 in CUT:
+    for c0, c1 in ((0, C // 2), (C // 2, C)):
         load(v("xt", 4 * c0, 4 * c1), T.x[:, 4 * c0:4 * c1])
     load(v("ut"), T.u[:], None, "s")
     load(v("nmi"), T.nm[:])
@@ -278,235 +368,248 @@ def rank_program(g, core, T, topo):
     load(v("vt"), T.v[:])
 
     iota(v("pi", 0, 1), [[1, 1]], 0, 1, False)
-    iota(v("r16"), [[0, 24], [1, 16]], 0, 0)
-    iota(v("c1"), [[16, 24]], 0, 0)
-    iota(v("kk", 1, 9), [[16, 4], [64, 2]], 0, 0)
-    iota(v("io5"), [[1, 512]], 0, 0)
-    em = v("em")
-    iota(em, [[0, 528]], 0, 0)
-    op("g", lambda: g.affine_select(ap(em), ap(em), [[-1, 528]], A.not_equal, 0.5, 3, 4), [em], [em])
-    iota(v("pt", 0, C), [[-256, 16], [-4096, 24]], 256 * 383, 0)
-    iota(v("pt", C, 512), [[256, K]], 256 * C, 0)
     ts(v("pi", 1, 2), v("pi", 0, 1), 15, None, A.bitwise_and)
-    ts(v("pi", 2, 3), v("pi", 0, 1), 4, 1, A.arith_shift_right, A.bitwise_and)
-    cp(v("col", 0, 2), v("pi", 1, 3))
-    for name, base, mark, step in (("inc", 1.0, BIG, 24), ("d24", 24.0, BIG, 17),
-                                   ("inct", 1.0, BIG, 24), ("keept", 1.0, 0.0, 24)):
-        ms(v(name), base)
-        ms(v(name, 0, None, step), mark)
-    ms(v("inct", 1, None, 25), BIG)
-    ms(v("keept", 1, None, 25), 0.0)
-    ts(csc, cl, 7.0, -1.0, A.is_lt, A.mult)
-    ts(cbi, cl, 7.0, -(2.0 ** -100), A.is_ge, A.add)
-    act(c24, cl, F.Copy, scale=24.0)
-    act(cu, cl, F.Identity, scale=-24.0, bias=float(C))
-    act(c16h, ch, F.Identity, scale=16.0, bias=-1.0)
-    act(c2l, cl, F.Identity, scale=2.0, bias=1.0)
-    act(cca, cl, F.Identity, scale=24.0, bias=-float(C))
-    ms(v("kk", 0, 1), 112.0)
-    iota(v("k17", 0, 8), [[17, 8]], 0, 0)
-    ms(v("k17", 8, 9), 0.0)
-    ts(v("l17", 0, 9), v("k17", 0, 9), cl, None, A.add)
-    ms(v("gt", 0, 16), BIG)
-    ms(v("ct", 0, 16), 0.0)
-    ms(v("nu", 24, 32), 0.0)
-    ms(v("sc"), 0.0)
-    act(v("col", 9, 10), cl, F.Copy, scale=-512.0)
-    act(v("keep"), v("r16"), F.Sign)
-    act(v("hh"), v("r16"), F.Sign, bias=6.5, scale=-1.0)
-    act(v("hp"), v("hh"), F.Identity, bias=1.0)
-    act(v("dc"), v("r16"), F.Abs, bias=v("col", 9, 10), scale=512.0)
-    act(v("d01"), v("dc"), F.Relu, bias=1.0, scale=-1.0)
-    act(v("dcf"), v("dc", 0, K), F.Copy, scale=1024.0)
-    act(v("ca"), v("io5"), F.Identity, bias=cca)
+    ts(v("pi", 2, 3), v("pi", 0, 1), 16, None, A.bitwise_and)
+    ts(v("pi", 3, 4), v("pi", 0, 1), 1, None, A.bitwise_and)
+    ts(v("pi", 4, 5), v("pi", 0, 1), 1, 7, A.arith_shift_right, A.bitwise_and)
+    ts(v("pi", 5, 6), v("pi", 0, 1), 2, 3, A.arith_shift_right, A.bitwise_and)
+    ts(v("pi", 6, 7), v("pi", 0, 1), 4, None, A.arith_shift_right)
+    cp(v("col", 0, 6), v("pi", 1, 7))
+    ts(cfirst, cl, 0.0, None, A.is_equal)
+    act(c24, cl, F.Copy, scale=float(SEG))
+    act(cof2, cfirst, F.Identity, scale=float(K), bias=191.0)
+    act(cca, cl, F.Identity, scale=32.0, bias=-512.0)
+    act(cfb, cfirst, F.Identity, scale=-2016.0, bias=2048.0)
+    act(cfin, cfirst, F.Copy, scale=2 * FAR)
+    act(ctmp, cfirst, F.Identity, scale=152.0, bias=FAR + 512)
+    act(cofp, cl, F.Identity, scale=-32.0, bias=ctmp)
+    iota(v("r16"), [[1, 16]], 0, 0)
+    iota(v("r4"), [[0, 16], [1, 4]], 0, 0)
+    iota(v("c1"), [[16, SEG]], 0, 0)
+    marks("d16", v("r16"), cl, FAR, FAR, 16, v("k1", 0, 16), v("k2", 0, 16))
+    marks("dg4", v("r4"), cquad, 256 * UNIT / 2, 255 * UNIT / 2, 4, v("k3"), v("k4"))
+    ts(v("lam"), v("c1"), 0.0, cl, A.mult, A.add)
+    act(v("dga"), ind(v("d16"), v("lam")), F.Copy)
+    act(v("cn"), v("c1"), F.Copy, scale=1.0 / 16)
+    act(v("dgb"), v("dga"), F.Copy)
+    tt(v("dgb", 15, None, 16), v("dgb", 15, None, 16), v("cn"), A.add)
+    act(v("dgf"), v("dga", 0, K), F.Copy, scale=256.0)
+    for k, (c0, c1) in enumerate(PIECES):
+        act(v("cc", c0, c1), v("cn", 0, c1 - c0), F.Copy, scale=UNIT / SLOTS[k])
+    iota(v("blk"), [[1, 8], [0, 16]], 0, 0)
+    ts(v("pw"), v("r16"), cl, 1.0, A.is_lt, A.add)
+    scan(v("pv"), v("pw"), v("pw"), UNIT / 2, A.mult, A.max)
+    ts(cw, cl, 7.0, v("pv", 15, 16), A.is_lt, A.mult)
+    ms(v("cm"), 0.0)
+    for s in range(4):
+        ts(v("cm", 5 * s, None, 16), v("blk", s, None, 4), cgrp, cw, A.is_equal, A.mult)
+    quant("n", v("cm"))
+    for k, (c0, c1) in enumerate(PIECES):
+        ms(v("sg", 512 * k + 16 * (c1 - c0), 512 * (k + 1)), 0.0)
+    iota(v("nam"), [[int(UNIT), K]], -191 * int(UNIT), 0)
+    for k in range(NP):
+        a, b, s = BASE[k] // 4, BASE[k + 1] // 4, SLOTS[k]
+        ms(v("inc", a, b), 1.0)
+        ms(v("inc", a, b, s), 4096.0)
+    ms(v("inc", BASE[-2] // 4 + SLOTS[-1] - 1, None, SLOTS[-1]), 8.0)
+    ms(v("dd", 0, BASE[1], SLOTS[0]), NONE)
+    ms(v("d32"), 32.0)
+    ms(v("d32", 0, None, 16), 4096.0)
+    ms(v("hold"), 0.0)
+    ms(v("hold", 0, None, 16), 2 * FAR)
+    ms(v("hold", 15, None, 16), -FAR)
+    ms(v("t4", 0, 1), 0.0)
+    ms(v("keept"), 1.0)
+    for k, (c0, c1) in enumerate(PIECES):
+        (lo, hi), a, b = ROWS[k], 16 * PAT[k], 16 * PAT[k + 1]
+        ms(v("keept", a, b, lo + hi), 0.0)
+        ms(v("keept", a + lo, b, lo + hi + 1), 0.0)
+        ms(v("ct", a + 32 * k, a + 32 * k + 16), 0.0)
+        ms(v("m3", 512 * k + 16 * (c1 - c0) + 15, 512 * (k + 1), 16), 0.0)
+    iota(v("ids"), [[1, 640]], 0, 0)
+    act(v("ca"), v("ids"), F.Identity, bias=cca)
+    choose(v("ca", 0, 512), [[0, 16], [1, 32]], A.is_ge, 4096.0, -8, 0)
+    act(v("pre", 640, 800), v("ids", 0, 160), F.Identity, scale=-1.0, bias=152.0)
+    iota(v("pt", 0, 512), [[-256, 16], [-4096, 32]], 256 * 511, 0)
+    iota(v("pt", 512, 640), [[256, K]], 256 * C, 0)
+    em = v("em")
+    ms(em, 0.0)
+    choose(em, [[-1, 528]], A.not_equal, 0.5, 3, 4)
     act(v("c2"), v("c1"), F.Identity, bias=cl)
     ts(v("lje"), v("c1"), 1.0 / 16, c24, A.mult, A.add)
-    tt(v("kn"), v("kk", 0, 8), v("kk", 1, 9), A.subtract)
-    ts(v("kn"), v("kn"), ch, None, A.mult)
-    tt(v("kn"), v("kn"), v("kk", 1, 9), A.add)
-    ts(v("kn"), v("kn"), 2.0, c2l, A.mult, A.add)
-    act(v("kb"), v("kn"), F.Copy, scale=-BIG)
-    cp(v("lkn"), v("kn"))
-    act(v("nrep"), ind(v("io5"), v("lkn")), F.Copy)
-    ts(v("c3"), v("c2"), -11.5, 1.0 / 24, A.add, A.mult)
-    cp(v("ci"), v("c3"))
-    ts(v("c3"), v("ci"), -24.0, None, A.mult)
-    tt(v("c3"), v("c3"), v("c2"), A.add)
-    ts(v("c4"), v("ci"), 1.0, None, A.add)
-    tt(v("c5"), v("c3"), v("c4"), A.is_ge)
-    tt(v("c6"), v("c5"), v("c4"), A.mult)
-    tt(v("c7"), v("c3"), v("c6"), A.subtract)
-    cp(v("lti"), v("c7", 0, 18))
-    ts(v("c8"), v("c4"), -2.0, 24.0, A.mult, A.add)
-    tt(v("c8"), v("c8"), v("c5"), A.mult)
-    tt(v("c8"), v("c8"), v("c4"), A.add)
-    cp(v("ltj"), v("c8", 0, 18))
-    ts(v("c9", 0, 2), v("c2", 0, 2), 25.0, -9.0, A.mult, A.add)
-    ts(v("c9", 2, 4), v("c2", 0, 2), -24.0, 591.0, A.mult, A.add)
-    tt(v("c9", 4, 6), v("c9", 0, 2), v("c9", 2, 4), A.min)
-    cp(v("lend"), v("c9", 4, 6))
-    ts(v("c5"), v("c3"), 16.0, None, A.mult)
-    tt(v("c5"), v("c5"), v("ci"), A.add)
+    ts(v("ci"), v("c2"), -11.5, 1.0 / SEG, A.add, A.mult)
+    act(v("c3"), v("c2"), F.Copy, scale=16.0)
+    ts(v("c5"), v("ci"), 1.0 - 16 * SEG, None, A.mult)
+    tt(v("c5"), v("c5"), v("c3"), A.add)
     cp(v("let"), v("c5"))
+    for k, (c0, c1) in enumerate(PIECES):
+        (lo, hi), a, b = ROWS[k], PAT[k], PAT[k + 1]
+        s, e = float(lo + hi), v("c2", 0, b - a)
+        ts(v("bi", a, b), e, (1 - s) / 2, 1 / s, A.add, A.mult)
+        ts(v("c4", a, b), v("bi", a, b), float(lo), None, A.add)
+        act(v("c6", a, b), v("c4", a, b), F.Identity, scale=-s, bias=s * lo)
+        tt(v("c6", a, b), v("c6", a, b), e, A.add)
+        act(v("c8", a, b), v("c4", a, b), F.Identity, scale=-2.0, bias=s)
+        act(v("c9", 2 * k, 2 * k + 2), v("c2", 0, 2), F.Identity, scale=s + 1, bias=15 + (s + 1) * c0 - s * lo)
+        act(v("c9", 16 + 2 * k, 18 + 2 * k), v("c2", 0, 2), F.Identity, scale=-s, bias=15 + s * (hi - c0 + 1))
+    tt(v("c9", 0, 2 * NP), v("c9", 0, 2 * NP), v("c9", 16, 16 + 2 * NP), A.min)
+    cp(v("lend"), v("c9", 0, 2 * NP))
+    n = PAT[-1]
+    tt(v("c7", 0, n), v("c6", 0, n), v("c4", 0, n), A.is_ge)
+    tt(v("c8", 0, n), v("c8", 0, n), v("c7", 0, n), A.mult)
+    tt(v("c7", 0, n), v("c7", 0, n), v("c4", 0, n), A.mult)
+    tt(v("c8", 0, n), v("c8", 0, n), v("c4", 0, n), A.add)
+    tt(v("c7", 0, n), v("c6", 0, n), v("c7", 0, n), A.subtract)
+    cp(v("ltj"), v("c8", 0, n))
+    cp(v("lti"), v("c7", 0, n))
+    ts(v("c10", 0, 2), v("lam", 0, 2), 8.0, -4.0, A.max, A.mult)
+    ts(v("l64", 0, 2), v("c10", 0, 2), 127.0, None, A.add)
+    ts(v("l64", 2, 4), v("lam", 0, 2), -4.0, 63.0, A.mult, A.add)
+    ts(c32, codd, 32.0, ch, A.mult, A.add)
+    tt(c32, c32, chalf, A.subtract)
+    act(v("c10", 2, 4), v("c1", 0, 2), F.Identity, scale=-0.5, bias=15.0)
+    ts(v("l32"), v("c10", 2, 4), c32, None, A.add)
     quant("u", v("ut"))
-    for c0, c1 in CUT:
+    for c0, c1 in ((0, C // 2), (C // 2, C)):
         quant("x0", v("xt", 4 * c0, 4 * c1), c0, c1)
     quant("h", v("ht"))
     quant("v", v("vt"))
     for b in range(4):
         quant("e", v("em", 3 - b, 515 - b), 128 * b, 128 * b + 128)
-    ts(v("lnm"), v("nmi"), 2.0, 1.0, A.mult, A.add)
-    ts(v("ni", 48, 56), v("nmi"), 2.0, 1.0, A.mult, A.add)
-    cp(ind(v("sc"), v("lnm")), v("io5", 0, K))
-    tt(v("s1"), ind(v("sc"), v("lkn")), v("d01", 0, K), A.mult)
-    scan(v("s2"), v("keep", 0, K), v("s1"), 0.0, A.mult, A.add)
-    pick("x0e", "x0", "lje")
-
-    def unpack_x(t, name):
-        for b in range(4):
-            mm(4 + b, "e", 128 * b, name)
-            if t > 0 or b < 2:
-                act(xpl(t, b), ps(4 + b, C), F.Copy)
+    for c0, c1 in PIECES:
+        pick("x0e", "x0", "lje", c0, c1)
+    cp(v("lnd0", 32, 40), v("nmi"))
+    cp(ind(v("tab", K, 2 * K), v("lnd0", 32, 40)), v("ids", 0, K))
 
     def border(t, on_v):
         for b in range(4):
-            win = ind(xpl(t + 1, b, 0, 512), v("lb"))
-            if b in on_v:
-                ts(v("bt", b, None, 4), win, 2.0, None, A.mult)
-            else:
-                act(v("bt", b, None, 4), win, F.Copy, scale=2.0)
+            move(b not in on_v, v("bt", b, None, 4), ind(xpl(t + 1, b, 0, 512), v("lb")), 2.0)
         quant("b%d" % t, v("bt"))
         s1 = send(v("ql%d" % t), v("qb%d" % t), "arb%d" % t, dt.uint8)
         s2 = send(v("sl%d" % t), v("sb%d" % t), "arb%d" % t)
         arrive("arb%d" % t, 2 * n_in, [v("ql%d" % t), v("sl%d" % t)], [s1, s2])
 
-    def diagonal(k, src):
-        scan(v("m1", k * C, (k + 1) * C), src, v("dc"), -1.0, A.max, A.subtract)
-        scan(v("m2", k * C, (k + 1) * C), v("keep"), v("m1", k * C, (k + 1) * C), 0.0, A.mult, A.max)
-
     for t in range(R):
         first = t == 0
-        qx = "x0" if first else "y%d" % (t - 1)
-        for k, (c0, c1) in enumerate(CUT):
-            mm(2 + k, "u", 0, qx, c0, c1)
-            act(v("sg", c0, c1), ps(2 + k, c1 - c0), F.Sign, bias=cbi, scale=csc)
-        for c0, c1 in CUT:
-            tr(v("x1", c0, c1), v("sg", c0, c1))
-            scan(v("hh", c0, c1, -1), v("hp", c0, c1, -1), v("x1", c0, c1, -1), 0.0, A.mult, A.add)
-            scan(v("bc", c0, c1), v("keep", c0, c1), v("hh", c0, c1), 0.0, A.mult, A.max)
-            tr(v("rt" if first else "re_", c0, c1), v("bc", c0, c1))
-        if first:
-            act(v("re_"), ind(v("rt"), v("lje")), F.Copy)
-            unpack_x(0, "x0e")
-        else:
-            act(v("rt", 0, 224), ind(v("re_"), v("let", 0, 14)), F.Copy)
-            cp(v("rt", 224, C), ind(v("re_"), v("let", 14, 24)))
-            unpack_x(t, qx)
+        qx = "x0e" if first else "y%d" % (t - 1)
+        lnd = "lnd%d" % t
+        if not first:
+            act(v("tab", K, 2 * K), ind(v("ids", 0, K), v(lnd, 40, 48)), F.Copy)
+        act(v("dd", BASE[-2] + SLOTS[-1] - 1, None, SLOTS[-1]), v("tab", K, 2 * K), F.Identity, bias=cfb)
+        for k, (c0, c1) in enumerate(PIECES):
+            n, sl, bank = c1 - c0, SLOTS[k], PB[k]
+            mm(bank, "u", 0, qx, 16 * c0, 16 * c1)
+            act(v("sg", 512 * k, 512 * k + 16 * n), ps(bank, 16 * n), F.Sign, bias=-(2.0 ** -100), scale=-1.0)
+            quant("i", v("sg", 512 * k, 512 * (k + 1)), K * k, K * (k + 1))
+            mm(bank, "n", 0, "i", K * k, K * (k + 1))
+            diagonal(v("wv", 4 * c0, 4 * c1), ps(bank, 4 * n), v("dg4", 0, 4 * n), -512 * UNIT)
+            own = v("wv", 4 * c0 + 3, 4 * c1, 4)
+            if k:
+                cp(v("dd", BASE[k], BASE[k + 1], sl), v("ag", BASE[k - 1] + SLOTS[k - 1] - 1, BASE[k], SLOTS[k - 1]))
+            for c in range(c0, c1):
+                out, name = v("dd", BASE[k] + 1 + c - c0, BASE[k + 1], sl), v("wv", 4 * c + 3, 4 * c + 4)
+                if c - c0 < ON_S["match"][k]:
+                    act(out, v("nam"), F.Abs, bias=name, scale=-1.0)
+                else:
+                    ts(out, v("nam"), name, 4096.0, A.not_equal, A.mult)
+            for r in range(4):
+                a, b = BASE[k] + 32 * sl * r, BASE[k] + 32 * sl * (r + 1)
+                scan(v("ag", a, b), v("inc", BASE[k] // 4, BASE[k + 1] // 4), v("dd", a, b), 0.0, A.add, A.min)
+            tt(v("t1", c0, c1), own, v("cc", c0, c1), A.add)
+            ts(v("of1", c0, c1), v("t1", c0, c1), sl / UNIT, 191.0 * sl, A.mult, A.add)
+            ts(v("of2", c0, c1), own, 1 / UNIT, cof2, A.mult, A.add)
+            act(v("g1", 16 * c0, 16 * c1), ind(v("ag", BASE[k], BASE[k + 1]), v("of1", c0, c1)), F.Copy)
+            diagonal(v("m1", 16 * c0, 16 * c1), v("g1", 16 * c0, 16 * c1), v("dgb", 16 * c0, 16 * c1))
+        for b in range(4):
+            mm(XB[b], "e", 128 * b, qx)
+            if not first or b not in ON_S["mix"]:
+                act(xpl(t, b), ps(XB[b], C), F.Copy)
+        if not first:
             border(t - 1, ())
-            ts(v("ni", 48, 56), v("lnd%d" % (t - 1), 8, 16), 255, None, A.bitwise_and)
-        diagonal(0, v("re_"))
-        diagonal(1, v("rt", 0, C, -1))
-        act(v("wf", 0, 24), v("m2", 15, C, 16), F.Copy)
-        cp(v("ni", 0, 48), v("m2", 15, 2 * C, 16))
-        ts(v("lo"), v("ni"), 1, 15, A.arith_shift_right, A.bitwise_and)
-        tt(v("oo"), v("ni"), v("lo"), A.subtract)
-        ts(v("off"), v("oo"), c16h, None, A.add)
-        for r in range(8):
-            dd = v("dd", C * r, C * (r + 1))
-            if r >= (2 if first else 5):
-                act(dd, v("rt"), F.Abs, bias=v("kb", r, r + 1), scale=BIG)
-            else:
-                ts(dd, v("rt"), v("kn", r, r + 1), 4096.0, A.not_equal, A.mult)
-            scan(v("ag", 24 + 408 * r, 408 * (r + 1)), v("inc"), dd, 0.0, A.add, A.min)
-        act(v("a1"), ind(v("wf", 0, 24), v("ltj")), F.Copy)
-        tt(v("nq"), ind(v("wf", 0, 24), v("lti")), v("a1"), A.not_equal)
-        scan(v("gt", 16, 304), v("inct"), v("nq"), 0.0, A.add, A.mult)
-        tt(v("gq"), ind(v("gt"), v("lend")), v("io5", 0, 32), A.subtract)
-        if first:
-            cp(v("ag", 23, None, 408), v("s2", 15, K, 16))
-        else:
-            ts(v("ag", 23, None, 408), v("lnd%d" % (t - 1), 0, 8), 0.0, None, A.add)
-        scan(v("u17"), v("d24"), v("ag", 23, None, 24), 0.0, A.add, A.min)
-        act(v("uu"), ind(v("u17"), v("l17", 0, 9)), F.Copy)
-        tr(v("tab", 0, K), v("uu", 0, K))
-        tr(v("tab", K, 2 * K), v("uu", 16, K + 16))
-        act(v("amg"), ind(v("tab"), v("off", 0, 24)), F.Copy)
-        scan(v("am"), v("amg"), v("dc"), -1.0, A.max, A.subtract)
-        scan(v("al"), v("keep"), v("am"), 0.0, A.mult, A.max)
-        tt(v("nu", 0, 24), v("al", 15, C, 16), v("gq", 0, 24), A.min)
-        ts(v("offp"), v("nu", 0, 24), cu, None, A.add)
-        act(v("mn"), v("nu"), F.Relu, bias=-1.0, scale=-1.0)
-        tt(v("alv"), ind(v("tab"), v("off", 24, 56)), v("ca"), A.is_equal)
-        scan(v("pre"), v("alv"), v("alv"), 0.0, A.add, A.max)
-        act(v("rg"), ind(v("pre"), v("offp")), F.Copy)
-        diagonal(2, v("rg"))
-        act(v("a2"), ind(v("nu", 0, 24), v("ltj")), F.Copy)
-        tt(v("nq2"), ind(v("nu", 0, 24), v("lti")), v("a2"), A.is_gt)
-        scan(v("ct", 16, 304), v("keept"), v("nq2"), 0.0, A.mult, A.add)
-        tt(v("cq"), ind(v("ct"), v("lend")), v("mn"), A.subtract)
-        tt(v("df"), v("m2", 2 * C + 15, 3 * C, 16), v("cq", 0, 24), A.add)
-        ts(v("offd"), v("df"), -1.0, None, A.add)
+        act(v("w64"), ind(v("wv"), v("l64")), F.Copy)
+        tr(v("t64"), v("w64"))
+        ts(v(lnd, 0, 32), ind(v("t64"), v("l32")), 1 / UNIT, 191.0, A.mult, A.add)
+        tr(v("ft"), v("ag", BASE[-2] + SLOTS[-1] - 1, None, SLOTS[-1]))
+        scan(v("t4", 1, K + 1), v("d32"), v("ft"), 0.0, A.add, A.min)
+        tr(v("tab", 0, K), v("t4", 0, K))
+        for c0, c1 in PIECES:
+            act(v("g2", 16 * c0, 16 * c1), ind(v("tab"), v("of2", c0, c1)), F.Copy)
+            diagonal(v("m2", 16 * c0, 16 * c1), v("g2", 16 * c0, 16 * c1), v("dga", 16 * c0, 16 * c1))
+            tt(v("kp", c0, c1), v("m1", 16 * c0 + 15, 16 * c1, 16), v("m2", 16 * c0 + 15, 16 * c1, 16), A.min)
+            ts(v("offp", c0, c1), v("kp", c0, c1), cofp, None, A.add)
+        for a, b in ((0, 20), (20, 40)):
+            tt(v("alv", 16 * a, 16 * b), ind(v("tab", 0, K), v(lnd, a, b)), v("ca", 16 * a, 16 * b), A.is_ge)
+        scan(v("pre", 0, 640, -1), v("alv", 0, 640, -1), v("alv", 0, 640, -1), 0.0, A.add, A.max)
+        for k, (c0, c1) in enumerate(PIECES):
+            a, n, w = PAT[k], USED[k], -(-(c1 - c0) // 16)
+            p0, p1, q0 = 16 * a, 16 * (a + n), 16 * a + 32 * k
+            act(v("a2", p0, p1), ind(v("kp", 0, c1), v("ltj", a, a + n)), F.Copy)
+            tt(v("nq", p0, p1), ind(v("kp", 0, c1), v("lti", a, a + n)), v("a2", p0, p1), A.is_gt)
+            scan(v("ct", q0 + 16, q0 + 16 + 16 * n), v("keept", p0, p1), v("nq", p0, p1), 0.0, A.mult, A.add)
+            move(k in ON_S["count"], v("g3", 16 * c0, 16 * c1), ind(v("pre"), v("offp", c0, c1)))
+            diagonal(v("m3", 512 * k, 512 * k + 16 * (c1 - c0)), v("g3", 16 * c0, 16 * c1), v("dga", 16 * c0, 16 * c1))
+            tt(v("dk", 32 * k, 32 * k + 16 * w), ind(v("ct", q0, q0 + 16 + 16 * n), v("lend", 2 * k, 2 * k + w)),
+               v("m3", 512 * k + 15, 512 * k + 256 * w, 16), A.subtract)
+            ts(v("offd", c0, c1), v("dk", 32 * k, 32 * k + c1 - c0), K - FAR, None, A.add)
+            if t == R - 1:
+                act(v("df", c0, c1), v("dk", 32 * k, 32 * k + c1 - c0), F.Identity, bias=K - FAR)
         if t == R - 1:
-            act(v("wf", 24, 48), v("df"), F.Identity, bias=-1.0)
-            store(T.ol[:, 0:C], v("wf", 24, 48))
-        cp(v("lfin"), v("u17", 16, None, 17))
-        act(v("fa"), ind(v("io5"), v("lfin")), F.Copy)
+            store(T.ol[:, 0:C], v("df"))
+        snd = "snd%d" % t
+        diagonal(v("hs", 0, K, -1), v("t4", 1, K + 1, -1), v("hold", 0, K, -1))
+        tr(v("fa"), v("hs"))
+        diagonal(v("s1"), v("fa"), v("dga", 0, K))
+        ts(v("ownb"), v("s1", 15, None, 16), FAR, None, A.add)
+        ts(v("lfin"), v("s1", 15, None, 16), cfin, None, A.add)
         for r in range(8):
-            act(v("jk", K * r, K * (r + 1)), v("fa"), F.Sign, bias=v("u17", 17 * r + 16, 17 * r + 17), scale=-1.0,
+            act(v("jk", K * r, K * (r + 1)), v("fa"), F.Sign, bias=v("ownb", r, r + 1), scale=-1.0,
                 accum_out=v("acc", r, r + 1))
-        ts(v("lrk"), v("acc"), 127.0, 0.5, A.add, A.mult)
-        ts(v("snd%d" % t, 0, 8), v("acc"), 127.0, 0.5, A.add, A.mult)
-        tt(v("fp"), ind(v("pt"), v("lfin")), v("nrep"), A.add)
-        cp(ind(v("sc", 0, K), v("lrk")), v("fp"))
-        scan(v("s1"), v("sc", 0, K), v("dcf"), -1.0, A.max, A.subtract)
-        scan(v("s2"), v("keep", 0, K), v("s1"), 0.0, A.mult, A.max)
-        cp(v("snd%d" % t, 8, 16), v("s2", 15, K, 16))
-        ts(v("bi"), v("snd%d" % t, 8, 16), 8, None, A.arith_shift_right)
-        cp(v("lb"), v("bi"))
-        s1 = send(v("lnd%d" % t), v("snd%d" % t), "arl%d" % t)
-        arrive("arl%d" % t, n_in, [v("lnd%d" % t)], [s1])
+        ts(v(snd, 8, 16), v("acc"), 127.0, 0.5, A.add, A.mult)
+        tt(v("fp"), ind(v("pt"), v("lfin")), v("ids", 0, K), A.add)
+        cp(ind(v("sc"), v(snd, 8, 16)), v("fp"))
+        diagonal(v("s2"), v("sc"), v("dgf"), -1024 * UNIT)
+        ts(v("lb"), v("s2", 15, None, 16), 1.0 / 256, FAR - 0.25, A.mult, A.add)
+        ts(v("pk"), v("s2", 15, None, 16), 256 * FAR, None, A.add)
+        ts(v("pn"), v("pk"), 255, None, A.bitwise_and)
+        cp(v(snd, 0, 8), v("pn"))
+        land = v("lnd%d" % (t + 1), 32, 48)
+        arrive("arl%d" % t, n_in, [land], [send(land, v(snd), "arl%d" % t)])
         fq = "h" if first else "l%d" % (t - 1)
         for b in range(4):
-            mm(b, "e", 128 * b, fq)
-            act(fpl(t, b), ps(b, K), F.Copy)
-        for c0, c1 in CUT:
-            lst = v("offd", c0 // 16, c1 // 16)
+            mm(FB[b % len(FB)], "e", 128 * b, fq)
+            act(fpl(t, b), ps(FB[b % len(FB)], K), F.Copy)
+        for c0, c1 in PIECES:
+            lst, e0, e1 = v("offd", c0, c1), 16 * c0, 16 * c1
             for b in range(4):
-                z = v("zt", 4 * c0 + b, 4 * c1, 4)
-                if b >= 2:
-                    act(v("eg", b * C + c0, b * C + c1), ind(fpl(t, b), lst), F.Copy)
-                    tt(z, v("ps%d" % (4 + b), c0, c1), v("eg", b * C + c0, b * C + c1), A.add)
+                z = v("zt", 4 * e0 + b, 4 * e1, 4)
+                if b in ON_S["mix"]:
+                    act(v("eg", b * C + e0, b * C + e1), ind(fpl(t, b), lst), F.Copy)
+                    tt(z, v("ps%d" % XB[b], e0, e1), v("eg", b * C + e0, b * C + e1), A.add)
                 else:
-                    tt(z, ind(fpl(t, b), lst), xpl(t, b, c0, c1), A.add)
-            quant("z", v("zt", 4 * c0, 4 * c1), c0, c1)
-        for k, (c0, c1) in enumerate(CUT):
+                    tt(z, ind(fpl(t, b), lst), xpl(t, b, e0, e1), A.add)
+            quant("z", v("zt", 4 * e0, 4 * e1), e0, e1)
+        for k, (c0, c1) in enumerate(PIECES):
+            e0, e1 = 16 * c0, 16 * c1
             for b in range(4):
-                bank = (4 * k + b) % 6
-                mm(bank, "w", 128 * b, "z", c0, c1)
-                if k == 1 and b % 2:
-                    ts(v("yt", 4 * c0 + b, 4 * c1, 4), ps(bank, c1 - c0), 0.03125, None, A.mult)
-                else:
-                    act(v("yt", 4 * c0 + b, 4 * c1, 4), ps(bank, c1 - c0), F.Copy, scale=0.03125)
-            quant("y%d" % t, v("yt", 4 * c0, 4 * c1), c0, c1)
+                bank = YB[k][b]
+                mm(bank, "w", 128 * b, "z", e0, e1)
+                move(b in ON_S["y"][k], v("yt", 4 * e0 + b, 4 * e1, 4), ps(bank, e1 - e0), 0.03125)
+            quant("y%d" % t, v("yt", 4 * e0, 4 * e1), e0, e1)
 
     t = R - 1
-    for k, (c0, c1) in enumerate(CUT):
+    for k, (c0, c1) in enumerate(PIECES):
+        e0, e1 = 16 * c0, 16 * c1
         for b in range(4):
-            bank = ((2, 3, 6, 7), (4, 5, 0, 1))[k][b]
-            mm(bank, "e", 128 * b, "y%d" % t, c0, c1)
-            if k == 1 and b % 2:
-                cp(xpl(R, b, c0, c1), ps(bank, c1 - c0))
-            else:
-                act(xpl(R, b, c0, c1), ps(bank, c1 - c0), F.Copy)
+            bank = (4 * k + b) % 8
+            mm(bank, "e", 128 * b, "y%d" % t, e0, e1)
+            move(k < NP - 1 or b % 2 == 0, xpl(R, b, e0, e1), ps(bank, e1 - e0))
     border(t, (1, 3))
     pick("o", "y%d" % t, "let")
     mm(0, "v", 0, "o")
     store(T.oc[:, 0:4 * C], v("qo"), T.qo[:].bitcast(dt.uint8))
     for k in range(4):
         store(T.osc[4 * k:4 * k + 4, 0:C], v("so"), T.so[32 * k:32 * k + 4, :])
-    ts(v("pk"), v("lnd%d" % t, 8, 16), 255, None, A.bitwise_and)
-    cp(v("lnm"), v("pk"))
-    ts(v("on"), ind(v("io5"), v("lnm")), -1.0, 0.5, A.add, A.mult)
+    act(v("on"), ind(v("ids", 0, K), v("lnd%d" % R, 32, 40)), F.Copy)
     store(T.ol[:, C:512], v("on"), T.on[0:128:16, :])
     act(v("yo", 0, C), ps(0, C), F.Copy)
     store(T.y[:, 0:C], v("yo", 0, C))

@@ -4,17 +4,18 @@ from concourse.mybir import dt, AluOpType as A, ActivationFunctionType as F
 C, K, R = 384, 128, 3
 SEG = 24
 PIECES = [(0, 12), (12, 24)]
-ON_S = {"match": (6, 4), "mix": (2, 3), "y": ((0, 1, 2, 3), (0, 2)), "count": (0, 1)}
-XB, YB, FB, PB = (1, 5, 6, 7), ((0, 2, 3, 4), (4, 5, 1, 0)), (2, 3), (0, 4)
-WAKE, HOP, FIRST, LOAD, CYCLE = 0.22, 1.8, 1.0, 1.8, 0.00092
-SEED, TRIES, TEMP, NOISE, WIN = 0, 2000, 0.03, 0.7, 1.5
+MIX = ((2, 3), (2, 3))
+MATCH = 5
+XB, YB, FB, PB = ((0, 1, 2, 3), (4, 5, 6, 7)), ((0, 1, 2, 3), (4, 5, 6, 7)), (0, 4), (0, 4)
+WAKE, HOP, FIRST, LOAD, CYCLE = 0.19, 2.2, 1.5, 1.8, 0.00095
+SEED, TRIES, TEMP, NOISE, WIN = 0, 40000, 0.015, 0.4, 1.0
 Q, U8, BF, F32, I32, U16, HALF = "float8_e4m3fn_x4", "uint8", "bfloat16", "float32", "int32", "uint16", "float16"
 WIDTH = {Q: 4, U8: 1, BF: 2, F32: 4, I32: 4, U16: 2, HALF: 2}
 FAR = 768.0
 UNIT = 1024.0
 NONE = 700.0
 NP = len(PIECES)
-SLOTS = [c1 - c0 + 1 + (c1 == SEG) for c0, c1 in PIECES]
+SLOTS = [max(c1 - c0 for c0, c1 in PIECES) + 2] * NP
 BASE = [K * sum(SLOTS[:k]) for k in range(NP + 1)]
 ROWS = [(max(c0, 1), c1 - 1) for c0, c1 in PIECES]
 USED = [-(-((hi - lo + 2) // 2 * (lo + hi)) // 16) for lo, hi in ROWS]
@@ -44,19 +45,21 @@ def _declare():
     shared("lnd", U16, [("lnd%d" % t, 48) for t in range(R + 1)])
     for name, n in (("xt", 4 * C), ("ht", 512), ("ut", 512), ("vt", 512), ("em", 528), ("cm", 512), ("xf", 16 * 512),
                     ("zt", 4 * C), ("yt", 4 * C), ("bt", 512), ("eg", 4 * C), ("sg", 512 * NP), ("nam", K),
-                    ("dd", BASE[-1]), ("ag", BASE[-1]), ("inc", BASE[-1] // 4), ("ft", K), ("d32", K), ("g1", C),
+                    ("dd", BASE[-1]), ("ag", BASE[-1]), ("inc", BASE[1] // 4), ("ft", K), ("d32", K), ("g1", C),
                     ("alv", 640), ("pre", 800), ("g3", C), ("nq", 16 * PAT[-1]), ("keept", 16 * PAT[-1]),
-                    ("ct", 16 * (PAT[-1] + 2 * NP)), ("jk", 8 * K), ("hold", K), ("blk", K)):
+                    ("ct", 16 * (PAT[-1] + 2 * NP)), ("jk", 8 * K), ("hold", K), ("blk", K), ("blj", K),
+                    ("wv", 4 * SEG), ("w64", 64), ("t64", 64)):
         own(name, n, BF)
-    for name, n in (("ids", 640), ("ca", 640), ("pt", 640), ("tab", 256), ("sc", K), ("yo", 512), ("on", K),
-                    ("df", SEG), ("wv", 4 * SEG), ("kp", SEG), ("t4", 160), ("d16", 16), ("w64", 64), ("t64", 64)):
+    for name, n in (("ids", 640), ("idm", 512), ("pt", 640), ("tab", 256), ("sc", K), ("yo", 512), ("on", K),
+                    ("df", SEG), ("kp", SEG), ("t4", 160), ("d16", 16)):
         own(name, n, F32)
     shared("cs", F32, (("col", 24), ("r16", 16), ("r4", 64), ("dg4", 64), ("k1", 64), ("k2", 64), ("k3", 64),
                        ("k4", 64), ("c1", 24), ("c2", 24), ("c3", 24), ("c4", 24), ("c5", 24), ("c6", 24), ("c7", 24),
                        ("c8", 24), ("c9", 32), ("c10", 8), ("cc", 24), ("cn", 24), ("dgf", K), ("pw", 16), ("pv", 16)))
     shared("fs", F32, (("t1", SEG), ("a2", 16 * PAT[-1]), ("dk", 32 * NP), ("acc", 8), ("fp", K), ("s1", K), ("s2", K),
                        ("ownb", 8)))
-    for name, n in (("dga", C), ("dgb", C), ("m1", C), ("g2", C), ("m2", C), ("m3", 512 * NP), ("hs", K), ("fa", K)):
+    for name, n in (("dga", C), ("dgb", C), ("m1", C), ("g2", C), ("m2", C), ("m3", 512 * NP), ("hs", K), ("fa", K),
+                    ("ca", 640), ("ga", 640)):
         own(name, n, HALF)
     own("nmi", 8, I32)
     shared("ns", I32, (("pi", 8), ("ci", 24), ("bi", 32)))
@@ -71,7 +74,7 @@ def _declare():
 
 
 _declare()
-POOL = {"v": 50, "s": 34, "t": 16, "y": 28, "g": 12}
+POOL = {"c": 121, "y": 22}
 SEMAPHORES = (["%s%d" % (e, i) for e in POOL for i in range(POOL[e])]
               + ["arl%d" % t for t in range(R)] + ["arb%d" % t for t in range(R)] + ["sent"])
 
@@ -100,21 +103,21 @@ def _depend(ops):
         o["dep"] = sorted(need - {-1, i})
 
 
-def _place(ops, before, order):
+def _place(ops, before, order, way):
     start, end = [0.0] * len(ops), [0.0] * len(ops)
-    busy = {e: [] for e in "vstgyx"}
+    busy = {e: [] for e in "vstgyxn"}
     for i in order:
-        o = ops[i]
-        at = max([end[d] + (WAKE / 2 if "x" in (o["e"], ops[d]["e"]) else WAKE) for d in before[i]], default=0.0)
-        line = busy[o["e"]]
+        e, _, cost = ops[i]["ways"][way[i]]
+        at = max([end[d] for d in before[i]], default=-WAKE) + WAKE
+        line = busy[e]
         k = len(line)
         while k and line[k - 1][1] > at:
             k -= 1
-        while k < len(line) and line[k][0] < at + o["cost"]:
+        while k < len(line) and line[k][0] < at + cost:
             at = max(at, line[k][1])
             k += 1
-        line.insert(k, (at, at + o["cost"]))
-        start[i], end[i] = at, at + o["cost"] + o["lat"]
+        line.insert(k, (at, at + cost))
+        start[i], end[i] = at, at + cost + (0.001 - WAKE if e == "n" else ops[i]["lat"])
     return start, end
 
 
@@ -127,26 +130,40 @@ def _order(ops):
             after[d].append(i)
     rank = [0.0] * n
     for i in range(n - 1, -1, -1):
-        rank[i] = ops[i]["cost"] + ops[i]["lat"] + max([rank[s] + WAKE for s in after[i]], default=0.0)
-    best = None
+        rank[i] = ops[i]["ways"][0][2] + ops[i]["lat"] + max([rank[s] + WAKE for s in after[i]], default=0.0)
+    either = {}
+    for i, o in enumerate(ops):
+        if len(o["ways"]) > 1:
+            either.setdefault(o.get("with", i), []).append(i)
+    either = list(either.values())
+    way = [0] * n
+    best = cur = None
+    marks = [i for i, o in enumerate(ops) if o["W"] and o["W"][0][0] in ("qy", "qz", "offd", "t4", "wv", "kp", "pre")]
     rng = np.random.default_rng(SEED)
-    cur = None
     for it in range(TRIES):
         for i in range(n - 1, -1, -1):
             for d in before[i]:
                 if rank[d] <= rank[i]:
                     rank[d] = rank[i] + 1e-6
-        end = _place(ops, before, sorted(range(n), key=lambda i: (-rank[i], i)))[1]
-        rank = _place(ops, after, sorted(range(n), key=lambda i: (-end[i], -i)))[1]
-        start, end = _place(ops, before, sorted(range(n), key=lambda i: (-rank[i], i)))
-        score = max(end) + 0.02 * sum(end) / n
+        if it % 8 == 0:
+            end = _place(ops, before, sorted(range(n), key=lambda i: (-rank[i], i)), way)[1]
+            rank = _place(ops, after, sorted(range(n), key=lambda i: (-end[i], -i)), way)[1]
+        start, end = _place(ops, before, sorted(range(n), key=lambda i: (-rank[i], i)), way)
+        score = max(end) + 0.02 * sum(end) / n + sum(end[i] for i in marks) / len(marks)
         if cur is None or score < cur[0] + TEMP * (1 - it / TRIES) * rng.exponential():
-            cur = (score, start)
+            cur = (score, start, way)
         if best is None or score < best[0]:
-            best = (score, start)
+            best = (score, start, way)
         t0 = rng.uniform(0, cur[0])
-        rank = [-x + (NOISE * rng.standard_normal() if abs(x - t0) < WIN else 0.0) for x in cur[1]]
-    MEMO["span"] = best[0]
+        way = list(cur[2])
+        if it % 2:
+            rank = [-x + (NOISE * rng.standard_normal() if abs(x - t0) < WIN else 0.0) for x in cur[1]]
+        else:
+            rank = [-x for x in cur[1]]
+            for k in rng.integers(0, len(either), int(rng.integers(1, 4))):
+                for i in either[k]:
+                    way[i] = 1 - way[i]
+    MEMO["way"] = best[2]
     return sorted(range(n), key=lambda i: (best[1][i], i))
 
 
@@ -156,9 +173,10 @@ def _emit(g, T, ops, tail):
         _depend(ops)
         MEMO["dep"] = [o["dep"] for o in ops]
         MEMO["order"] = _order(ops)
-    order = MEMO["order"]
-    for o, d in zip(ops, MEMO["dep"]):
-        o["dep"] = d
+    for o, dep, w in zip(ops, MEMO["dep"], MEMO["way"]):
+        o["e"], o["f"] = o["ways"][w][:2]
+        o["dep"] = sorted({x for d in dep for x in (ops[d]["dep"] if ops[d]["e"] == "n" else [d])})
+    order = [i for i in MEMO["order"] if ops[i]["e"] != "n"]
     pos = {i: k for k, i in enumerate(order)}
     known = {e: set() for e in queue}
     for i in order:
@@ -176,27 +194,31 @@ def _emit(g, T, ops, tail):
                 kn.update(ops[d]["known"])
         o["known"] = set(kn)
     own = [i for i in order if ops[i]["e"] != "x"]
-    slots = {e: [[None, 0] for _ in range(POOL[e])] for e in POOL}
+    waiters = {i: [] for i in own}
+    for i in own:
+        for d in ops[i]["waits"]:
+            if ops[d]["e"] != "x":
+                waiters[d].append(i)
+    teams = {}
+    for i in own:
+        teams.setdefault(i if ops[i]["dma"] else tuple(waiters[i]), []).append(i)
+    slots = {e: [[[], 0] for _ in range(POOL[e])] for e in POOL}
     for i in own:
         o = ops[i]
-        e = "y" if o["dma"] else o["e"]
-        if o["dma"] or o.get("inc"):
-            o["inc"] = True
-            free = [k for k, s in enumerate(slots[e]) if s[0] is None or s[0] in o["known"]]
-            if free:
-                k = free[0]
-            else:
-                k = min(range(POOL[e]), key=lambda m: pos[slots[e][m][0]])
-                o["waits"].append(slots[e][k][0])
+        if (o["dma"] or o.get("inc")) and "sem" not in o:
+            team = teams[i if o["dma"] else tuple(waiters[i])]
+            e = "y" if o["dma"] else "c"
+            k = [k for k, s in enumerate(slots[e]) if all(d in ops[j]["known"] for d in s[0] for j in team)][0]
             step = 16 if o["dma"] else 1
-            slots[e][k] = [i, slots[e][k][1] + step]
-            o["sem"], o["val"], o["step"] = "%s%d" % (e, k), slots[e][k][1], step
+            slots[e][k] = [team, slots[e][k][1] + step * len(team)]
+            for j in team:
+                ops[j].update(inc=True, sem="%s%d" % (e, k), val=slots[e][k][1], step=step)
     waited = set()
     for i in own:
         o = ops[i]
-        for d in o["waits"]:
-            queue[o["e"]].wait_ge(T.sem[ops[d]["sem"]], ops[d]["val"])
-            waited.add(d)
+        for name, val in dict.fromkeys((ops[d]["sem"], ops[d]["val"]) for d in o["waits"]):
+            queue[o["e"]].wait_ge(T.sem[name], val)
+        waited.update(o["waits"])
         ins = o["f"]()
         if o.get("inc"):
             ins.then_inc(T.sem[o["sem"]], o["step"])
@@ -244,7 +266,7 @@ def rank_program(g, core, T, topo):
         for x in outs:
             wr.append(x["use"][0])
             rd.extend(x["use"][1:])
-        ops.append({"e": e, "f": f, "R": rd, "W": wr, "dma": dma, "after": [], "cost": cost, "lat": lat})
+        ops.append({"ways": [(e, f, cost)], "R": rd, "W": wr, "dma": dma, "after": [], "lat": lat})
         return len(ops) - 1
 
     def ap(x):
@@ -283,15 +305,43 @@ def rank_program(g, core, T, topo):
         outs = [out] + ([kw["accum_out"]] if "accum_out" in kw else [])
         ins = [a] + [kw[k] for k in ("bias", "scale") if k in kw]
         op("s", lambda: SE.activation(ap(out), ap(a), f, **{k: ap(x) for k, x in kw.items()}), outs, ins,
-           span(out, [a], 1.0, False) + (0.02 if len(outs) > 1 else 0.0))
+           span(out, [a], 1.0, False) + (0.02 if len(outs) > 1 else 0.0) + (0.0 if a["ind"] else 0.02))
 
-    def move(on_s, out, a, scale=None):
-        if on_s:
-            act(out, a, F.Copy, **({} if scale is None else {"scale": scale}))
-        elif scale is None:
+    def either():
+        o = ops.pop()
+        ops[-1]["ways"] += o["ways"]
+        ops[-1]["R"] += o["R"]
+        ops[-1]["W"] += o["W"]
+
+    def optional(tag, first):
+        ops[-1]["ways"].insert(first, ("n", None, 0.0))
+        ops[-1]["with"] = tag
+
+    def apart(tag, first, tmp, win, whole, rest):
+        act(tmp, win, F.Copy)
+        optional(tag, first)
+        for f in ((rest, whole) if first else (whole, rest)):
+            f()
+        either()
+        ops[-1]["with"] = tag
+
+    def fill(out, c):
+        ms(out, c)
+        act(out, v("ids", 0, out["n"]), F.Identity, scale=0.0, bias=c)
+        either()
+
+    def shift(out, a, scale, bias):
+        act(out, a, F.Identity, scale=scale, bias=bias)
+        ts(out, a, scale, bias, A.mult, A.add)
+        either()
+
+    def move(out, a, scale=None):
+        act(out, a, F.Copy, **({} if scale is None else {"scale": scale}))
+        if scale is None:
             cp(out, a)
         else:
             ts(out, a, scale, None, A.mult)
+        either()
 
     def quant(name, tile, a=0, b=None):
         q, s = v("q" + name, a, b), v("s" + name, a, b)
@@ -301,14 +351,14 @@ def rank_program(g, core, T, topo):
         q1, s1, q2, s2 = v("q" + st, a, a + 128), v("s" + st, a, a + 128), v("q" + mv, c0, c1), v("s" + mv, c0, c1)
         out = v("ps%d" % bank, 0, q2["n"])
         op("t", lambda: PE.matmul_mx(ap(out), ap(q1), ap(s1), ap(q2), ap(s2), True, True), [out], [q1, s1, q2, s2],
-           0.000625 * (q2["n"] + 16))
+           0.0008 * (q2["n"] + 16))
 
     def iota(out, pat, base, cm, small=True):
         kw = {"allow_small_or_imprecise_dtypes": True} if small else {}
         op("g", lambda: g.iota(ap(out), pat, base, cm, **kw), [out], [], 0.13 + 2 * CYCLE * out["n"])
 
-    def choose(out, pat, o, fill, base, cm):
-        op("g", lambda: g.affine_select(ap(out), ap(out), pat, o, fill, base, cm), [out], [out],
+    def choose(out, a, pat, o, other, base, cm):
+        op("g", lambda: g.affine_select(ap(out), ap(a), pat, o, other, base, cm), [out], [a],
            0.17 + 2 * CYCLE * out["n"])
 
     def load(out, src, cast=None, e="y"):
@@ -329,22 +379,22 @@ def rank_program(g, core, T, topo):
                   HOP + 0.0014 * a["n"] * a["w"])
 
     def arrive(sem, val, outs, after):
-        ops.append({"e": "x", "sem": sem, "val": val, "R": [], "W": [x["use"][0] for x in outs], "dma": False,
-                    "after": after, "cost": 0.0, "lat": 0.0})
+        ops.append({"ways": [("x", None, 0.0)], "sem": sem, "val": val, "R": [], "W": [x["use"][0] for x in outs],
+                    "dma": False, "after": after, "lat": 0.001 - WAKE})
 
     def pick(dst, src, lst, c0=0, c1=SEG):
         out, a = v("q" + dst, 16 * c0, 16 * c1), ind(v("q" + src), v(lst, c0, c1), dt.uint32)
         op("v", lambda: VE.tensor_copy(ap(out).bitcast(dt.uint32), ap(a)), [out], [a], span(out, [a]))
-        act(v("s" + dst, 16 * c0, 16 * c1), ind(v("s" + src), v(lst, c0, c1)), F.Copy)
+        move(v("s" + dst, 16 * c0, 16 * c1), ind(v("s" + src), v(lst, c0, c1)))
 
     def diagonal(out, src, marks, low=-4096.0):
         scan(out, src, marks, low, A.max, A.subtract)
 
     def marks(out, at, lane, big, end, step, k1, k2):
-        ts(k1, at, lane, 2 * big, A.is_lt, A.mult)
-        ts(k2, at, lane, big, A.is_le, A.mult)
-        tt(v(out), k1, k2, A.subtract)
-        ts(v(out, step - 1, None, step), v(out, step - 1, None, step), big + end, None, A.add)
+        act(k1, at, F.Sign, scale=-1.0, bias=lane)
+        act(k2, k1, F.Abs, scale=2 * big, bias=big / 2)
+        shift(v(out), k2, 1.0, -1.5 * big)
+        shift(v(out, step - 1, None, step), v(out, step - 1, None, step), 1.0, big + end)
 
     def xpl(t, b, c0=0, c1=C):
         return v("xf", (4 * t + b) * 512 + c0, (4 * t + b) * 512 + c1)
@@ -362,10 +412,9 @@ def rank_program(g, core, T, topo):
         load(v("xt", 4 * c0, 4 * c1), T.x[:, 4 * c0:4 * c1])
     load(v("ut"), T.u[:], None, "s")
     load(v("nmi"), T.nm[:])
-    load(v("ht"), T.h[:])
-    load(v("qw"), T.wc[:], dt.uint8)
-    load(v("sw"), T.ws[:])
-    load(v("vt"), T.v[:])
+    for out, src, cast in (("ht", T.h, None), ("qw", T.wc, dt.uint8), ("sw", T.ws, None), ("vt", T.v, None)):
+        load(v(out), src[:], cast)
+        ops[-1]["after"] = [0, 1]
 
     iota(v("pi", 0, 1), [[1, 1]], 0, 1, False)
     ts(v("pi", 1, 2), v("pi", 0, 1), 15, None, A.bitwise_and)
@@ -375,70 +424,72 @@ def rank_program(g, core, T, topo):
     ts(v("pi", 5, 6), v("pi", 0, 1), 2, 3, A.arith_shift_right, A.bitwise_and)
     ts(v("pi", 6, 7), v("pi", 0, 1), 4, None, A.arith_shift_right)
     cp(v("col", 0, 6), v("pi", 1, 7))
-    ts(cfirst, cl, 0.0, None, A.is_equal)
-    act(c24, cl, F.Copy, scale=float(SEG))
-    act(cof2, cfirst, F.Identity, scale=float(K), bias=191.0)
-    act(cca, cl, F.Identity, scale=32.0, bias=-512.0)
-    act(cfb, cfirst, F.Identity, scale=-2016.0, bias=2048.0)
-    act(cfin, cfirst, F.Copy, scale=2 * FAR)
-    act(ctmp, cfirst, F.Identity, scale=152.0, bias=FAR + 512)
-    act(cofp, cl, F.Identity, scale=-32.0, bias=ctmp)
+    act(cfirst, cl, F.Relu, scale=-1.0, bias=1.0)
+    shift(c24, cl, float(SEG), 0.0)
+    shift(cof2, cfirst, float(K), 191.0)
+    shift(cca, cl, 32.0, -512.0)
+    shift(cfb, cfirst, -2016.0, 2048.0)
+    shift(cfin, cfirst, 2 * FAR, 0.0)
+    shift(ctmp, cfirst, 152.0, FAR + 512)
+    shift(cofp, cl, -32.0, ctmp)
     iota(v("r16"), [[1, 16]], 0, 0)
     iota(v("r4"), [[0, 16], [1, 4]], 0, 0)
     iota(v("c1"), [[16, SEG]], 0, 0)
     marks("d16", v("r16"), cl, FAR, FAR, 16, v("k1", 0, 16), v("k2", 0, 16))
     marks("dg4", v("r4"), cquad, 256 * UNIT / 2, 255 * UNIT / 2, 4, v("k3"), v("k4"))
     ts(v("lam"), v("c1"), 0.0, cl, A.mult, A.add)
-    act(v("dga"), ind(v("d16"), v("lam")), F.Copy)
-    act(v("cn"), v("c1"), F.Copy, scale=1.0 / 16)
-    act(v("dgb"), v("dga"), F.Copy)
+    move(v("dga"), ind(v("d16"), v("lam")))
+    move(v("cn"), v("c1"), 1.0 / 16)
+    move(v("dgb"), v("dga"))
     tt(v("dgb", 15, None, 16), v("dgb", 15, None, 16), v("cn"), A.add)
-    act(v("dgf"), v("dga", 0, K), F.Copy, scale=256.0)
+    move(v("dgf"), v("dga", 0, K), 256.0)
     for k, (c0, c1) in enumerate(PIECES):
-        act(v("cc", c0, c1), v("cn", 0, c1 - c0), F.Copy, scale=UNIT / SLOTS[k])
+        move(v("cc", c0, c1), v("cn", 0, c1 - c0), UNIT / SLOTS[k])
     iota(v("blk"), [[1, 8], [0, 16]], 0, 0)
     ts(v("pw"), v("r16"), cl, 1.0, A.is_lt, A.add)
     scan(v("pv"), v("pw"), v("pw"), UNIT / 2, A.mult, A.max)
     ts(cw, cl, 7.0, v("pv", 15, 16), A.is_lt, A.mult)
     ms(v("cm"), 0.0)
+    act(v("blj"), v("blk"), F.Abs, scale=-1.0, bias=cgrp)
     for s in range(4):
-        ts(v("cm", 5 * s, None, 16), v("blk", s, None, 4), cgrp, cw, A.is_equal, A.mult)
+        act(v("cm", 5 * s, None, 16), v("blj", s, None, 4), F.Relu, scale=-64 * UNIT, bias=cw)
     quant("n", v("cm"))
     for k, (c0, c1) in enumerate(PIECES):
         ms(v("sg", 512 * k + 16 * (c1 - c0), 512 * (k + 1)), 0.0)
     iota(v("nam"), [[int(UNIT), K]], -191 * int(UNIT), 0)
-    for k in range(NP):
-        a, b, s = BASE[k] // 4, BASE[k + 1] // 4, SLOTS[k]
-        ms(v("inc", a, b), 1.0)
-        ms(v("inc", a, b, s), 4096.0)
-    ms(v("inc", BASE[-2] // 4 + SLOTS[-1] - 1, None, SLOTS[-1]), 8.0)
+    iota(v("ids"), [[1, 640]], 0, 0)
+    ms(v("inc"), 1.0)
+    ms(v("inc", 0, None, SLOTS[0]), 4096.0)
+    ms(v("inc", SLOTS[0] - 1, None, SLOTS[0]), 8.0)
     ms(v("dd", 0, BASE[1], SLOTS[0]), NONE)
+    ms(v("dd", SLOTS[0] - 1, BASE[1], SLOTS[0]), NONE)
     ms(v("d32"), 32.0)
     ms(v("d32", 0, None, 16), 4096.0)
     ms(v("hold"), 0.0)
     ms(v("hold", 0, None, 16), 2 * FAR)
     ms(v("hold", 15, None, 16), -FAR)
     ms(v("t4", 0, 1), 0.0)
-    ms(v("keept"), 1.0)
+    fill(v("keept"), 1.0)
     for k, (c0, c1) in enumerate(PIECES):
         (lo, hi), a, b = ROWS[k], 16 * PAT[k], 16 * PAT[k + 1]
-        ms(v("keept", a, b, lo + hi), 0.0)
-        ms(v("keept", a + lo, b, lo + hi + 1), 0.0)
-        ms(v("ct", a + 32 * k, a + 32 * k + 16), 0.0)
-        ms(v("m3", 512 * k + 16 * (c1 - c0) + 15, 512 * (k + 1), 16), 0.0)
-    iota(v("ids"), [[1, 640]], 0, 0)
-    act(v("ca"), v("ids"), F.Identity, bias=cca)
-    choose(v("ca", 0, 512), [[0, 16], [1, 32]], A.is_ge, 4096.0, -8, 0)
-    act(v("pre", 640, 800), v("ids", 0, 160), F.Identity, scale=-1.0, bias=152.0)
+        fill(v("keept", a, b, lo + hi), 0.0)
+        fill(v("keept", a + lo, b, lo + hi + 1), 0.0)
+        fill(v("ct", a + 32 * k, a + 32 * k + 16), 0.0)
+        fill(v("m3", 512 * k + 16 * (c1 - c0) + 15, 512 * (k + 1), 16), 0.0)
+    choose(v("idm"), v("ids", 0, 512), [[0, 16], [1, 32]], A.is_ge, 4096.0, -8, 0)
+    shift(v("ca", 0, 512), v("idm"), 1.0, cca)
+    shift(v("ca", 512, 640), v("ids", 512, 640), 1.0, cca)
+    shift(v("pre", 640, 800), v("ids", 0, 160), -1.0, 152.0)
+    shift(v("pre", 0, 32), v("ids", 0, 32), -1.0, 160.0)
     iota(v("pt", 0, 512), [[-256, 16], [-4096, 32]], 256 * 511, 0)
     iota(v("pt", 512, 640), [[256, K]], 256 * C, 0)
     em = v("em")
-    ms(em, 0.0)
-    choose(em, [[-1, 528]], A.not_equal, 0.5, 3, 4)
-    act(v("c2"), v("c1"), F.Identity, bias=cl)
+    iota(em, [[0, 528]], 0, 0)
+    choose(em, em, [[-1, 528]], A.not_equal, 0.5, 3, 4)
+    shift(v("c2"), v("c1"), 1.0, cl)
     ts(v("lje"), v("c1"), 1.0 / 16, c24, A.mult, A.add)
     ts(v("ci"), v("c2"), -11.5, 1.0 / SEG, A.add, A.mult)
-    act(v("c3"), v("c2"), F.Copy, scale=16.0)
+    move(v("c3"), v("c2"), 16.0)
     ts(v("c5"), v("ci"), 1.0 - 16 * SEG, None, A.mult)
     tt(v("c5"), v("c5"), v("c3"), A.add)
     cp(v("let"), v("c5"))
@@ -447,11 +498,11 @@ def rank_program(g, core, T, topo):
         s, e = float(lo + hi), v("c2", 0, b - a)
         ts(v("bi", a, b), e, (1 - s) / 2, 1 / s, A.add, A.mult)
         ts(v("c4", a, b), v("bi", a, b), float(lo), None, A.add)
-        act(v("c6", a, b), v("c4", a, b), F.Identity, scale=-s, bias=s * lo)
+        shift(v("c6", a, b), v("c4", a, b), -s, s * lo)
         tt(v("c6", a, b), v("c6", a, b), e, A.add)
-        act(v("c8", a, b), v("c4", a, b), F.Identity, scale=-2.0, bias=s)
-        act(v("c9", 2 * k, 2 * k + 2), v("c2", 0, 2), F.Identity, scale=s + 1, bias=15 + (s + 1) * c0 - s * lo)
-        act(v("c9", 16 + 2 * k, 18 + 2 * k), v("c2", 0, 2), F.Identity, scale=-s, bias=15 + s * (hi - c0 + 1))
+        shift(v("c8", a, b), v("c4", a, b), -2.0, s)
+        shift(v("c9", 2 * k, 2 * k + 2), v("c2", 0, 2), s + 1, 15 + (s + 1) * c0 - s * lo)
+        shift(v("c9", 16 + 2 * k, 18 + 2 * k), v("c2", 0, 2), -s, 15 + s * (hi - c0 + 1))
     tt(v("c9", 0, 2 * NP), v("c9", 0, 2 * NP), v("c9", 16, 16 + 2 * NP), A.min)
     cp(v("lend"), v("c9", 0, 2 * NP))
     n = PAT[-1]
@@ -465,9 +516,9 @@ def rank_program(g, core, T, topo):
     ts(v("c10", 0, 2), v("lam", 0, 2), 8.0, -4.0, A.max, A.mult)
     ts(v("l64", 0, 2), v("c10", 0, 2), 127.0, None, A.add)
     ts(v("l64", 2, 4), v("lam", 0, 2), -4.0, 63.0, A.mult, A.add)
-    ts(c32, codd, 32.0, ch, A.mult, A.add)
+    shift(c32, codd, 32.0, ch)
     tt(c32, c32, chalf, A.subtract)
-    act(v("c10", 2, 4), v("c1", 0, 2), F.Identity, scale=-0.5, bias=15.0)
+    shift(v("c10", 2, 4), v("c1", 0, 2), -0.5, 15.0)
     ts(v("l32"), v("c10", 2, 4), c32, None, A.add)
     quant("u", v("ut"))
     for c0, c1 in ((0, C // 2), (C // 2, C)):
@@ -481,9 +532,9 @@ def rank_program(g, core, T, topo):
     cp(v("lnd0", 32, 40), v("nmi"))
     cp(ind(v("tab", K, 2 * K), v("lnd0", 32, 40)), v("ids", 0, K))
 
-    def border(t, on_v):
+    def border(t):
         for b in range(4):
-            move(b not in on_v, v("bt", b, None, 4), ind(xpl(t + 1, b, 0, 512), v("lb")), 2.0)
+            move(v("bt", b, None, 4), ind(xpl(t + 1, b, 0, 512), v("lb")), 2.0)
         quant("b%d" % t, v("bt"))
         s1 = send(v("ql%d" % t), v("qb%d" % t), "arb%d" % t, dt.uint8)
         s2 = send(v("sl%d" % t), v("sb%d" % t), "arb%d" % t)
@@ -494,8 +545,8 @@ def rank_program(g, core, T, topo):
         qx = "x0e" if first else "y%d" % (t - 1)
         lnd = "lnd%d" % t
         if not first:
-            act(v("tab", K, 2 * K), ind(v("ids", 0, K), v(lnd, 40, 48)), F.Copy)
-        act(v("dd", BASE[-2] + SLOTS[-1] - 1, None, SLOTS[-1]), v("tab", K, 2 * K), F.Identity, bias=cfb)
+            move(v("tab", K, 2 * K), ind(v("ids", 0, K), v(lnd, 40, 48)))
+        shift(v("dd", BASE[-2] + SLOTS[-1] - 1, None, SLOTS[-1]), v("tab", K, 2 * K), 1.0, cfb)
         for k, (c0, c1) in enumerate(PIECES):
             n, sl, bank = c1 - c0, SLOTS[k], PB[k]
             mm(bank, "u", 0, qx, 16 * c0, 16 * c1)
@@ -503,63 +554,70 @@ def rank_program(g, core, T, topo):
             quant("i", v("sg", 512 * k, 512 * (k + 1)), K * k, K * (k + 1))
             mm(bank, "n", 0, "i", K * k, K * (k + 1))
             diagonal(v("wv", 4 * c0, 4 * c1), ps(bank, 4 * n), v("dg4", 0, 4 * n), -512 * UNIT)
-            own = v("wv", 4 * c0 + 3, 4 * c1, 4)
             if k:
-                cp(v("dd", BASE[k], BASE[k + 1], sl), v("ag", BASE[k - 1] + SLOTS[k - 1] - 1, BASE[k], SLOTS[k - 1]))
+                move(v("dd", BASE[k], BASE[k + 1], sl), v("ag", BASE[k - 1] + c0 - PIECES[k - 1][0], BASE[k], sl))
             for c in range(c0, c1):
                 out, name = v("dd", BASE[k] + 1 + c - c0, BASE[k + 1], sl), v("wv", 4 * c + 3, 4 * c + 4)
-                if c - c0 < ON_S["match"][k]:
-                    act(out, v("nam"), F.Abs, bias=name, scale=-1.0)
-                else:
-                    ts(out, v("nam"), name, 4096.0, A.not_equal, A.mult)
+                ts(out, v("nam"), name, 4096.0, A.not_equal, A.mult)
+                act(out, v("nam"), F.Abs, bias=name, scale=-1.0)
+                either()
+                if c - c0 < MATCH:
+                    ops[-1]["ways"].reverse()
             for r in range(4):
                 a, b = BASE[k] + 32 * sl * r, BASE[k] + 32 * sl * (r + 1)
-                scan(v("ag", a, b), v("inc", BASE[k] // 4, BASE[k + 1] // 4), v("dd", a, b), 0.0, A.add, A.min)
-            tt(v("t1", c0, c1), own, v("cc", c0, c1), A.add)
-            ts(v("of1", c0, c1), v("t1", c0, c1), sl / UNIT, 191.0 * sl, A.mult, A.add)
-            ts(v("of2", c0, c1), own, 1 / UNIT, cof2, A.mult, A.add)
-            act(v("g1", 16 * c0, 16 * c1), ind(v("ag", BASE[k], BASE[k + 1]), v("of1", c0, c1)), F.Copy)
+                scan(v("ag", a, b), v("inc"), v("dd", a, b), 0.0, A.add, A.min)
+        own = v("wv", 3, None, 4)
+        tt(v("t1"), own, v("cc"), A.add)
+        ts(v("of1"), v("t1"), sl / UNIT, 191.0 * sl, A.mult, A.add)
+        ts(v("of2"), own, 1 / UNIT, cof2, A.mult, A.add)
+        for k, (c0, c1) in enumerate(PIECES):
+            move(v("g1", 16 * c0, 16 * c1), ind(v("ag", BASE[k], BASE[k + 1]), v("of1", c0, c1)))
             diagonal(v("m1", 16 * c0, 16 * c1), v("g1", 16 * c0, 16 * c1), v("dgb", 16 * c0, 16 * c1))
-        for b in range(4):
-            mm(XB[b], "e", 128 * b, qx)
-            if not first or b not in ON_S["mix"]:
-                act(xpl(t, b), ps(XB[b], C), F.Copy)
+            for b in range(4):
+                mm(XB[k][b], "e", 128 * b, qx, 16 * c0, 16 * c1)
+                if first and b:
+                    act(xpl(t, b, 16 * c0, 16 * c1), ps(XB[k][b], 16 * (c1 - c0)), F.Copy)
+                    optional(("z", t, k, b), b not in MIX[k])
+                else:
+                    move(xpl(t, b, 16 * c0, 16 * c1), ps(XB[k][b], 16 * (c1 - c0)))
         if not first:
-            border(t - 1, ())
-        act(v("w64"), ind(v("wv"), v("l64")), F.Copy)
+            border(t - 1)
+        move(v("w64"), ind(v("wv"), v("l64")))
         tr(v("t64"), v("w64"))
         ts(v(lnd, 0, 32), ind(v("t64"), v("l32")), 1 / UNIT, 191.0, A.mult, A.add)
         tr(v("ft"), v("ag", BASE[-2] + SLOTS[-1] - 1, None, SLOTS[-1]))
         scan(v("t4", 1, K + 1), v("d32"), v("ft"), 0.0, A.add, A.min)
         tr(v("tab", 0, K), v("t4", 0, K))
         for c0, c1 in PIECES:
-            act(v("g2", 16 * c0, 16 * c1), ind(v("tab"), v("of2", c0, c1)), F.Copy)
+            move(v("g2", 16 * c0, 16 * c1), ind(v("tab"), v("of2", c0, c1)))
             diagonal(v("m2", 16 * c0, 16 * c1), v("g2", 16 * c0, 16 * c1), v("dga", 16 * c0, 16 * c1))
             tt(v("kp", c0, c1), v("m1", 16 * c0 + 15, 16 * c1, 16), v("m2", 16 * c0 + 15, 16 * c1, 16), A.min)
             ts(v("offp", c0, c1), v("kp", c0, c1), cofp, None, A.add)
-        for a, b in ((0, 20), (20, 40)):
-            tt(v("alv", 16 * a, 16 * b), ind(v("tab", 0, K), v(lnd, a, b)), v("ca", 16 * a, 16 * b), A.is_ge)
-        scan(v("pre", 0, 640, -1), v("alv", 0, 640, -1), v("alv", 0, 640, -1), 0.0, A.add, A.max)
+        for a, b in ((2, 14), (14, 26), (26, 40)):
+            out, ca, ga = v("alv", 16 * a, 16 * b), v("ca", 16 * a, 16 * b), v("ga", 16 * a, 16 * b)
+            win = ind(v("tab", 0, K), v(lnd, a, b))
+            apart(("a", t, a), False, ga, win, lambda: tt(out, win, ca, A.is_ge), lambda: tt(out, ga, ca, A.is_ge))
+        scan(v("pre", 32, 640, -1), v("alv", 32, 640, -1), v("alv", 32, 640, -1), 0.0, A.add, A.max)
         for k, (c0, c1) in enumerate(PIECES):
             a, n, w = PAT[k], USED[k], -(-(c1 - c0) // 16)
             p0, p1, q0 = 16 * a, 16 * (a + n), 16 * a + 32 * k
-            act(v("a2", p0, p1), ind(v("kp", 0, c1), v("ltj", a, a + n)), F.Copy)
+            move(v("a2", p0, p1), ind(v("kp", 0, c1), v("ltj", a, a + n)))
             tt(v("nq", p0, p1), ind(v("kp", 0, c1), v("lti", a, a + n)), v("a2", p0, p1), A.is_gt)
             scan(v("ct", q0 + 16, q0 + 16 + 16 * n), v("keept", p0, p1), v("nq", p0, p1), 0.0, A.mult, A.add)
-            move(k in ON_S["count"], v("g3", 16 * c0, 16 * c1), ind(v("pre"), v("offp", c0, c1)))
+            move(v("g3", 16 * c0, 16 * c1), ind(v("pre"), v("offp", c0, c1)))
             diagonal(v("m3", 512 * k, 512 * k + 16 * (c1 - c0)), v("g3", 16 * c0, 16 * c1), v("dga", 16 * c0, 16 * c1))
             tt(v("dk", 32 * k, 32 * k + 16 * w), ind(v("ct", q0, q0 + 16 + 16 * n), v("lend", 2 * k, 2 * k + w)),
                v("m3", 512 * k + 15, 512 * k + 256 * w, 16), A.subtract)
             ts(v("offd", c0, c1), v("dk", 32 * k, 32 * k + c1 - c0), K - FAR, None, A.add)
             if t == R - 1:
-                act(v("df", c0, c1), v("dk", 32 * k, 32 * k + c1 - c0), F.Identity, bias=K - FAR)
+                shift(v("df", c0, c1), v("dk", 32 * k, 32 * k + c1 - c0), 1.0, K - FAR)
         if t == R - 1:
             store(T.ol[:, 0:C], v("df"))
         snd = "snd%d" % t
         diagonal(v("hs", 0, K, -1), v("t4", 1, K + 1, -1), v("hold", 0, K, -1))
         tr(v("fa"), v("hs"))
         diagonal(v("s1"), v("fa"), v("dga", 0, K))
-        ts(v("ownb"), v("s1", 15, None, 16), FAR, None, A.add)
+        shift(v("ownb"), v("s1", 15, None, 16), 1.0, FAR)
         ts(v("lfin"), v("s1", 15, None, 16), cfin, None, A.add)
         for r in range(8):
             act(v("jk", K * r, K * (r + 1)), v("fa"), F.Sign, bias=v("ownb", r, r + 1), scale=-1.0,
@@ -577,23 +635,23 @@ def rank_program(g, core, T, topo):
         fq = "h" if first else "l%d" % (t - 1)
         for b in range(4):
             mm(FB[b % len(FB)], "e", 128 * b, fq)
-            act(fpl(t, b), ps(FB[b % len(FB)], K), F.Copy)
-        for c0, c1 in PIECES:
+            move(fpl(t, b), ps(FB[b % len(FB)], K))
+        for k, (c0, c1) in enumerate(PIECES):
             lst, e0, e1 = v("offd", c0, c1), 16 * c0, 16 * c1
             for b in range(4):
                 z = v("zt", 4 * e0 + b, 4 * e1, 4)
-                if b in ON_S["mix"]:
-                    act(v("eg", b * C + e0, b * C + e1), ind(fpl(t, b), lst), F.Copy)
-                    tt(z, v("ps%d" % XB[b], e0, e1), v("eg", b * C + e0, b * C + e1), A.add)
+                eg, win = v("eg", b * C + e0, b * C + e1), ind(fpl(t, b), lst)
+                if b:
+                    apart(("z", t, k, b), b in MIX[k], eg, win, lambda: tt(z, win, xpl(t, b, e0, e1), A.add),
+                          lambda: tt(z, ps(XB[k][b], e1 - e0), eg, A.add))
                 else:
-                    tt(z, ind(fpl(t, b), lst), xpl(t, b, e0, e1), A.add)
+                    tt(z, win, xpl(t, b, e0, e1), A.add)
             quant("z", v("zt", 4 * e0, 4 * e1), e0, e1)
         for k, (c0, c1) in enumerate(PIECES):
             e0, e1 = 16 * c0, 16 * c1
             for b in range(4):
-                bank = YB[k][b]
-                mm(bank, "w", 128 * b, "z", e0, e1)
-                move(b in ON_S["y"][k], v("yt", 4 * e0 + b, 4 * e1, 4), ps(bank, e1 - e0), 0.03125)
+                mm(YB[k][b], "w", 128 * b, "z", e0, e1)
+                move(v("yt", 4 * e0 + b, 4 * e1, 4), ps(YB[k][b], e1 - e0), 0.03125)
             quant("y%d" % t, v("yt", 4 * e0, 4 * e1), e0, e1)
 
     t = R - 1
@@ -602,20 +660,20 @@ def rank_program(g, core, T, topo):
         for b in range(4):
             bank = (4 * k + b) % 8
             mm(bank, "e", 128 * b, "y%d" % t, e0, e1)
-            move(k < NP - 1 or b % 2 == 0, xpl(R, b, e0, e1), ps(bank, e1 - e0))
-    border(t, (1, 3))
+            move(xpl(R, b, e0, e1), ps(bank, e1 - e0))
+    border(t)
     pick("o", "y%d" % t, "let")
     mm(0, "v", 0, "o")
     store(T.oc[:, 0:4 * C], v("qo"), T.qo[:].bitcast(dt.uint8))
     for k in range(4):
         store(T.osc[4 * k:4 * k + 4, 0:C], v("so"), T.so[32 * k:32 * k + 4, :])
-    act(v("on"), ind(v("ids", 0, K), v("lnd%d" % R, 32, 40)), F.Copy)
+    move(v("on"), ind(v("ids", 0, K), v("lnd%d" % R, 32, 40)))
     store(T.ol[:, C:512], v("on"), T.on[0:128:16, :])
-    act(v("yo", 0, C), ps(0, C), F.Copy)
+    move(v("yo", 0, C), ps(0, C))
     store(T.y[:, 0:C], v("yo", 0, C))
     fq = "l%d" % t
     mm(1, "v", 0, fq)
-    cp(v("yo", C, 512), ps(1, K))
+    move(v("yo", C, 512), ps(1, K))
     store(T.y[:, C:512], v("yo", C, 512))
     store(T.oc[:, 4 * C:4 * 512], v("q" + fq), ap(v("q" + fq)).bitcast(dt.uint8), "s")
     for k in range(4):

@@ -6,16 +6,17 @@ SEG = 24
 PIECES = [(0, 12), (12, 24)]
 MIX = ((2, 3), (2, 3))
 MATCH = 5
-XB, YB, FB, PB = ((0, 1, 2, 3), (4, 5, 6, 7)), ((0, 1, 2, 3), (4, 5, 6, 7)), (0, 4), (0, 4)
-WAKE, HOP, FIRST, LOAD, CYCLE = 0.19, 2.2, 1.5, 1.8, 0.00095
-SEED, TRIES, TEMP, NOISE, WIN = 0, 40000, 0.015, 0.4, 1.0
+XB, YB, FB, PB = ((1, 1, 2, 3), (5, 5, 6, 7)), ((0, 1, 2, 3), (4, 5, 6, 7)), (0, 4, 1, 5), (0, 4)
+WAKE, HOP, SHORT, FIRST, LOAD, CYCLE = 0.22, 2.2, 0.8, 1.5, 1.8, 0.00089
+SEED, TRIES, TEMP, NOISE, WIN, PUSH = 1, 36000, 0.015, 0.4, 1.0, 8
+MARKS = ("qy", "qz", "offd", "t4", "wv", "kp", "pre", "ag", "zt")
 Q, U8, BF, F32, I32, U16, HALF = "float8_e4m3fn_x4", "uint8", "bfloat16", "float32", "int32", "uint16", "float16"
 WIDTH = {Q: 4, U8: 1, BF: 2, F32: 4, I32: 4, U16: 2, HALF: 2}
 FAR = 768.0
 UNIT = 1024.0
 NONE = 700.0
 NP = len(PIECES)
-SLOTS = [max(c1 - c0 for c0, c1 in PIECES) + 2] * NP
+SLOTS = [max(c1 - c0 for c0, c1 in PIECES) + 1] * NP
 BASE = [K * sum(SLOTS[:k]) for k in range(NP + 1)]
 ROWS = [(max(c0, 1), c1 - 1) for c0, c1 in PIECES]
 USED = [-(-((hi - lo + 2) // 2 * (lo + hi)) // 16) for lo, hi in ROWS]
@@ -46,6 +47,7 @@ def _declare():
     for name, n in (("xt", 4 * C), ("ht", 512), ("ut", 512), ("vt", 512), ("em", 528), ("cm", 512), ("xf", 16 * 512),
                     ("zt", 4 * C), ("yt", 4 * C), ("bt", 512), ("eg", 4 * C), ("sg", 512 * NP), ("nam", K),
                     ("dd", BASE[-1]), ("ag", BASE[-1]), ("inc", BASE[1] // 4), ("ft", K), ("d32", K), ("g1", C),
+                    ("fin", K), ("fbm", K),
                     ("alv", 640), ("pre", 800), ("g3", C), ("nq", 16 * PAT[-1]), ("keept", 16 * PAT[-1]),
                     ("ct", 16 * (PAT[-1] + 2 * NP)), ("jk", 8 * K), ("hold", K), ("blk", K), ("blj", K),
                     ("wv", 4 * SEG), ("w64", 64), ("t64", 64)):
@@ -55,11 +57,11 @@ def _declare():
         own(name, n, F32)
     shared("cs", F32, (("col", 24), ("r16", 16), ("r4", 64), ("dg4", 64), ("k1", 64), ("k2", 64), ("k3", 64),
                        ("k4", 64), ("c1", 24), ("c2", 24), ("c3", 24), ("c4", 24), ("c5", 24), ("c6", 24), ("c7", 24),
-                       ("c8", 24), ("c9", 32), ("c10", 8), ("cc", 24), ("cn", 24), ("dgf", K), ("pw", 16), ("pv", 16)))
-    shared("fs", F32, (("t1", SEG), ("a2", 16 * PAT[-1]), ("dk", 32 * NP), ("acc", 8), ("fp", K), ("s1", K), ("s2", K),
-                       ("ownb", 8)))
-    for name, n in (("dga", C), ("dgb", C), ("m1", C), ("g2", C), ("m2", C), ("m3", 512 * NP), ("hs", K), ("fa", K),
-                    ("ca", 640), ("ga", 640)):
+                       ("c8", 24), ("c9", 32), ("c10", 8), ("cc", 24), ("cn", 24), ("cn8", 24), ("dgf", K), ("pw", 16),
+                       ("pv", 16)))
+    shared("fs", F32, (("t1", SEG), ("a2", 16 * PAT[-1]), ("acc", 8), ("fp", K), ("s2", K), ("ownb", 8)))
+    for name, n in (("dga", C), ("dgb", C), ("dgc", 256 * NP), ("m1", C), ("g2", C), ("m2", C), ("m3", C), ("hs", K),
+                    ("fa", K), ("ca", 640), ("ga", 640), ("s1", K)):
         own(name, n, HALF)
     own("nmi", 8, I32)
     shared("ns", I32, (("pi", 8), ("ci", 24), ("bi", 32)))
@@ -74,9 +76,10 @@ def _declare():
 
 
 _declare()
-POOL = {"c": 121, "y": 22}
+POOL = {"c": 118, "y": 23}
 SEMAPHORES = (["%s%d" % (e, i) for e in POOL for i in range(POOL[e])]
-              + ["arl%d" % t for t in range(R)] + ["arb%d" % t for t in range(R)] + ["sent"])
+              + ["arl%d" % t for t in range(R)] + ["arb%d" % t for t in range(R)] + ["arr%d" % t for t in range(R - 1)]
+              + ["sent"])
 
 
 def _depend(ops):
@@ -103,21 +106,25 @@ def _depend(ops):
         o["dep"] = sorted(need - {-1, i})
 
 
-def _place(ops, before, order, way):
-    start, end = [0.0] * len(ops), [0.0] * len(ops)
-    busy = {e: [] for e in "vstgyxn"}
+def _place(before, order, queue, cost, lag):
+    start, end = [0.0] * len(order), [0.0] * len(order)
+    lo, hi = {e: [] for e in "vstgyxn"}, {e: [] for e in "vstgyxn"}
     for i in order:
-        e, _, cost = ops[i]["ways"][way[i]]
-        at = max([end[d] for d in before[i]], default=-WAKE) + WAKE
-        line = busy[e]
-        k = len(line)
-        while k and line[k - 1][1] > at:
+        at = 0.0
+        for d in before[i]:
+            if end[d] > at:
+                at = end[d]
+        a, b, c = lo[queue[i]], hi[queue[i]], cost[i]
+        n = k = len(a)
+        while k and b[k - 1] > at:
             k -= 1
-        while k < len(line) and line[k][0] < at + cost:
-            at = max(at, line[k][1])
+        while k < n and a[k] < at + c:
+            if b[k] > at:
+                at = b[k]
             k += 1
-        line.insert(k, (at, at + cost))
-        start[i], end[i] = at, at + cost + (0.001 - WAKE if e == "n" else ops[i]["lat"])
+        a.insert(k, at)
+        b.insert(k, at + c)
+        start[i], end[i] = at, at + c + lag[i]
     return start, end
 
 
@@ -128,41 +135,55 @@ def _order(ops):
     for i, o in enumerate(ops):
         for d in o["dep"]:
             after[d].append(i)
-    rank = [0.0] * n
+    late = [-(o["ways"][0][2] + o["lat"] + WAKE) for o in ops]
     for i in range(n - 1, -1, -1):
-        rank[i] = ops[i]["ways"][0][2] + ops[i]["lat"] + max([rank[s] + WAKE for s in after[i]], default=0.0)
+        late[i] += min([late[s] for s in after[i]], default=0.0)
     either = {}
     for i, o in enumerate(ops):
         if len(o["ways"]) > 1:
             either.setdefault(o.get("with", i), []).append(i)
     either = list(either.values())
+    marks = [i for i, o in enumerate(ops) if o["W"] and o["W"][0][0] in MARKS]
+    marks += 4 * [max(i for i, o in enumerate(ops) if o["W"] and o["W"][0][0] == "qb")]
     way = [0] * n
     best = cur = None
-    marks = [i for i, o in enumerate(ops) if o["W"] and o["W"][0][0] in ("qy", "qz", "offd", "t4", "wv", "kp", "pre")]
     rng = np.random.default_rng(SEED)
     for it in range(TRIES):
+        queue = [o["ways"][w][0] for o, w in zip(ops, way)]
+        cost = [o["ways"][w][2] for o, w in zip(ops, way)]
+        lag = [0.001 if e == "n" else o["lat"] + WAKE for o, e in zip(ops, queue)]
         for i in range(n - 1, -1, -1):
             for d in before[i]:
-                if rank[d] <= rank[i]:
-                    rank[d] = rank[i] + 1e-6
-        if it % 8 == 0:
-            end = _place(ops, before, sorted(range(n), key=lambda i: (-rank[i], i)), way)[1]
-            rank = _place(ops, after, sorted(range(n), key=lambda i: (-end[i], -i)), way)[1]
-        start, end = _place(ops, before, sorted(range(n), key=lambda i: (-rank[i], i)), way)
+                if late[d] >= late[i]:
+                    late[d] = late[i] - 1e-6
+        order = sorted(range(n), key=lambda i: late[i])
+        if it % PUSH == 0:
+            end = _place(before, order, queue, cost, lag)[1]
+            end = _place(after, sorted(range(n), key=lambda i: (-end[i], -i)), queue, cost, lag)[1]
+            order = sorted(range(n), key=lambda i: (-end[i], i))
+        start, end = _place(before, order, queue, cost, lag)
         score = max(end) + 0.02 * sum(end) / n + sum(end[i] for i in marks) / len(marks)
         if cur is None or score < cur[0] + TEMP * (1 - it / TRIES) * rng.exponential():
             cur = (score, start, way)
         if best is None or score < best[0]:
             best = (score, start, way)
-        t0 = rng.uniform(0, cur[0])
-        way = list(cur[2])
-        if it % 2:
-            rank = [-x + (NOISE * rng.standard_normal() if abs(x - t0) < WIN else 0.0) for x in cur[1]]
+        way, late = list(cur[2]), list(cur[1])
+        t0 = rng.uniform(0, max(late))
+        near = [i for i in range(n) if abs(late[i] - t0) < WIN]
+        kind = it % 4
+        if kind == 0:
+            for i, x in zip(near, rng.standard_normal(len(near))):
+                late[i] += NOISE * x
+        elif kind == 1:
+            for i in rng.choice(near, min(3, len(near))):
+                late[i] += 2 * NOISE * rng.standard_normal()
         else:
-            rank = [-x for x in cur[1]]
-            for k in rng.integers(0, len(either), int(rng.integers(1, 4))):
-                for i in either[k]:
+            some = [k for k in either if abs(late[k[0]] - t0) < 2 * WIN] or either
+            for k in rng.integers(0, len(some), kind - 1):
+                for i in some[k]:
                     way[i] = 1 - way[i]
+            for i, x in zip(near, rng.standard_normal(len(near))):
+                late[i] += 0.1 * NOISE * x
     MEMO["way"] = best[2]
     return sorted(range(n), key=lambda i: (best[1][i], i))
 
@@ -351,7 +372,7 @@ def rank_program(g, core, T, topo):
         q1, s1, q2, s2 = v("q" + st, a, a + 128), v("s" + st, a, a + 128), v("q" + mv, c0, c1), v("s" + mv, c0, c1)
         out = v("ps%d" % bank, 0, q2["n"])
         op("t", lambda: PE.matmul_mx(ap(out), ap(q1), ap(s1), ap(q2), ap(s2), True, True), [out], [q1, s1, q2, s2],
-           0.0008 * (q2["n"] + 16))
+           0.0007 * (q2["n"] + 16))
 
     def iota(out, pat, base, cm, small=True):
         kw = {"allow_small_or_imprecise_dtypes": True} if small else {}
@@ -376,7 +397,7 @@ def rank_program(g, core, T, topo):
         cost = 0.35 if sent[0] else 0.35 + FIRST
         sent[0] += n_out
         return op("g", lambda: g.remote_dma(o, i, T.sem[sem], T.sem.sent, pid, rid, mask), [], [a], cost, False,
-                  HOP + 0.0014 * a["n"] * a["w"])
+                  HOP + 0.0014 * a["n"] * a["w"] + (SHORT if a["w"] == 2 else 0.0))
 
     def arrive(sem, val, outs, after):
         ops.append({"ways": [("x", None, 0.0)], "sem": sem, "val": val, "R": [], "W": [x["use"][0] for x in outs],
@@ -405,16 +426,16 @@ def rank_program(g, core, T, topo):
     def ps(b, n):
         return v("ps%d" % b, 0, n)
 
-    (cl, ch, codd, chalf, cquad, cgrp, cfirst, c24, cof2, cofp, cca, cfb, cfin, ctmp, cw, c32) = (
-        v("col", i, i + 1) for i in range(16))
+    (cl, ch, codd, chalf, cquad, cgrp, cfirst, c24, cof2, cofp, cca, cfb, cfin, ctmp, cw, c32, c8) = (
+        v("col", i, i + 1) for i in range(17))
 
-    for c0, c1 in ((0, C // 2), (C // 2, C)):
+    for c0, c1 in ((0, K), (K, 2 * K), (2 * K, C)):
         load(v("xt", 4 * c0, 4 * c1), T.x[:, 4 * c0:4 * c1])
     load(v("ut"), T.u[:], None, "s")
     load(v("nmi"), T.nm[:])
     for out, src, cast in (("ht", T.h, None), ("qw", T.wc, dt.uint8), ("sw", T.ws, None), ("vt", T.v, None)):
         load(v(out), src[:], cast)
-        ops[-1]["after"] = [0, 1]
+        ops[-1]["after"] = [0, 1, 2]
 
     iota(v("pi", 0, 1), [[1, 1]], 0, 1, False)
     ts(v("pi", 1, 2), v("pi", 0, 1), 15, None, A.bitwise_and)
@@ -427,10 +448,11 @@ def rank_program(g, core, T, topo):
     act(cfirst, cl, F.Relu, scale=-1.0, bias=1.0)
     shift(c24, cl, float(SEG), 0.0)
     shift(cof2, cfirst, float(K), 191.0)
-    shift(cca, cl, 32.0, -512.0)
-    shift(cfb, cfirst, -2016.0, 2048.0)
-    shift(cfin, cfirst, 2 * FAR, 0.0)
-    shift(ctmp, cfirst, 152.0, FAR + 512)
+    shift(cca, cl, 32.0, -520.0)
+    shift(cfb, cfirst, -2024.0, 2048.0)
+    shift(cfin, cfirst, 2 * FAR, 8.0)
+    shift(ctmp, cfirst, 144.0, FAR + 520)
+    shift(c8, cfirst, -8.0, 8.0)
     shift(cofp, cl, -32.0, ctmp)
     iota(v("r16"), [[1, 16]], 0, 0)
     iota(v("r4"), [[0, 16], [1, 4]], 0, 0)
@@ -441,7 +463,8 @@ def rank_program(g, core, T, topo):
     move(v("dga"), ind(v("d16"), v("lam")))
     move(v("cn"), v("c1"), 1.0 / 16)
     move(v("dgb"), v("dga"))
-    tt(v("dgb", 15, None, 16), v("dgb", 15, None, 16), v("cn"), A.add)
+    shift(v("cn8"), v("cn"), 1.0, c8)
+    tt(v("dgb", 15, None, 16), v("dgb", 15, None, 16), v("cn8"), A.add)
     move(v("dgf"), v("dga", 0, K), 256.0)
     for k, (c0, c1) in enumerate(PIECES):
         move(v("cc", c0, c1), v("cn", 0, c1 - c0), UNIT / SLOTS[k])
@@ -460,9 +483,7 @@ def rank_program(g, core, T, topo):
     iota(v("ids"), [[1, 640]], 0, 0)
     ms(v("inc"), 1.0)
     ms(v("inc", 0, None, SLOTS[0]), 4096.0)
-    ms(v("inc", SLOTS[0] - 1, None, SLOTS[0]), 8.0)
     ms(v("dd", 0, BASE[1], SLOTS[0]), NONE)
-    ms(v("dd", SLOTS[0] - 1, BASE[1], SLOTS[0]), NONE)
     ms(v("d32"), 32.0)
     ms(v("d32", 0, None, 16), 4096.0)
     ms(v("hold"), 0.0)
@@ -475,7 +496,7 @@ def rank_program(g, core, T, topo):
         fill(v("keept", a, b, lo + hi), 0.0)
         fill(v("keept", a + lo, b, lo + hi + 1), 0.0)
         fill(v("ct", a + 32 * k, a + 32 * k + 16), 0.0)
-        fill(v("m3", 512 * k + 16 * (c1 - c0) + 15, 512 * (k + 1), 16), 0.0)
+        move(v("dgc", 256 * k, 256 * k + 16 * (c1 - c0)), v("dga", 0, 16 * (c1 - c0)))
     choose(v("idm"), v("ids", 0, 512), [[0, 16], [1, 32]], A.is_ge, 4096.0, -8, 0)
     shift(v("ca", 0, 512), v("idm"), 1.0, cca)
     shift(v("ca", 512, 640), v("ids", 512, 640), 1.0, cca)
@@ -521,7 +542,7 @@ def rank_program(g, core, T, topo):
     shift(v("c10", 2, 4), v("c1", 0, 2), -0.5, 15.0)
     ts(v("l32"), v("c10", 2, 4), c32, None, A.add)
     quant("u", v("ut"))
-    for c0, c1 in ((0, C // 2), (C // 2, C)):
+    for c0, c1 in ((0, K), (K, 2 * K), (2 * K, C)):
         quant("x0", v("xt", 4 * c0, 4 * c1), c0, c1)
     quant("h", v("ht"))
     quant("v", v("vt"))
@@ -546,7 +567,7 @@ def rank_program(g, core, T, topo):
         lnd = "lnd%d" % t
         if not first:
             move(v("tab", K, 2 * K), ind(v("ids", 0, K), v(lnd, 40, 48)))
-        shift(v("dd", BASE[-2] + SLOTS[-1] - 1, None, SLOTS[-1]), v("tab", K, 2 * K), 1.0, cfb)
+        shift(v("fbm"), v("tab", K, 2 * K), 1.0, cfb)
         for k, (c0, c1) in enumerate(PIECES):
             n, sl, bank = c1 - c0, SLOTS[k], PB[k]
             mm(bank, "u", 0, qx, 16 * c0, 16 * c1)
@@ -575,7 +596,7 @@ def rank_program(g, core, T, topo):
             diagonal(v("m1", 16 * c0, 16 * c1), v("g1", 16 * c0, 16 * c1), v("dgb", 16 * c0, 16 * c1))
             for b in range(4):
                 mm(XB[k][b], "e", 128 * b, qx, 16 * c0, 16 * c1)
-                if first and b:
+                if first and b > 1:
                     act(xpl(t, b, 16 * c0, 16 * c1), ps(XB[k][b], 16 * (c1 - c0)), F.Copy)
                     optional(("z", t, k, b), b not in MIX[k])
                 else:
@@ -585,7 +606,8 @@ def rank_program(g, core, T, topo):
         move(v("w64"), ind(v("wv"), v("l64")))
         tr(v("t64"), v("w64"))
         ts(v(lnd, 0, 32), ind(v("t64"), v("l32")), 1 / UNIT, 191.0, A.mult, A.add)
-        tr(v("ft"), v("ag", BASE[-2] + SLOTS[-1] - 1, None, SLOTS[-1]))
+        tt(v("fin"), v("ag", BASE[-2] + SLOTS[-1] - 1, None, SLOTS[-1]), v("fbm"), A.min)
+        tr(v("ft"), v("fin"))
         scan(v("t4", 1, K + 1), v("d32"), v("ft"), 0.0, A.add, A.min)
         tr(v("tab", 0, K), v("t4", 0, K))
         for c0, c1 in PIECES:
@@ -605,12 +627,12 @@ def rank_program(g, core, T, topo):
             tt(v("nq", p0, p1), ind(v("kp", 0, c1), v("lti", a, a + n)), v("a2", p0, p1), A.is_gt)
             scan(v("ct", q0 + 16, q0 + 16 + 16 * n), v("keept", p0, p1), v("nq", p0, p1), 0.0, A.mult, A.add)
             move(v("g3", 16 * c0, 16 * c1), ind(v("pre"), v("offp", c0, c1)))
-            diagonal(v("m3", 512 * k, 512 * k + 16 * (c1 - c0)), v("g3", 16 * c0, 16 * c1), v("dga", 16 * c0, 16 * c1))
-            tt(v("dk", 32 * k, 32 * k + 16 * w), ind(v("ct", q0, q0 + 16 + 16 * n), v("lend", 2 * k, 2 * k + w)),
-               v("m3", 512 * k + 15, 512 * k + 256 * w, 16), A.subtract)
-            ts(v("offd", c0, c1), v("dk", 32 * k, 32 * k + c1 - c0), K - FAR, None, A.add)
+            ts(v("dgc", 256 * k + 15, 256 * (k + 1), 16),
+               ind(v("ct", q0, q0 + 16 + 16 * n), v("lend", 2 * k, 2 * k + 1)), v("d16", 15, 16), None, A.add)
+            diagonal(v("m3", 16 * c0, 16 * c1), v("g3", 16 * c0, 16 * c1), v("dgc", 256 * k, 256 * k + 16 * (c1 - c0)))
+            ts(v("offd", c0, c1), v("m3", 16 * c0 + 15, 16 * c1, 16), -1.0, K - FAR, A.mult, A.add)
             if t == R - 1:
-                shift(v("df", c0, c1), v("dk", 32 * k, 32 * k + c1 - c0), 1.0, K - FAR)
+                shift(v("df", c0, c1), v("m3", 16 * c0 + 15, 16 * c1, 16), -1.0, K - FAR)
         if t == R - 1:
             store(T.ol[:, 0:C], v("df"))
         snd = "snd%d" % t
@@ -623,6 +645,9 @@ def rank_program(g, core, T, topo):
             act(v("jk", K * r, K * (r + 1)), v("fa"), F.Sign, bias=v("ownb", r, r + 1), scale=-1.0,
                 accum_out=v("acc", r, r + 1))
         ts(v(snd, 8, 16), v("acc"), 127.0, 0.5, A.add, A.mult)
+        if t < R - 1:
+            land = v("lnd%d" % (t + 1), 40, 48)
+            arrive("arr%d" % t, n_in, [land], [send(land, v(snd, 8, 16), "arr%d" % t)])
         tt(v("fp"), ind(v("pt"), v("lfin")), v("ids", 0, K), A.add)
         cp(ind(v("sc"), v(snd, 8, 16)), v("fp"))
         diagonal(v("s2"), v("sc"), v("dgf"), -1024 * UNIT)
@@ -630,8 +655,8 @@ def rank_program(g, core, T, topo):
         ts(v("pk"), v("s2", 15, None, 16), 256 * FAR, None, A.add)
         ts(v("pn"), v("pk"), 255, None, A.bitwise_and)
         cp(v(snd, 0, 8), v("pn"))
-        land = v("lnd%d" % (t + 1), 32, 48)
-        arrive("arl%d" % t, n_in, [land], [send(land, v(snd), "arl%d" % t)])
+        land = v("lnd%d" % (t + 1), 32, 40)
+        arrive("arl%d" % t, n_in, [land], [send(land, v(snd, 0, 8), "arl%d" % t)])
         fq = "h" if first else "l%d" % (t - 1)
         for b in range(4):
             mm(FB[b % len(FB)], "e", 128 * b, fq)
@@ -641,7 +666,7 @@ def rank_program(g, core, T, topo):
             for b in range(4):
                 z = v("zt", 4 * e0 + b, 4 * e1, 4)
                 eg, win = v("eg", b * C + e0, b * C + e1), ind(fpl(t, b), lst)
-                if b:
+                if b > 1:
                     apart(("z", t, k, b), b in MIX[k], eg, win, lambda: tt(z, win, xpl(t, b, e0, e1), A.add),
                           lambda: tt(z, ps(XB[k][b], e1 - e0), eg, A.add))
                 else:

import numpy as np
from concourse.mybir import dt, AluOpType as A, ActivationFunctionType as F

C, K, R = 384, 128, 3
SEG = 24
PIECES = [(0, 12), (12, 24)]
MIX = ((2, 3), (2, 3))
MATCH = 5
XB, YB, FB, PB = ((1, 1, 2, 3), (5, 5, 6, 7)), ((0, 1, 2, 3), (4, 5, 6, 7)), (0, 4, 1, 5), (0, 4)
WAKE, HOP, SHORT, FIRST, LOAD, CYCLE = 0.22, 2.2, 0.8, 1.5, 1.8, 0.00089
SEED, TRIES, TEMP, NOISE, WIN, PUSH = 1, 36000, 0.015, 0.4, 1.0, 8
MARKS = ("qy", "qz", "offd", "t4", "wv", "kp", "pre", "ag", "zt")
Q, U8, BF, F32, I32, U16, HALF = "float8_e4m3fn_x4", "uint8", "bfloat16", "float32", "int32", "uint16", "float16"
WIDTH = {Q: 4, U8: 1, BF: 2, F32: 4, I32: 4, U16: 2, HALF: 2}
FAR = 768.0
UNIT = 1024.0
NONE = 700.0
NP = len(PIECES)
SLOTS = [max(c1 - c0 for c0, c1 in PIECES) + 1] * NP
BASE = [K * sum(SLOTS[:k]) for k in range(NP + 1)]
ROWS = [(max(c0, 1), c1 - 1) for c0, c1 in PIECES]
USED = [-(-((hi - lo + 2) // 2 * (lo + hi)) // 16) for lo, hi in ROWS]
PAT = [sum(n + n % 2 for n in USED[:k]) for k in range(NP + 1)]
SCRATCH, PLACE, MEMO = {}, {}, {}


def _declare():
    def own(name, n, d):
        SCRATCH[name] = ("sbuf", [128, n], d)
        PLACE[name] = (name, 0, n)

    def shared(buf, d, items):
        at = 0
        for name, n in items:
            PLACE[name] = (buf, at, n)
            at += (n + 31) // 32 * 32
        SCRATCH[buf] = ("sbuf", [128, at], d)
    for name, n in (("w", 512), ("u", K), ("v", K), ("e", 512), ("n", K), ("x0", C), ("x0e", C), ("h", K), ("o", C),
                    ("z", C), ("i", K * NP)):
        own("q" + name, n, Q)
        own("s" + name, n, U8)
    for name, n in (("y", C), ("b", K), ("l", K)):
        shared("q" + name, Q, [("q%s%d" % (name, t), n) for t in range(R)])
        shared("s" + name, U8, [("s%s%d" % (name, t), n) for t in range(R)])
    shared("snd", U16, [("snd%d" % t, 16) for t in range(R)])
    shared("lnd", U16, [("lnd%d" % t, 48) for t in range(R + 1)])
    for name, n in (("xt", 4 * C), ("ht", 512), ("ut", 512), ("vt", 512), ("em", 528), ("cm", 512), ("xf", 16 * 512),
                    ("zt", 4 * C), ("yt", 4 * C), ("bt", 512), ("eg", 4 * C), ("sg", 512 * NP), ("nam", K),
                    ("dd", BASE[-1]), ("ag", BASE[-1]), ("inc", BASE[1] // 4), ("ft", K), ("d32", K), ("g1", C),
                    ("fin", K), ("fbm", K),
                    ("alv", 640), ("pre", 800), ("g3", C), ("nq", 16 * PAT[-1]), ("keept", 16 * PAT[-1]),
                    ("ct", 16 * (PAT[-1] + 2 * NP)), ("jk", 8 * K), ("hold", K), ("blk", K), ("blj", K),
                    ("wv", 4 * SEG), ("w64", 64), ("t64", 64)):
        own(name, n, BF)
    for name, n in (("ids", 640), ("idm", 512), ("pt", 640), ("tab", 256), ("sc", K), ("yo", 512), ("on", K),
                    ("df", SEG), ("kp", SEG), ("t4", 160), ("d16", 16)):
        own(name, n, F32)
    shared("cs", F32, (("col", 24), ("r16", 16), ("r4", 64), ("dg4", 64), ("k1", 64), ("k2", 64), ("k3", 64),
                       ("k4", 64), ("c1", 24), ("c2", 24), ("c3", 24), ("c4", 24), ("c5", 24), ("c6", 24), ("c7", 24),
                       ("c8", 24), ("c9", 32), ("c10", 8), ("cc", 24), ("cn", 24), ("cn8", 24), ("dgf", K), ("pw", 16),
                       ("pv", 16)))
    shared("fs", F32, (("t1", SEG), ("a2", 16 * PAT[-1]), ("acc", 8), ("fp", K), ("s2", K), ("ownb", 8)))
    for name, n in (("dga", C), ("dgb", C), ("dgc", 256 * NP), ("m1", C), ("g2", C), ("m2", C), ("m3", C), ("hs", K),
                    ("fa", K), ("ca", 640), ("ga", 640), ("s1", K)):
        own(name, n, HALF)
    own("nmi", 8, I32)
    shared("ns", I32, (("pi", 8), ("ci", 24), ("bi", 32)))
    shared("nd", I32, (("pk", 8), ("pn", 8)))
    for name, n in (("lje", 24), ("let", 24), ("lti", PAT[-1]), ("ltj", PAT[-1]), ("lend", 2 * NP), ("lam", 24),
                    ("l64", 4), ("l32", 2), ("of1", 24), ("of2", 24), ("offp", 24), ("offd", 24), ("lfin", 8),
                    ("lb", 8)):
        own(name, n, U16)
    for b in range(8):
        SCRATCH["ps%d" % b] = ("psum", [128, 512], F32)
        PLACE["ps%d" % b] = ("ps%d" % b, 0, 512)


_declare()
POOL = {"c": 118, "y": 23}
SEMAPHORES = (["%s%d" % (e, i) for e in POOL for i in range(POOL[e])]
              + ["arl%d" % t for t in range(R)] + ["arb%d" % t for t in range(R)] + ["arr%d" % t for t in range(R - 1)]
              + ["sent"])


def _depend(ops):
    lastw = {b: np.full(SCRATCH[b][1][1], -1) for b in SCRATCH}
    readers = {b: [] for b in SCRATCH}
    for i, o in enumerate(ops):
        need = set(o["after"])
        for b, idx in o["R"]:
            need.update(int(d) for d in np.unique(lastw[b][idx]))
        for b, idx in o["W"]:
            need.update(int(d) for d in np.unique(lastw[b][idx]))
            for rd in readers[b]:
                if rd[1][idx].any():
                    need.add(rd[0])
        for b, idx in o["W"]:
            lastw[b][idx] = i
            for rd in readers[b]:
                rd[1][idx] = False
            readers[b] = [rd for rd in readers[b] if rd[1].any()]
        for b, idx in o["R"]:
            m = np.zeros(len(lastw[b]), bool)
            m[idx] = True
            readers[b].append((i, m))
        o["dep"] = sorted(need - {-1, i})


def _place(before, order, queue, cost, lag):
    start, end = [0.0] * len(order), [0.0] * len(order)
    lo, hi = {e: [] for e in "vstgyxn"}, {e: [] for e in "vstgyxn"}
    for i in order:
        at = 0.0
        for d in before[i]:
            if end[d] > at:
                at = end[d]
        a, b, c = lo[queue[i]], hi[queue[i]], cost[i]
        n = k = len(a)
        while k and b[k - 1] > at:
            k -= 1
        while k < n and a[k] < at + c:
            if b[k] > at:
                at = b[k]
            k += 1
        a.insert(k, at)
        b.insert(k, at + c)
        start[i], end[i] = at, at + c + lag[i]
    return start, end


def _order(ops):
    n = len(ops)
    before = [o["dep"] for o in ops]
    after = [[] for _ in range(n)]
    for i, o in enumerate(ops):
        for d in o["dep"]:
            after[d].append(i)
    late = [-(o["ways"][0][2] + o["lat"] + WAKE) for o in ops]
    for i in range(n - 1, -1, -1):
        late[i] += min([late[s] for s in after[i]], default=0.0)
    either = {}
    for i, o in enumerate(ops):
        if len(o["ways"]) > 1:
            either.setdefault(o.get("with", i), []).append(i)
    either = list(either.values())
    marks = [i for i, o in enumerate(ops) if o["W"] and o["W"][0][0] in MARKS]
    marks += 4 * [max(i for i, o in enumerate(ops) if o["W"] and o["W"][0][0] == "qb")]
    way = [0] * n
    best = cur = None
    rng = np.random.default_rng(SEED)
    for it in range(TRIES):
        queue = [o["ways"][w][0] for o, w in zip(ops, way)]
        cost = [o["ways"][w][2] for o, w in zip(ops, way)]
        lag = [0.001 if e == "n" else o["lat"] + WAKE for o, e in zip(ops, queue)]
        for i in range(n - 1, -1, -1):
            for d in before[i]:
                if late[d] >= late[i]:
                    late[d] = late[i] - 1e-6
        order = sorted(range(n), key=lambda i: late[i])
        if it % PUSH == 0:
            end = _place(before, order, queue, cost, lag)[1]
            end = _place(after, sorted(range(n), key=lambda i: (-end[i], -i)), queue, cost, lag)[1]
            order = sorted(range(n), key=lambda i: (-end[i], i))
        start, end = _place(before, order, queue, cost, lag)
        score = max(end) + 0.02 * sum(end) / n + sum(end[i] for i in marks) / len(marks)
        if cur is None or score < cur[0] + TEMP * (1 - it / TRIES) * rng.exponential():
            cur = (score, start, way)
        if best is None or score < best[0]:
            best = (score, start, way)
        way, late = list(cur[2]), list(cur[1])
        t0 = rng.uniform(0, max(late))
        near = [i for i in range(n) if abs(late[i] - t0) < WIN]
        kind = it % 4
        if kind == 0:
            for i, x in zip(near, rng.standard_normal(len(near))):
                late[i] += NOISE * x
        elif kind == 1:
            for i in rng.choice(near, min(3, len(near))):
                late[i] += 2 * NOISE * rng.standard_normal()
        else:
            some = [k for k in either if abs(late[k[0]] - t0) < 2 * WIN] or either
            for k in rng.integers(0, len(some), kind - 1):
                for i in some[k]:
                    way[i] = 1 - way[i]
            for i, x in zip(near, rng.standard_normal(len(near))):
                late[i] += 0.1 * NOISE * x
    MEMO["way"] = best[2]
    return sorted(range(n), key=lambda i: (best[1][i], i))


def _emit(g, T, ops, tail):
    queue = {"v": g.vector, "s": g.scalar, "t": g.tensor, "g": g, "y": g.sync}
    if not MEMO:
        _depend(ops)
        MEMO["dep"] = [o["dep"] for o in ops]
        MEMO["order"] = _order(ops)
    for o, dep, w in zip(ops, MEMO["dep"], MEMO["way"]):
        o["e"], o["f"] = o["ways"][w][:2]
        o["dep"] = sorted({x for d in dep for x in (ops[d]["dep"] if ops[d]["e"] == "n" else [d])})
    order = [i for i in MEMO["order"] if ops[i]["e"] != "n"]
    pos = {i: k for k, i in enumerate(order)}
    known = {e: set() for e in queue}
    for i in order:
        o = ops[i]
        if o["e"] == "x":
            o["known"] = set()
            continue
        kn = known[o["e"]]
        o["waits"] = []
        for d in sorted(o["dep"], key=lambda d: -pos[d]):
            if d not in kn:
                o["waits"].append(d)
                ops[d]["inc"] = True
                kn.add(d)
                kn.update(ops[d]["known"])
        o["known"] = set(kn)
    own = [i for i in order if ops[i]["e"] != "x"]
    waiters = {i: [] for i in own}
    for i in own:
        for d in ops[i]["waits"]:
            if ops[d]["e"] != "x":
                waiters[d].append(i)
    teams = {}
    for i in own:
        teams.setdefault(i if ops[i]["dma"] else tuple(waiters[i]), []).append(i)
    slots = {e: [[[], 0] for _ in range(POOL[e])] for e in POOL}
    for i in own:
        o = ops[i]
        if (o["dma"] or o.get("inc")) and "sem" not in o:
            team = teams[i if o["dma"] else tuple(waiters[i])]
            e = "y" if o["dma"] else "c"
            k = [k for k, s in enumerate(slots[e]) if all(d in ops[j]["known"] for d in s[0] for j in team)][0]
            step = 16 if o["dma"] else 1
            slots[e][k] = [team, slots[e][k][1] + step * len(team)]
            for j in team:
                ops[j].update(inc=True, sem="%s%d" % (e, k), val=slots[e][k][1], step=step)
    waited = set()
    for i in own:
        o = ops[i]
        for name, val in dict.fromkeys((ops[d]["sem"], ops[d]["val"]) for d in o["waits"]):
            queue[o["e"]].wait_ge(T.sem[name], val)
        waited.update(o["waits"])
        ins = o["f"]()
        if o.get("inc"):
            ins.then_inc(T.sem[o["sem"]], o["step"])
    for name, val in tail:
        g.wait_ge(T.sem[name], val)
    for i in own:
        if ops[i]["dma"] and i not in waited:
            queue[ops[i]["e"]].wait_ge(T.sem[ops[i]["sem"]], ops[i]["val"])


def rank_program(g, core, T, topo):
    rank = T.rank_of(core)
    if rank is None:
        return
    nr = len(T.cores)
    nxt, prv = T.cores[(rank + 1) % nr], T.cores[(rank - 1) % nr]
    rid, pid = topo.addr(nxt)[0], topo.addr(nxt)[1]
    mask, n_out, n_in = topo.mask(core, nxt), len(topo.engines(core, nxt)), len(topo.engines(prv, core))
    VE, SE, PE = g.vector, g.scalar, g.tensor
    ops = []
    sent = [0]

    def v(name, a=0, b=None, s=1):
        buf, at, n = PLACE[name]
        b = n if b is None else b
        if s > 0:
            ap, idx = T[buf][:, at + a:at + b:s], np.arange(at + a, at + b, s)
        else:
            lo = at + a - 1
            ap, idx = T[buf][:, slice(at + b - 1, lo if lo >= 0 else None, -1)], np.arange(at + a, at + b)
        ps = buf.startswith("ps")
        return {"ap": ap, "use": [(buf, np.arange(512) if ps else idx)], "n": len(idx), "ps": ps,
                "w": WIDTH[SCRATCH[buf][2]], "ind": False}

    def ind(win, off, cast=None):
        ap = win["ap"] if cast is None else win["ap"].bitcast(cast)
        return {"ap": ap.indirect(off["ap"]), "use": win["use"] + off["use"], "ps": False, "n": 16 * off["n"],
                "w": win["w"], "ind": True}

    def op(e, f, outs, ins, cost, dma=False, lat=0.0):
        rd, wr = [], []
        for x in ins:
            if isinstance(x, dict):
                (wr if x["ps"] else rd).extend(x["use"])
        for x in outs:
            wr.append(x["use"][0])
            rd.extend(x["use"][1:])
        ops.append({"ways": [(e, f, cost)], "R": rd, "W": wr, "dma": dma, "after": [], "lat": lat})
        return len(ops) - 1

    def ap(x):
        return x["ap"] if isinstance(x, dict) else x

    def span(out, ins, rate=1.0, fast=True):
        if out["ind"]:
            return 0.05 + 3.8 * CYCLE * out["n"]
        if ins[0]["ind"]:
            return 0.06 + 1.56 * CYCLE * out["n"]
        narrow = fast and all(x["w"] <= 2 for x in [out] + ins)
        return CYCLE * max(64, out["n"] * rate * (0.5 if narrow else 1.0))

    def ts(out, a, s1, s2, o0, o1=None):
        tail = (o0,) if s2 is None else (o0, o1)
        op("v", lambda: VE.tensor_scalar(ap(out), ap(a), ap(s1), ap(s2), *tail), [out], [a, s1, s2], span(out, [a]))

    def tt(out, a, b, o):
        op("v", lambda: VE.tensor_tensor(ap(out), ap(a), ap(b), o), [out], [a, b],
           span(out, [a, b], 1.0 if a["ps"] else 2.0))

    def cp(out, a):
        op("v", lambda: VE.tensor_copy(ap(out), ap(a)), [out], [a], span(out, [a]))

    def scan(out, d0, d1, init, o0, o1):
        op("v", lambda: VE.tensor_tensor_scan(ap(out), ap(d0), ap(d1), init, o0, o1), [out], [d0, d1],
           span(out, [d0, d1]))

    def tr(out, a):
        op("v", lambda: VE.transpose(ap(out), ap(a)), [out], [a], span(out, [a]))

    def ms(out, c):
        op("v", lambda: VE.memset(ap(out), c), [out], [], span(out, [out]))

    def act(out, a, f, **kw):
        outs = [out] + ([kw["accum_out"]] if "accum_out" in kw else [])
        ins = [a] + [kw[k] for k in ("bias", "scale") if k in kw]
        op("s", lambda: SE.activation(ap(out), ap(a), f, **{k: ap(x) for k, x in kw.items()}), outs, ins,
           span(out, [a], 1.0, False) + (0.02 if len(outs) > 1 else 0.0) + (0.0 if a["ind"] else 0.02))

    def either():
        o = ops.pop()
        ops[-1]["ways"] += o["ways"]
        ops[-1]["R"] += o["R"]
        ops[-1]["W"] += o["W"]

    def optional(tag, first):
        ops[-1]["ways"].insert(first, ("n", None, 0.0))
        ops[-1]["with"] = tag

    def apart(tag, first, tmp, win, whole, rest):
        act(tmp, win, F.Copy)
        optional(tag, first)
        for f in ((rest, whole) if first else (whole, rest)):
            f()
        either()
        ops[-1]["with"] = tag

    def fill(out, c):
        ms(out, c)
        act(out, v("ids", 0, out["n"]), F.Identity, scale=0.0, bias=c)
        either()

    def shift(out, a, scale, bias):
        act(out, a, F.Identity, scale=scale, bias=bias)
        ts(out, a, scale, bias, A.mult, A.add)
        either()

    def move(out, a, scale=None):
        act(out, a, F.Copy, **({} if scale is None else {"scale": scale}))
        if scale is None:
            cp(out, a)
        else:
            ts(out, a, scale, None, A.mult)
        either()

    def quant(name, tile, a=0, b=None):
        q, s = v("q" + name, a, b), v("s" + name, a, b)
        op("v", lambda: VE.quantize_mx(ap(q), ap(s), ap(tile)), [q, s], [tile], 0.012 + 0.00022 * tile["n"])

    def mm(bank, st, a, mv, c0=0, c1=None):
        q1, s1, q2, s2 = v("q" + st, a, a + 128), v("s" + st, a, a + 128), v("q" + mv, c0, c1), v("s" + mv, c0, c1)
        out = v("ps%d" % bank, 0, q2["n"])
        op("t", lambda: PE.matmul_mx(ap(out), ap(q1), ap(s1), ap(q2), ap(s2), True, True), [out], [q1, s1, q2, s2],
           0.0007 * (q2["n"] + 16))

    def iota(out, pat, base, cm, small=True):
        kw = {"allow_small_or_imprecise_dtypes": True} if small else {}
        op("g", lambda: g.iota(ap(out), pat, base, cm, **kw), [out], [], 0.13 + 2 * CYCLE * out["n"])

    def choose(out, a, pat, o, other, base, cm):
        op("g", lambda: g.affine_select(ap(out), ap(a), pat, o, other, base, cm), [out], [a],
           0.17 + 2 * CYCLE * out["n"])

    def load(out, src, cast=None, e="y"):
        dst = out["ap"] if cast is None else out["ap"].bitcast(cast)
        q = g.sync if e == "y" else g.scalar
        op(e, lambda: q.dma_start(dst, src), [out], [], 0.06, True, LOAD + 0.0007 * out["n"] * out["w"])

    def store(dst, a, src=None, e="y"):
        q = g.sync if e == "y" else g.scalar
        op(e, lambda: q.dma_start(dst, ap(a) if src is None else src), [], [a], 0.06, True,
           LOAD + 0.0007 * a["n"] * a["w"])

    def send(out, a, sem, cast=None):
        o, i = (out["ap"], a["ap"]) if cast is None else (out["ap"].bitcast(cast), a["ap"].bitcast(cast))
        cost = 0.35 if sent[0] else 0.35 + FIRST
        sent[0] += n_out
        return op("g", lambda: g.remote_dma(o, i, T.sem[sem], T.sem.sent, pid, rid, mask), [], [a], cost, False,
                  HOP + 0.0014 * a["n"] * a["w"] + (SHORT if a["w"] == 2 else 0.0))

    def arrive(sem, val, outs, after):
        ops.append({"ways": [("x", None, 0.0)], "sem": sem, "val": val, "R": [], "W": [x["use"][0] for x in outs],
                    "dma": False, "after": after, "lat": 0.001 - WAKE})

    def pick(dst, src, lst, c0=0, c1=SEG):
        out, a = v("q" + dst, 16 * c0, 16 * c1), ind(v("q" + src), v(lst, c0, c1), dt.uint32)
        op("v", lambda: VE.tensor_copy(ap(out).bitcast(dt.uint32), ap(a)), [out], [a], span(out, [a]))
        move(v("s" + dst, 16 * c0, 16 * c1), ind(v("s" + src), v(lst, c0, c1)))

    def diagonal(out, src, marks, low=-4096.0):
        scan(out, src, marks, low, A.max, A.subtract)

    def marks(out, at, lane, big, end, step, k1, k2):
        act(k1, at, F.Sign, scale=-1.0, bias=lane)
        act(k2, k1, F.Abs, scale=2 * big, bias=big / 2)
        shift(v(out), k2, 1.0, -1.5 * big)
        shift(v(out, step - 1, None, step), v(out, step - 1, None, step), 1.0, big + end)

    def xpl(t, b, c0=0, c1=C):
        return v("xf", (4 * t + b) * 512 + c0, (4 * t + b) * 512 + c1)

    def fpl(t, b):
        return xpl(t + 1, b, C, 512)

    def ps(b, n):
        return v("ps%d" % b, 0, n)

    (cl, ch, codd, chalf, cquad, cgrp, cfirst, c24, cof2, cofp, cca, cfb, cfin, ctmp, cw, c32, c8) = (
        v("col", i, i + 1) for i in range(17))

    for c0, c1 in ((0, K), (K, 2 * K), (2 * K, C)):
        load(v("xt", 4 * c0, 4 * c1), T.x[:, 4 * c0:4 * c1])
    load(v("ut"), T.u[:], None, "s")
    load(v("nmi"), T.nm[:])
    for out, src, cast in (("ht", T.h, None), ("qw", T.wc, dt.uint8), ("sw", T.ws, None), ("vt", T.v, None)):
        load(v(out), src[:], cast)
        ops[-1]["after"] = [0, 1, 2]

    iota(v("pi", 0, 1), [[1, 1]], 0, 1, False)
    ts(v("pi", 1, 2), v("pi", 0, 1), 15, None, A.bitwise_and)
    ts(v("pi", 2, 3), v("pi", 0, 1), 16, None, A.bitwise_and)
    ts(v("pi", 3, 4), v("pi", 0, 1), 1, None, A.bitwise_and)
    ts(v("pi", 4, 5), v("pi", 0, 1), 1, 7, A.arith_shift_right, A.bitwise_and)
    ts(v("pi", 5, 6), v("pi", 0, 1), 2, 3, A.arith_shift_right, A.bitwise_and)
    ts(v("pi", 6, 7), v("pi", 0, 1), 4, None, A.arith_shift_right)
    cp(v("col", 0, 6), v("pi", 1, 7))
    act(cfirst, cl, F.Relu, scale=-1.0, bias=1.0)
    shift(c24, cl, float(SEG), 0.0)
    shift(cof2, cfirst, float(K), 191.0)
    shift(cca, cl, 32.0, -520.0)
    shift(cfb, cfirst, -2024.0, 2048.0)
    shift(cfin, cfirst, 2 * FAR, 8.0)
    shift(ctmp, cfirst, 144.0, FAR + 520)
    shift(c8, cfirst, -8.0, 8.0)
    shift(cofp, cl, -32.0, ctmp)
    iota(v("r16"), [[1, 16]], 0, 0)
    iota(v("r4"), [[0, 16], [1, 4]], 0, 0)
    iota(v("c1"), [[16, SEG]], 0, 0)
    marks("d16", v("r16"), cl, FAR, FAR, 16, v("k1", 0, 16), v("k2", 0, 16))
    marks("dg4", v("r4"), cquad, 256 * UNIT / 2, 255 * UNIT / 2, 4, v("k3"), v("k4"))
    ts(v("lam"), v("c1"), 0.0, cl, A.mult, A.add)
    move(v("dga"), ind(v("d16"), v("lam")))
    move(v("cn"), v("c1"), 1.0 / 16)
    move(v("dgb"), v("dga"))
    shift(v("cn8"), v("cn"), 1.0, c8)
    tt(v("dgb", 15, None, 16), v("dgb", 15, None, 16), v("cn8"), A.add)
    move(v("dgf"), v("dga", 0, K), 256.0)
    for k, (c0, c1) in enumerate(PIECES):
        move(v("cc", c0, c1), v("cn", 0, c1 - c0), UNIT / SLOTS[k])
    iota(v("blk"), [[1, 8], [0, 16]], 0, 0)
    ts(v("pw"), v("r16"), cl, 1.0, A.is_lt, A.add)
    scan(v("pv"), v("pw"), v("pw"), UNIT / 2, A.mult, A.max)
    ts(cw, cl, 7.0, v("pv", 15, 16), A.is_lt, A.mult)
    ms(v("cm"), 0.0)
    act(v("blj"), v("blk"), F.Abs, scale=-1.0, bias=cgrp)
    for s in range(4):
        act(v("cm", 5 * s, None, 16), v("blj", s, None, 4), F.Relu, scale=-64 * UNIT, bias=cw)
    quant("n", v("cm"))
    for k, (c0, c1) in enumerate(PIECES):
        ms(v("sg", 512 * k + 16 * (c1 - c0), 512 * (k + 1)), 0.0)
    iota(v("nam"), [[int(UNIT), K]], -191 * int(UNIT), 0)
    iota(v("ids"), [[1, 640]], 0, 0)
    ms(v("inc"), 1.0)
    ms(v("inc", 0, None, SLOTS[0]), 4096.0)
    ms(v("dd", 0, BASE[1], SLOTS[0]), NONE)
    ms(v("d32"), 32.0)
    ms(v("d32", 0, None, 16), 4096.0)
    ms(v("hold"), 0.0)
    ms(v("hold", 0, None, 16), 2 * FAR)
    ms(v("hold", 15, None, 16), -FAR)
    ms(v("t4", 0, 1), 0.0)
    fill(v("keept"), 1.0)
    for k, (c0, c1) in enumerate(PIECES):
        (lo, hi), a, b = ROWS[k], 16 * PAT[k], 16 * PAT[k + 1]
        fill(v("keept", a, b, lo + hi), 0.0)
        fill(v("keept", a + lo, b, lo + hi + 1), 0.0)
        fill(v("ct", a + 32 * k, a + 32 * k + 16), 0.0)
        move(v("dgc", 256 * k, 256 * k + 16 * (c1 - c0)), v("dga", 0, 16 * (c1 - c0)))
    choose(v("idm"), v("ids", 0, 512), [[0, 16], [1, 32]], A.is_ge, 4096.0, -8, 0)
    shift(v("ca", 0, 512), v("idm"), 1.0, cca)
    shift(v("ca", 512, 640), v("ids", 512, 640), 1.0, cca)
    shift(v("pre", 640, 800), v("ids", 0, 160), -1.0, 152.0)
    shift(v("pre", 0, 32), v("ids", 0, 32), -1.0, 160.0)
    iota(v("pt", 0, 512), [[-256, 16], [-4096, 32]], 256 * 511, 0)
    iota(v("pt", 512, 640), [[256, K]], 256 * C, 0)
    em = v("em")
    iota(em, [[0, 528]], 0, 0)
    choose(em, em, [[-1, 528]], A.not_equal, 0.5, 3, 4)
    shift(v("c2"), v("c1"), 1.0, cl)
    ts(v("lje"), v("c1"), 1.0 / 16, c24, A.mult, A.add)
    ts(v("ci"), v("c2"), -11.5, 1.0 / SEG, A.add, A.mult)
    move(v("c3"), v("c2"), 16.0)
    ts(v("c5"), v("ci"), 1.0 - 16 * SEG, None, A.mult)
    tt(v("c5"), v("c5"), v("c3"), A.add)
    cp(v("let"), v("c5"))
    for k, (c0, c1) in enumerate(PIECES):
        (lo, hi), a, b = ROWS[k], PAT[k], PAT[k + 1]
        s, e = float(lo + hi), v("c2", 0, b - a)
        ts(v("bi", a, b), e, (1 - s) / 2, 1 / s, A.add, A.mult)
        ts(v("c4", a, b), v("bi", a, b), float(lo), None, A.add)
        shift(v("c6", a, b), v("c4", a, b), -s, s * lo)
        tt(v("c6", a, b), v("c6", a, b), e, A.add)
        shift(v("c8", a, b), v("c4", a, b), -2.0, s)
        shift(v("c9", 2 * k, 2 * k + 2), v("c2", 0, 2), s + 1, 15 + (s + 1) * c0 - s * lo)
        shift(v("c9", 16 + 2 * k, 18 + 2 * k), v("c2", 0, 2), -s, 15 + s * (hi - c0 + 1))
    tt(v("c9", 0, 2 * NP), v("c9", 0, 2 * NP), v("c9", 16, 16 + 2 * NP), A.min)
    cp(v("lend"), v("c9", 0, 2 * NP))
    n = PAT[-1]
    tt(v("c7", 0, n), v("c6", 0, n), v("c4", 0, n), A.is_ge)
    tt(v("c8", 0, n), v("c8", 0, n), v("c7", 0, n), A.mult)
    tt(v("c7", 0, n), v("c7", 0, n), v("c4", 0, n), A.mult)
    tt(v("c8", 0, n), v("c8", 0, n), v("c4", 0, n), A.add)
    tt(v("c7", 0, n), v("c6", 0, n), v("c7", 0, n), A.subtract)
    cp(v("ltj"), v("c8", 0, n))
    cp(v("lti"), v("c7", 0, n))
    ts(v("c10", 0, 2), v("lam", 0, 2), 8.0, -4.0, A.max, A.mult)
    ts(v("l64", 0, 2), v("c10", 0, 2), 127.0, None, A.add)
    ts(v("l64", 2, 4), v("lam", 0, 2), -4.0, 63.0, A.mult, A.add)
    shift(c32, codd, 32.0, ch)
    tt(c32, c32, chalf, A.subtract)
    shift(v("c10", 2, 4), v("c1", 0, 2), -0.5, 15.0)
    ts(v("l32"), v("c10", 2, 4), c32, None, A.add)
    quant("u", v("ut"))
    for c0, c1 in ((0, K), (K, 2 * K), (2 * K, C)):
        quant("x0", v("xt", 4 * c0, 4 * c1), c0, c1)
    quant("h", v("ht"))
    quant("v", v("vt"))
    for b in range(4):
        quant("e", v("em", 3 - b, 515 - b), 128 * b, 128 * b + 128)
    for c0, c1 in PIECES:
        pick("x0e", "x0", "lje", c0, c1)
    cp(v("lnd0", 32, 40), v("nmi"))
    cp(ind(v("tab", K, 2 * K), v("lnd0", 32, 40)), v("ids", 0, K))

    def border(t):
        for b in range(4):
            move(v("bt", b, None, 4), ind(xpl(t + 1, b, 0, 512), v("lb")), 2.0)
        quant("b%d" % t, v("bt"))
        s1 = send(v("ql%d" % t), v("qb%d" % t), "arb%d" % t, dt.uint8)
        s2 = send(v("sl%d" % t), v("sb%d" % t), "arb%d" % t)
        arrive("arb%d" % t, 2 * n_in, [v("ql%d" % t), v("sl%d" % t)], [s1, s2])

    for t in range(R):
        first = t == 0
        qx = "x0e" if first else "y%d" % (t - 1)
        lnd = "lnd%d" % t
        if not first:
            move(v("tab", K, 2 * K), ind(v("ids", 0, K), v(lnd, 40, 48)))
        shift(v("fbm"), v("tab", K, 2 * K), 1.0, cfb)
        for k, (c0, c1) in enumerate(PIECES):
            n, sl, bank = c1 - c0, SLOTS[k], PB[k]
            mm(bank, "u", 0, qx, 16 * c0, 16 * c1)
            act(v("sg", 512 * k, 512 * k + 16 * n), ps(bank, 16 * n), F.Sign, bias=-(2.0 ** -100), scale=-1.0)
            quant("i", v("sg", 512 * k, 512 * (k + 1)), K * k, K * (k + 1))
            mm(bank, "n", 0, "i", K * k, K * (k + 1))
            diagonal(v("wv", 4 * c0, 4 * c1), ps(bank, 4 * n), v("dg4", 0, 4 * n), -512 * UNIT)
            if k:
                move(v("dd", BASE[k], BASE[k + 1], sl), v("ag", BASE[k - 1] + c0 - PIECES[k - 1][0], BASE[k], sl))
            for c in range(c0, c1):
                out, name = v("dd", BASE[k] + 1 + c - c0, BASE[k + 1], sl), v("wv", 4 * c + 3, 4 * c + 4)
                ts(out, v("nam"), name, 4096.0, A.not_equal, A.mult)
                act(out, v("nam"), F.Abs, bias=name, scale=-1.0)
                either()
                if c - c0 < MATCH:
                    ops[-1]["ways"].reverse()
            for r in range(4):
                a, b = BASE[k] + 32 * sl * r, BASE[k] + 32 * sl * (r + 1)
                scan(v("ag", a, b), v("inc"), v("dd", a, b), 0.0, A.add, A.min)
        own = v("wv", 3, None, 4)
        tt(v("t1"), own, v("cc"), A.add)
        ts(v("of1"), v("t1"), sl / UNIT, 191.0 * sl, A.mult, A.add)
        ts(v("of2"), own, 1 / UNIT, cof2, A.mult, A.add)
        for k, (c0, c1) in enumerate(PIECES):
            move(v("g1", 16 * c0, 16 * c1), ind(v("ag", BASE[k], BASE[k + 1]), v("of1", c0, c1)))
            diagonal(v("m1", 16 * c0, 16 * c1), v("g1", 16 * c0, 16 * c1), v("dgb", 16 * c0, 16 * c1))
            for b in range(4):
                mm(XB[k][b], "e", 128 * b, qx, 16 * c0, 16 * c1)
                if first and b > 1:
                    act(xpl(t, b, 16 * c0, 16 * c1), ps(XB[k][b], 16 * (c1 - c0)), F.Copy)
                    optional(("z", t, k, b), b not in MIX[k])
                else:
                    move(xpl(t, b, 16 * c0, 16 * c1), ps(XB[k][b], 16 * (c1 - c0)))
        if not first:
            border(t - 1)
        move(v("w64"), ind(v("wv"), v("l64")))
        tr(v("t64"), v("w64"))
        ts(v(lnd, 0, 32), ind(v("t64"), v("l32")), 1 / UNIT, 191.0, A.mult, A.add)
        tt(v("fin"), v("ag", BASE[-2] + SLOTS[-1] - 1, None, SLOTS[-1]), v("fbm"), A.min)
        tr(v("ft"), v("fin"))
        scan(v("t4", 1, K + 1), v("d32"), v("ft"), 0.0, A.add, A.min)
        tr(v("tab", 0, K), v("t4", 0, K))
        for c0, c1 in PIECES:
            move(v("g2", 16 * c0, 16 * c1), ind(v("tab"), v("of2", c0, c1)))
            diagonal(v("m2", 16 * c0, 16 * c1), v("g2", 16 * c0, 16 * c1), v("dga", 16 * c0, 16 * c1))
            tt(v("kp", c0, c1), v("m1", 16 * c0 + 15, 16 * c1, 16), v("m2", 16 * c0 + 15, 16 * c1, 16), A.min)
            ts(v("offp", c0, c1), v("kp", c0, c1), cofp, None, A.add)
        for a, b in ((2, 14), (14, 26), (26, 40)):
            out, ca, ga = v("alv", 16 * a, 16 * b), v("ca", 16 * a, 16 * b), v("ga", 16 * a, 16 * b)
            win = ind(v("tab", 0, K), v(lnd, a, b))
            apart(("a", t, a), False, ga, win, lambda: tt(out, win, ca, A.is_ge), lambda: tt(out, ga, ca, A.is_ge))
        scan(v("pre", 32, 640, -1), v("alv", 32, 640, -1), v("alv", 32, 640, -1), 0.0, A.add, A.max)
        for k, (c0, c1) in enumerate(PIECES):
            a, n, w = PAT[k], USED[k], -(-(c1 - c0) // 16)
            p0, p1, q0 = 16 * a, 16 * (a + n), 16 * a + 32 * k
            move(v("a2", p0, p1), ind(v("kp", 0, c1), v("ltj", a, a + n)))
            tt(v("nq", p0, p1), ind(v("kp", 0, c1), v("lti", a, a + n)), v("a2", p0, p1), A.is_gt)
            scan(v("ct", q0 + 16, q0 + 16 + 16 * n), v("keept", p0, p1), v("nq", p0, p1), 0.0, A.mult, A.add)
            move(v("g3", 16 * c0, 16 * c1), ind(v("pre"), v("offp", c0, c1)))
            ts(v("dgc", 256 * k + 15, 256 * (k + 1), 16),
               ind(v("ct", q0, q0 + 16 + 16 * n), v("lend", 2 * k, 2 * k + 1)), v("d16", 15, 16), None, A.add)
            diagonal(v("m3", 16 * c0, 16 * c1), v("g3", 16 * c0, 16 * c1), v("dgc", 256 * k, 256 * k + 16 * (c1 - c0)))
            ts(v("offd", c0, c1), v("m3", 16 * c0 + 15, 16 * c1, 16), -1.0, K - FAR, A.mult, A.add)
            if t == R - 1:
                shift(v("df", c0, c1), v("m3", 16 * c0 + 15, 16 * c1, 16), -1.0, K - FAR)
        if t == R - 1:
            store(T.ol[:, 0:C], v("df"))
        snd = "snd%d" % t
        diagonal(v("hs", 0, K, -1), v("t4", 1, K + 1, -1), v("hold", 0, K, -1))
        tr(v("fa"), v("hs"))
        diagonal(v("s1"), v("fa"), v("dga", 0, K))
        shift(v("ownb"), v("s1", 15, None, 16), 1.0, FAR)
        ts(v("lfin"), v("s1", 15, None, 16), cfin, None, A.add)
        for r in range(8):
            act(v("jk", K * r, K * (r + 1)), v("fa"), F.Sign, bias=v("ownb", r, r + 1), scale=-1.0,
                accum_out=v("acc", r, r + 1))
        ts(v(snd, 8, 16), v("acc"), 127.0, 0.5, A.add, A.mult)
        if t < R - 1:
            land = v("lnd%d" % (t + 1), 40, 48)
            arrive("arr%d" % t, n_in, [land], [send(land, v(snd, 8, 16), "arr%d" % t)])
        tt(v("fp"), ind(v("pt"), v("lfin")), v("ids", 0, K), A.add)
        cp(ind(v("sc"), v(snd, 8, 16)), v("fp"))
        diagonal(v("s2"), v("sc"), v("dgf"), -1024 * UNIT)
        ts(v("lb"), v("s2", 15, None, 16), 1.0 / 256, FAR - 0.25, A.mult, A.add)
        ts(v("pk"), v("s2", 15, None, 16), 256 * FAR, None, A.add)
        ts(v("pn"), v("pk"), 255, None, A.bitwise_and)
        cp(v(snd, 0, 8), v("pn"))
        land = v("lnd%d" % (t + 1), 32, 40)
        arrive("arl%d" % t, n_in, [land], [send(land, v(snd, 0, 8), "arl%d" % t)])
        fq = "h" if first else "l%d" % (t - 1)
        for b in range(4):
            mm(FB[b % len(FB)], "e", 128 * b, fq)
            move(fpl(t, b), ps(FB[b % len(FB)], K))
        for k, (c0, c1) in enumerate(PIECES):
            lst, e0, e1 = v("offd", c0, c1), 16 * c0, 16 * c1
            for b in range(4):
                z = v("zt", 4 * e0 + b, 4 * e1, 4)
                eg, win = v("eg", b * C + e0, b * C + e1), ind(fpl(t, b), lst)
                if b > 1:
                    apart(("z", t, k, b), b in MIX[k], eg, win, lambda: tt(z, win, xpl(t, b, e0, e1), A.add),
                          lambda: tt(z, ps(XB[k][b], e1 - e0), eg, A.add))
                else:
                    tt(z, win, xpl(t, b, e0, e1), A.add)
            quant("z", v("zt", 4 * e0, 4 * e1), e0, e1)
        for k, (c0, c1) in enumerate(PIECES):
            e0, e1 = 16 * c0, 16 * c1
            for b in range(4):
                mm(YB[k][b], "w", 128 * b, "z", e0, e1)
                move(v("yt", 4 * e0 + b, 4 * e1, 4), ps(YB[k][b], e1 - e0), 0.03125)
            quant("y%d" % t, v("yt", 4 * e0, 4 * e1), e0, e1)

    t = R - 1
    for k, (c0, c1) in enumerate(PIECES):
        e0, e1 = 16 * c0, 16 * c1
        for b in range(4):
            bank = (4 * k + b) % 8
            mm(bank, "e", 128 * b, "y%d" % t, e0, e1)
            move(xpl(R, b, e0, e1), ps(bank, e1 - e0))
    border(t)
    pick("o", "y%d" % t, "let")
    mm(0, "v", 0, "o")
    store(T.oc[:, 0:4 * C], v("qo"), T.qo[:].bitcast(dt.uint8))
    for k in range(4):
        store(T.osc[4 * k:4 * k + 4, 0:C], v("so"), T.so[32 * k:32 * k + 4, :])
    move(v("on"), ind(v("ids", 0, K), v("lnd%d" % R, 32, 40)))
    store(T.ol[:, C:512], v("on"), T.on[0:128:16, :])
    move(v("yo", 0, C), ps(0, C))
    store(T.y[:, 0:C], v("yo", 0, C))
    fq = "l%d" % t
    mm(1, "v", 0, fq)
    move(v("yo", C, 512), ps(1, K))
    store(T.y[:, C:512], v("yo", C, 512))
    store(T.oc[:, 4 * C:4 * 512], v("q" + fq), ap(v("q" + fq)).bitcast(dt.uint8), "s")
    for k in range(4):
        store(T.osc[4 * k:4 * k + 4, C:512], v("s" + fq), T.sl[32 * k:32 * k + 4, K * t:K * (t + 1)],
              "s" if k < 2 else "y")
    _emit(g, T, ops, [("sent", sent[0])])
